import numpy as np, ml_dtypes
CORES = [40,41,42,43,44,45,46,47]
N = 8
BF = ml_dtypes.bfloat16
S, L, R, B, CAP = 4, 512, 3, 2304, 128
A, W = S * L, B + R * L
def parts(rng):
    x = rng.integers(0, 256, (N, 8, 16, B)); k = rng.integers(0, B, (N, 8, 16, B))
    head = rng.integers(0, B, (N, 8, 6, 64)); clan = rng.integers(0, 64, (N, 8, 1, B))
    k[:, :, :6] = np.where(rng.random((N, 8, 6, B)) < 0.35, np.take_along_axis(head, np.repeat(clan, 6, axis=2), 3), k[:, :, :6])
    return x, k, rng.integers(800, 1201, (N, 8, R)), rng.integers(0, 256, (N, 8, 16, R))
def pack(x, k, th, w):
    return {"xf": np.ascontiguousarray(x.reshape(N, 128, B)).astype(np.float32).astype(BF), "kin": np.ascontiguousarray(k.reshape(N, 128, B)).astype(np.int32),
            "th": np.ascontiguousarray(th).astype(np.int32), "w": np.ascontiguousarray(w.reshape(N, 128, R)).astype(np.int32)}
def setup_inputs(rng):
    return pack(*parts(rng))
def setup_inputs_spread(rng):
    x, k, th, w = parts(rng)
    size = np.exp2(8 * rng.random((N, 8, 1, B))) * (rng.random((N, 8, 1, B)) > 0.0625)
    x = np.minimum((size * rng.random(x.shape)).astype(np.int64), 255)
    few = np.minimum((B * rng.random(k.shape) ** rng.choice(np.array([1.0, 2.0, 4.0]), (N, 8, 1, 1))).astype(np.int64), B - 1)
    k = np.where(rng.random(k.shape) < 0.5, few, k)
    th = np.minimum(np.exp2(4 + 8 * rng.random(th.shape)).astype(np.int64), 4095)
    w = np.minimum((np.exp2(8 * rng.random((N, 8, 1, R))) * rng.random(w.shape)).astype(np.int64), 255)
    return pack(x, k, th, w)
def setup_inputs_ends(rng):
    x, k, th, w = parts(rng)
    kind = rng.integers(0, 3, (N, 8, 1, B)); x = 255 * np.where(kind == 2, rng.integers(0, 2, x.shape), kind)
    loose = rng.random((N, 8, 1, B)) < 0.2; loose[..., 0] = True; loose[..., B - 1] = True
    k[:, 7] = rng.integers(0, B - 32, (N, 16, B))
    end = (B - 1) * rng.integers(0, 2, k.shape); k = np.where(loose, k, end)
    top = np.arange(B - 32, B - 2); top = top[(top & (S - 1)) != 0][-16:]; last = S * (L - 1) + np.arange(R)
    kg, xg = k[:, 7], x[:, 7]
    mid = S * np.arange(CAP // 2, L - 1) + 1; xg[:, :, mid] = 255
    kg[:, :, last] = B - 2; xg[:, :, last] = 0; xg[:, :, top] = 255; kg[:, :, top] = end[:, 7][:, :, top]
    for q in range(N): kg[q, :, B - 2] = rng.permutation(top)
    th = 4095 * rng.integers(0, 2, th.shape); th[:, 7] = 4095 * ((np.arange(R) + 1) & 1)
    w = 255 * rng.integers(0, 2, w.shape); w[:, 7] = 255
    return pack(x, k, th, w)
def setup_inputs_corners(rng):
    x, k, th, w = parts(rng); i = np.arange(L); v = S * i; u = v + 1; mm = v + 2; own = np.arange(B)
    z = rng.integers(0, 6, (N, 4, 16, B)); k[:, 1::2] = np.where(z == 0, 0, np.where(z == 1, B - 1, np.where(z == 2, own, k[:, 1::2])))
    e = k[..., mm]; k[..., mm] = e + ((e & (S - 1)) == 1)
    th = rng.choice(np.array([0, 1, 700, 1000, 1100, 4095]), th.shape); w = rng.choice(np.array([0, 1, 128, 255]), w.shape)
    for q in range(N):
        for g in range(8):
            F = int(rng.choice(np.array([0, 1, CAP - 1, CAP, CAP + 1, L])))
            if q == 0: F = (0, 1, CAP - 1, CAP, CAP + 1, L, CAP, L)[g]
            must = q == 0 and g == 3
            lose = np.zeros(L, bool); o = rng.permutation(L)
            if must: o = np.concatenate([np.array([0]), 1 + rng.permutation(L - 2), np.array([L - 1])])
            lose[o[:F]] = True
            if q == N - 1 and g == 7: lose = i >= L - CAP
            t0 = int(rng.choice(np.array([1, 17, 300, 2399]))); how = rng.integers(0, 4, L)
            if must: how[0] = 1
            far0 = np.where(lose & (how == 3), t0, np.where(rng.random(L) < 0.5, t0 - 1, rng.integers(0, t0, L)))
            kg, xg = k[q, g], x[q, g]; base = rng.integers(0, 100, (16, L))
            xg[:, v] = base; xg[:, mm] = base + far0 // 16 + (np.arange(16)[:, None] < (far0 & 15))
            src = np.nonzero(~lose | (how == 3))[0]; at = np.searchsorted(src, i); goal = mm.copy()
            named = lose & (how == 2) & (at > 0); none = lose & ((how == 0) | ((how == 2) & (at == 0))); blood = lose & (how == 1)
            bl, wl = np.nonzero(blood)[0], np.nonzero(~lose)[0]
            if must: bl, wl = bl[1:], wl[:-1]
            pairs = min(len(bl), len(wl)); bl = bl[np.argsort(rng.random(len(bl)))[:pairs]]; wl = wl[np.argsort(rng.random(len(wl)))[:pairs]]
            ok = bl < wl; bl, wl = bl[ok], wl[ok]
            if must: bl, wl = np.append(bl, 0), np.append(wl, L - 1)
            goal[wl] = mm[bl]; xg[:, v[wl]] = xg[:, goal[wl]]
            j = (rng.random(L) * at).astype(np.int64)
            if np.any(named):
                goal[named] = goal[src[j[named]]]; xg[:, v[named]] = xg[:, goal[named]]
            goal[none] = np.where(rng.random(L) < 0.5, v, S * rng.integers(0, L, L))[none]
            kg[:, v] = u; kg[:, u] = goal; row = rng.integers(0, 6, L); kg[row[blood], mm[blood]] = u[blood]
            th[q, g, 0] = t0
    return pack(x, k, th, w)
def setup_inputs_ties(rng):
    x, k, th, w = parts(rng); x = rng.integers(0, 3, x.shape); x[:, 1::2] = rng.integers(0, 2, (N, 4, 16, B))
    crowd = rng.integers(0, B, (N, 8, 48)); j = rng.integers(0, 48, (N, 8, 16 * B))
    c = np.take_along_axis(crowd, j, 2).reshape(k.shape); m = rng.random(k.shape) < 0.6; m[:, 1::2] = False; k = np.where(m, c, k)
    th = rng.integers(3, 13, th.shape); one = int(rng.integers(0, 8)); x[:, one] = 255; th[:, one] = rng.integers(0, 2, (N, R))
    return pack(x, k, th, w)
def court(rng, xg, kg, t, goal, d):
    v = S * np.arange(L) + t; u = S * rng.permutation(L) + 3; base = rng.integers(0, 240, (16, L))
    xg[:, v] = base; xg[:, goal] = base + d // 16 + (np.arange(16)[:, None] < (d & 15))
    kg[8, v] = u; kg[(8 + t) & 15, u] = goal
def setup_inputs_turns(rng):
    x, k, th, w = parts(rng); own = np.arange(B); o = int(rng.integers(0, N)); towns = rng.permutation(8)[:4]; row = np.arange(16)[:, None]
    for full in range(2):
        q = (o + full) % N; t = 2 - full
        k[q, :, :6] = (k[q, :, :6] & -2) | (own & 1)
        count = 16 * rng.integers(1, 5, 8); count[int(rng.integers(0, 8))] += 15
        if full: count[:] = L
        th[q, :, 1] = 0
        for g in range(8):
            a, b = int(rng.integers(17, 100)), int(rng.integers(17, 100))
            d = np.where(rng.permutation(L) < count[g], rng.integers(0, a, L), a + rng.integers(0, 15, L))
            court(rng, x[q, g], k[q, g], 0, S * rng.permutation(L) + 3, d)
            d = np.where(rng.random(L) < 0.5, b - 1, b + rng.integers(0, 15, L))
            court(rng, x[q, g], k[q, g], t, S * rng.permutation(L) + 1 + full, d)
            th[q, g, 0] = a; th[q, g, t] = b
    for j in range(2, N):
        q = (o + j) % N
        for g in towns:
            xg, kg = x[q, g], k[q, g]
            high = int(rng.integers(200, 235)); y = rng.integers(0, 21, (8, B))
            xg[0::2] = high + y; xg[1::2] = high - y; xg += row < rng.integers(0, 16, B)
            low = int(rng.integers(20, 50)); y = rng.integers(0, 20, (8, L)); tight = np.zeros((16, L), np.int64)
            tight[0::2] = low + y; tight[1::2] = low - y; tight += row < rng.integers(0, 4, L)
            loose = np.clip(rng.integers(0, 71, L) + rng.integers(-8, 9, (16, L)), 0, 70)
            xg[:, S * np.arange(L)] = np.where(rng.random(L) < 0.5, tight, loose)
            kg += (kg & (S - 1)) == 0
            th[q, g, 0] = 16 * (high - low)
    return pack(x, k, th, w)
def check_inputs(d):
    bad = []
    for a, lo, hi in (("xf", 0, 255), ("kin", 0, B - 1), ("th", 0, 4095), ("w", 0, 255)):
        b = np.asarray(d[a]).astype(np.float64)
        if not (np.min(b) >= lo and np.max(b) <= hi): bad.append("range of " + a)
        if np.any(b != np.floor(b)): bad.append("whole numbers in " + a)
    return bad
def pick(a, ix):
    return np.stack([np.stack([np.take(a[q, g], ix[q, g], axis=1) for g in range(8)]) for q in range(N)])
def score(xc, xv):
    return np.add.reduce(np.abs(xc - xv[:, :, :, None, :]), axis=2)
def reference(xf, kin, th, w):
    X = np.zeros((N, 8, 16, W), np.int32); X[..., :B] = xf.astype(np.float32).reshape(N, 8, 16, B).astype(np.int32)
    K = np.zeros((N, 8, 16, W), np.int32); K[..., :B] = kin.reshape(N, 8, 16, B)
    wt = w.astype(np.int32).reshape(N, 8, 16, R); lane = np.arange(L, dtype=np.int32); last = np.zeros(N, np.int32)
    qa = np.arange(N).reshape(N, 1, 1, 1); ga = np.arange(8).reshape(1, 8, 1, 1); ka = np.arange(16).reshape(1, 1, 16, 1)
    for t in range(R):
        v = S * lane + t; n = B + L * t + lane; kv = K[..., v]; xv = X[..., v]
        c = K[qa, ga, (ka + t) & 15, kv]
        bar = ((c & (S - 1)) == t) | np.any(pick(K[:, :, :6], c) == kv[:, :, :6, None, :], axis=2)
        s = np.where(bar, 1000000, score(pick(X, c), xv))
        best = np.argmin(s, axis=2); low = np.min(s, axis=2); some = low < 1000000
        m = np.where(some, np.take_along_axis(c, best[:, :, None, :], 2)[:, :, 0], -1 - lane)
        taken = np.any((m[..., :, None] == m[..., None, :]) & (lane[:, None] > lane[None, :]), axis=3)
        wed = some & ~taken & (low < th[:, :, t][:, :, None] + (last & 15)[:, None, None])
        last = np.add.reduce(np.add.reduce(wed.astype(np.int32), axis=2), axis=1)
        ms = np.where(wed, m, v); km = pick(K, ms); xm = pick(X, ms)
        vb = np.broadcast_to(v, (N, 8, 1, L)); nb = np.broadcast_to(n, (N, 8, 1, L))
        child = np.concatenate([vb, ms[:, :, None, :], kv[:, :, 0:2], km[:, :, 0:2], nb, nb, kv[:, :, 7:8], km[:, :, 9:16]], axis=2)
        lost = (~wed).astype(np.int32); ask = ~wed & (np.add.accumulate(lost, axis=2) - lost < CAP)
        far = 1 + t % (N - 1); Kq = np.roll(K, -far, axis=0); Xq = np.roll(X, -far, axis=0)
        a = np.add.reduce(wt[..., t][..., None] * xv, axis=2) & (A - 1)
        cx = pick(Xq, pick(Kq, a)); bq = np.argmin(score(cx, xv), axis=2)
        near = np.take_along_axis(cx, bq[:, :, None, None, :], 3)[:, :, :, 0]
        X[..., n] = np.where(wed[:, :, None], (xv + xm) >> 1, np.where(ask[:, :, None], near, xv))
        K[..., n] = np.where(wed[:, :, None], child, kv)
        K[:, :, 6, v] = np.where(wed, m, kv[:, :, 6]); K[:, :, 7, v] = np.where(wed, n, kv[:, :, 7]); K[:, :, 9 + t, v] = np.where(ask, n, kv[:, :, 9 + t])
        qi, gi, li = np.nonzero(wed); mi = m[qi, gi, li]; K[qi, gi, 6, mi] = v[li]; K[qi, gi, 7, mi] = n[li]
    return {"yk": K.reshape(N, 128, W).astype(np.float32), "yx": np.ascontiguousarray(X[..., B:]).reshape(N, 128, R * L).astype(np.float32).astype(BF)}

@@ -1,0 +1,749 @@
+import numpy as np
+from concourse.mybir import dt, AluOpType, AxisListType, ActivationFunctionType
+
+A = AluOpType
+F = ActivationFunctionType
+B0, L, R, NR = 2304, 512, 3, 8
+W = B0 + R * L
+DUM = B0 + 2 * L
+CEN = 1920.0
+MAGIC = 12582912.0
+NG1, NBB, NRB, NDB, NCC = 8, 3, 5, 5, 8
+f32, bf, f16, i32, u16 = "float32", "bfloat16", "float16", "int32", "uint16"
+SB = {
+    "ki": ([B0], i32), "kk": ([L + W], f32), "xx": ([W], bf), "dtab": ([DUM], f32), "tt": ([DUM + 48], i32),
+    "rk0": ([2048], i32), "rk1": ([2048], f32), "rk2": ([2048], f32),
+    "rx0": ([B0], bf), "rx1": ([B0 + L], bf), "rx2": ([B0 + 2 * L], bf),
+    "cb": ([2560], f32), "nb": ([1536], f32), "pkv": ([L], i32),
+    "kvr": ([R, L], u16), "of1": ([R * L], u16), "cu": ([R * L], u16), "cc": ([NCC, 64], f16), "kp": ([L], bf),
+    "g1": ([NG1, L], f16), "gh": ([2, 2, L], f16), "gt": ([2, L], bf),
+    "bb": ([NBB, L, 2], bf), "rb": ([NRB, L, 2], bf), "db": ([NDB, L, 2], bf),
+    "xv": ([R, L], bf), "dv": ([2, L], f32), "xq": ([L], bf), "kv16": ([L], f16), "kve": ([L], f16),
+    "sc1": ([L], f32), "sc2": ([L], f32), "uu": ([L], bf), "sd1": ([272], f32), "li": ([2, L], bf),
+    "km": ([L], f32), "km16": ([L], f16), "xm16": ([L], f16), "cn": ([L], f16),
+    "ga": ([2048], bf), "ra": ([8, 256], bf), "xa": ([128], bf), "ai": ([2, 128], i32), "du": ([128], u16),
+    "sm": ([16, 32], f32), "si": ([6, 32], i32), "su": ([12, 32], u16), "m16": ([32], f16), "d1": ([32], bf),
+    "pc": ([4], i32), "col": ([48], f32), "ix": ([144], f32), "lane": ([L], f32),
+    "we": ([10, 144], bf), "weh": ([144], f16), "ws": ([16, 144], f16), "rr": ([16, 128], f16), "ll": ([16, 128], f16),
+    "mb": ([5, 128], bf), "mh": ([10, 128], f16), "blk": ([128], f32), "mask": ([32], f32),
+    "kc": ([2, L], bf), "rs0": ([L], bf), "rstk": ([L], bf), "dm0": ([L], bf), "rs1": ([272], bf), "scm": ([L], bf),
+    "ia": ([5, 32], f32), "itc": ([32], f16), "kq": ([128], f16),
+    "thi": ([4], i32), "thf": ([4], f32), "wi": ([4], i32), "l8": ([128], f32),
+}
+SCRATCH = {n: ("sbuf", [128] + s, d) for n, (s, d) in SB.items()}
+for _b in range(8):
+    SCRATCH["p%d" % _b] = ("psum", [128, 512], f32)
+NDS = 80
+SEMAPHORES = ["eV", "eA", "eP", "eG"] + ["q%d" % i for i in range(NDS)]
+SHAPES = {n: v[1] for n, v in SCRATCH.items()}
+SHAPES.update({"kin": [128, B0], "xf": [128, B0], "th": [8, R], "w": [128, R], "yk": [128, W], "yx": [128, R * L]})
+WIDE = {n: (2 if v[2] in (bf, f16, u16) else 4) for n, v in SCRATCH.items()}
+
+MODES = ["VAVAAVAA", "AAAVAAAA", "AAVAVAAAA"]
+CY, PCY, GAM, SIG = 1.04, 0.52, 1.56, 3.8
+LAT_X, LAT_S = 120.0, 60.0
+SEED, PEN, TRIES = 0, 12.0, 4000
+S_ = slice
+ALL = slice(None)
+
+
+def ap(n, *ix):
+    return (n, (ALL,) + ix)
+
+
+def pap(n, ps, *ix):
+    return (n, (ps,) + ix)
+
+
+def ind(win, off):
+    return ("*", win, off)
+
+
+_cache = {}
+
+
+def region(a):
+    key = repr(a)
+    if key not in _cache:
+        n, ix = a
+        sh = SHAPES[n]
+        ps = np.arange(sh[0])[ix[0]]
+        tot = int(np.prod(sh[1:]))
+        cs = np.arange(tot).reshape(sh[1:])[ix[1:]].reshape(-1)
+        pm = sum(1 << int(p) for p in ps)
+        bits = np.zeros(tot, np.uint8)
+        bits[cs] = 1
+        cm = int.from_bytes(np.packbits(bits, bitorder="little").tobytes(), "little")
+        _cache[key] = (n, pm, cm, len(cs), len(ps))
+    return _cache[key]
+
+
+def flat(xs):
+    out = []
+    for x in xs:
+        if isinstance(x, tuple):
+            out += [x[1], x[2]] if x[0] == "*" else [x]
+    return out
+
+
+def kof(t, j, e):
+    return (2 * j + e + (1 if t == 1 else 0)) % 16
+
+
+BOTH = (0, 1)
+DYN = [[(0, BOTH), (1, BOTH)], [(2, BOTH), (3, BOTH)], [(2, BOTH), (4, (0,)), (3, BOTH)]]
+STA = [[(j, BOTH) for j in range(2, 8)], [(j, BOTH) for j in (0, 1, 4, 5, 6, 7)], [(j, BOTH) for j in (0, 1, 5, 6, 7)] + [(4, (1,))]]
+
+
+def build():
+    ops = []
+
+    def add(alts, reads, writes, lat=0.0, kind="c", extra=None):
+        ops.append({"alts": alts, "r": [region(x) for x in flat(reads)], "w": [region(x) for x in flat(writes)],
+                    "lat": lat, "kind": kind, "extra": extra})
+
+    def split(out):
+        return ([out[2]], [out[1]]) if out[0] == "*" else ([], [out])
+
+    def vcost(out, ins, tt=False):
+        if out[0] == "*":
+            return 50 + region(out[2])[3] * 16 * SIG * CY
+        n = region(out)[3]
+        if ins[0][0] == "*":
+            return 50 + n * GAM * CY
+        if tt:
+            f = 1.0 if any(x[0][0] == "p" and x[0][1:].isdigit() for x in ins) else 2.0
+        else:
+            f = 0.5 if all(WIDE[x[0]] == 2 for x in [out] + ins) else 1.0
+        return max(64, n * f) * CY + 20
+
+    def acost(out, in_):
+        n = region(out)[3]
+        return 65 + n * GAM * CY if in_[0] == "*" else max(64, n) * CY + 40
+
+    def vop(name, out, args, ins, tt=False):
+        r, w = split(out)
+        add([("V", vcost(out, ins, tt), (name, [out] + args, {}))], r + [x for x in args if isinstance(x, tuple)], w)
+
+    def copy(out, in_):
+        vop("tensor_copy", out, [in_], [in_])
+
+    def tt(out, a, b, op):
+        vop("tensor_tensor", out, [a, b, op], [a, b], True)
+
+    def ts(out, a, s1, op0, s2=None, op1=None):
+        vop("tensor_scalar", out, [a, s1, s2, op0] + ([] if op1 is None else [op1]), [a])
+
+    def memset(out, c):
+        add([("V", max(64, region(out)[3] * WIDE[out[0]] / 4) * CY + 20, ("memset", [out, c], {}))], [], [out])
+
+    def scan(out, d0, d1, op0, op1):
+        vop("tensor_tensor_scan", out, [d0, d1, 0.0, op0, op1], [d0, d1])
+
+    def actalt(out, in_, func, scale, bias):
+        kw = {}
+        if scale is not None:
+            kw["scale"] = scale
+        if bias is not None:
+            kw["bias"] = bias
+        return ("A", acost(out, in_), ("activation", [out, in_, func], kw))
+
+    def act(out, in_, func, scale=None, bias=None):
+        add([actalt(out, in_, func, scale, bias)], [in_, scale, bias], [out])
+
+    def lin(out, in_, scale=None, bias=None, eng="VA"):
+        alts = []
+        if "A" in eng:
+            alts.append(actalt(out, in_, F.Identity, scale, bias))
+        if "V" in eng:
+            if scale is None and bias is None:
+                c = ("tensor_copy", [out, in_], {})
+            elif scale is None:
+                c = ("tensor_scalar", [out, in_, bias, None, A.add], {})
+            elif bias is None:
+                c = ("tensor_scalar", [out, in_, scale, None, A.mult], {})
+            else:
+                c = ("tensor_scalar", [out, in_, scale, bias, A.mult, A.add], {})
+            alts.append(("V", vcost(out, [in_]), c))
+        if "G" in eng:
+            n = region(out)[3]
+            alts.append(("G", 170 + 2 * CY * n, ("affine_select", [out, in_, [[0, n]], A.is_ge, 0.0, 0, 0], {})))
+        add(alts, [in_, scale, bias], [out])
+
+    def mm(lst, group=None):
+        cost = sum(max(64, region(x[2])[3]) * (WIDE[x[2][0]] ** 2 / 4) * PCY for x in lst)
+        add([("P", cost, ("mm", lst, {"group": group}))], [x[1] for x in lst] + [x[2] for x in lst], [x[0] for x in lst], lat=60.0)
+
+    def iota(out, pat, base, cm, extra=None):
+        kw = {} if SCRATCH[out[0]][2] == i32 else {"allow_small_or_imprecise_dtypes": True}
+        add([("G", 130 + 2 * CY * region(out)[3], ("iota", [out, pat, base, cm], kw))], [], [out], extra=extra)
+
+    def dma(pairs, q="Y"):
+        by = sum(region(o)[3] * region(o)[4] * WIDE.get(o[0], 2 if o[0] == "yx" else 4) for o, i in pairs)
+        add([(q, 60.0 * len(pairs), ("dma", pairs, {}))], [i for o, i in pairs], [o for o, i in pairs],
+            lat=1900 + by / 250.0 + 150 * len(pairs), kind="d")
+
+    def push(dst, src, t):
+        by = region(dst)[3] * 128 * WIDE[dst[0]]
+        add([("G", 300.0, ("push", [dst, src, t], {}))], [src], [dst], lat=2000 + by / 200.0, kind="p")
+
+    def P(b, *ix):
+        return ap("p%d" % b, *(ix if ix else (ALL,)))
+
+    def c1(i):
+        return ap("col", S_(i, i + 1))
+
+    def mk(k):
+        return ap("mask", S_(k, k + 1))
+
+    def wsl(name, i, r):
+        return ap(name, i, S_(15 - r, 143 - r))
+
+    def vcols(t):
+        return S_(t, 2048, 4)
+
+    def kk(a, b, step=1, ps=ALL):
+        return pap("kk", ps, S_(L + a, L + b, step))
+
+    dma([(ap("ki", S_(0, 1152)), ap("kin", S_(0, 1152))), (ap("ki", S_(1152, B0)), ap("kin", S_(1152, B0)))])
+    dma([(ap("xx", S_(0, B0)), ap("xf", ALL))])
+    dma([(pap("thi", S_(0, 8), S_(0, R)), ap("th", ALL)), (ap("wi", S_(0, R)), ap("w", ALL))])
+
+    PM, PG, C15, M67, N67, SCN, SVN, M06, WYC, DE, DO, GE9 = range(12)
+    BCN, BVN, NASK, WF, TH, THR = 12, 15, 18, 21, 24, 27
+    TOT = 30
+    iota(ap("pc", S_(0, 1)), [[0, 1]], 0, 1, 1e6)
+    iota(ap("ix", ALL), [[1, 144]], 0, 0, 1e6)
+    ts(ap("pc", S_(1, 2)), ap("pc", S_(0, 1)), 15, A.bitwise_and)
+    ts(ap("pc", S_(2, 3)), ap("pc", S_(0, 1)), 4, A.arith_shift_right)
+    copy(ap("col", S_(0, 2)), ap("pc", S_(1, 3)))
+    ts(c1(C15), c1(PG), 16.0, A.mult, 15.0, A.add)
+    ts(ap("mask", S_(0, 16)), ap("ix", S_(0, 16)), c1(PM), A.is_equal)
+    ts(ap("mask", S_(16, 32)), ap("mask", S_(0, 16)), -CEN, A.mult)
+    ts(c1(M67), mk(6), 1.0, A.mult, mk(7), A.add)
+    ts(c1(N67), c1(M67), -1.0, A.mult, 1.0, A.add)
+    ts(c1(SCN), mk(0), 4.0, A.mult, c1(M67), A.add)
+    ts(c1(M06), c1(PM), 6.5, A.is_lt, 131072.0, A.mult)
+    ts(c1(WYC), mk(1), -1024.0, A.mult, mk(0), A.add)
+    ts(c1(31), mk(1), 1024.0, A.mult)
+    ts(c1(DE), c1(PM), float(DUM), A.add)
+    ts(c1(DO), c1(PM), float(DUM + 16), A.add)
+    ts(c1(GE9), c1(PM), 8.5, A.is_gt)
+    ts(c1(32), c1(PM), 16.0, A.mult)
+    copy(c1(33), ap("pc", S_(0, 1)))
+    for t in range(R):
+        n0 = B0 + L * t
+        ts(c1(34 + t), mk(0), t - CEN, A.mult)
+        ts(c1(BCN + t), c1(M67), n0 - CEN, A.mult, c1(34 + t), A.add)
+        ts(c1(NASK + t), mk(9 + t), -1.0, A.mult, 1.0, A.add)
+    copy(ap("col", S_(WF, WF + R)), ap("wi", S_(0, R)))
+    E32, EM16, E16, EBAR, E2048, EY, EZ, EW = range(8)
+    for i, c in [(E32, 32.0), (EM16, -16.0), (E16, 16.0), (EBAR, c1(M06)), (E2048, 2048.0), (EY, c1(WYC)), (EZ, c1(31)),
+                 (EW, c1(WF)), (EW + 1, c1(WF + 1)), (EW + 2, c1(WF + 2))]:
+        ts(ap("we", i, ALL), ap("ix", ALL), c1(C15), A.is_equal, c, A.mult)
+    ts(ap("weh", ALL), ap("ix", ALL), c1(C15), A.is_equal)
+    for k in range(16):
+        lin(ap("ws", k, ALL), ap("weh", ALL), scale=mk(k))
+    iota(ap("blk", ALL), [[1, 8], [0, 16]], 0, 0, 1e6)
+    ts(ap("blk", ALL), ap("blk", ALL), c1(PG), A.is_equal, 1.0 / 64, A.mult)
+    for k in range(16):
+        lin(ap("rr", k, ALL), ap("blk", ALL), scale=mk(k))
+    add([("G", 170 + 2 * CY * 2048, ("affine_select", [ap("ll", ALL), ap("rr", ALL), [[0, 16], [-1, 128]], A.not_equal, -1.0 / 64, 0, 1], {}))],
+        [ap("rr", ALL)], [ap("ll", ALL)])
+    IB, NIB, HIB, ZB, ONB = [ap("mb", i, ALL) for i in range(5)]
+    IH, HIH, NI64, DN67, P1, P2, D9 = [ap("mh", i, ALL) for i in range(7)]
+    ix128 = ap("ix", S_(0, 128))
+    for m, c in [(IB, 1.0), (NIB, -1.0), (HIB, -0.5), (IH, 1.0), (HIH, 0.5), (NI64, -1.0 / 64), (DN67, c1(N67)), (D9, c1(GE9)),
+                 (ap("mh", 7, ALL), c1(NASK)), (ap("mh", 8, ALL), c1(NASK + 1)), (ap("mh", 9, ALL), c1(NASK + 2))]:
+        ts(m, ix128, c1(33), A.is_equal, c, A.mult)
+    memset(ZB, 0.0)
+    memset(ONB, 1.0 / 8192)
+    tt(P1, wsl("ws", 0, 2), wsl("ws", 1, 3), A.add)
+    tt(P1, P1, wsl("ws", 7, 8), A.add)
+    tt(P2, wsl("ws", 0, 4), wsl("ws", 1, 5), A.add)
+    tt(P2, P2, D9, A.add)
+    iota(ap("kc", 0, ALL), [[0, 32], [1, 2], [2, 8]], 0, 0)
+    iota(ap("dtab", S_(0, B0)), [[0, B0 // 4], [1, 4]], 0, 0)
+    iota(ap("dtab", S_(B0, DUM)), [[0, 2 * L // 4], [1, 4]], 0, 0)
+    iota(ap("uu", ALL), [[0, 32], [1, 16]], 0, 0)
+    iota(ap("kc", 1, ALL), [[0, 32], [1, 2], [2, 8]], 1, 0)
+    memset(ap("kc", 1, S_(15, L, 16)), 0.0)
+    ts(ap("rs0", ALL), ap("uu", ALL), 0.0, A.is_equal)
+    ts(ap("rstk", ALL), ap("uu", ALL), 0.0, A.is_equal, 16777216.0, A.mult)
+    ts(ap("dm0", ALL), ap("uu", ALL), c1(PM), A.is_gt, 61.0, A.mult)
+    ts(ap("scm", ALL), ap("uu", ALL), 0.0, A.mult, mk(0), A.add)
+    ts(ap("kp", ALL), ap("uu", ALL), -4096.0, A.mult, 65536.0, A.add)
+    memset(ap("rs1", ALL), 0.0)
+    memset(ap("rs1", S_(0, 272, 17)), 1.0)
+    iota(ap("lane", ALL), [[1, L]], 0, 0)
+    iota(ap("tt", S_(0, DUM + 32)), [[0, DUM + 32]], 0, 0)
+    iota(ap("tt", S_(DUM + 32, DUM + 48)), [[0, 16]], -1, 0)
+    iota(ap("ia", 0, ALL), [[16, 32]], 0, 0)
+    iota(ap("ia", 1, ALL), [[0, 16], [16, 2]], 0, 0)
+    ts(ap("itc", ALL), ap("ia", 0, ALL), c1(PM), A.add, -1535.0, A.add)
+    ts(ap("ia", 1, ALL), ap("ia", 1, ALL), c1(DE), A.add)
+    ts(ap("ia", 2, ALL), ap("ia", 0, ALL), c1(PM), A.add, -float(L), A.add)
+    iota(ap("blk", ALL), [[256, 8], [1, 16]], 0, 0)
+    ts(ap("kq", ALL), ap("blk", ALL), c1(32), A.add)
+    iota(ap("nb", S_(512, 1536)), [[0, 1024]], 0, 0)
+    p8 = S_(0, 8)
+    iota(pap("l8", p8, ALL), [[1, 8], [0, 16]], 0, -1)
+    ts(pap("l8", p8, ALL), pap("l8", p8, ALL), 0.0, A.is_equal)
+    copy(pap("thf", p8, S_(0, R)), pap("thi", p8, S_(0, R)))
+    mm([(P(7, S_(0, R)), pap("l8", p8, ALL), pap("thf", p8, S_(0, R)))])
+    ts(ap("col", S_(TH, TH + R)), P(7, S_(0, R)), 16.0, A.mult, -1.0, A.add)
+
+    def lists(t):
+        copy(ap("kvr", t, S_(0, L, 2)), ap("ki", S_(t, 1024, 4)))
+        copy(ap("kvr", t, S_(1, L, 2)), ap("ki", S_(1024 + t, 2048, 4)))
+        js = STA[t]
+        groups = [[x] for x in js] if t == 0 else [js[:2], js[2:]]
+        for gr in groups:
+            dma([(o1(t, j, e), pap("kvr", S_(kof(t, j, e), 128, 16), t, ALL)) for j, es in gr for e in es])
+
+    def o1(t, j, e):
+        c = t * L + 64 * j + 32 * e
+        return ap("of1", S_(c, c + 32))
+
+    def cu(t, j, e=None):
+        c = t * L + 64 * j
+        return ap("cu", S_(c, c + 64)) if e is None else ap("cu", S_(c + 32 * e, c + 32 * e + 32))
+
+    def rows06(c0, c1_):
+        dma([(pap("dtab", S_(j, 128, 16), S_(c0, c1_)), kk(c0, c1_, 1, S_(j, 128, 16))) for j in range(6)])
+
+    lists(0)
+    lin(kk(0, 1152), ap("ki", S_(0, 1152)))
+    lin(kk(1152, B0), ap("ki", S_(1152, B0)))
+    rows06(0, B0)
+    push(ap("rk0", ALL), ap("ki", S_(0, 2048)), 0)
+    for t in range(R):
+        push(ap("rx%d" % t, S_(0, B0)), ap("xx", S_(0, B0)), t)
+        lin(ap("xv", t, ALL), ap("xx", vcols(t)), eng="G" if t else "VA")
+    dma([(pap("yk", S_(j, 128, 16), S_(0, B0)), kk(0, B0, 1, S_(j, 128, 16))) for j in range(16) if j not in (6, 7, 9, 10, 11)])
+    for t in range(R):
+        mm([(P(6, S_(0, 32)), wsl("we", EW + t, r), ap("xv", t, S_(r, L, 16))) for r in range(16)])
+        copy(ap("si", 2, ALL), P(6, S_(0, 32)))
+        ts(ap("si", 3, ALL), ap("si", 2, ALL), 2047, A.bitwise_and)
+        copy(ap("su", t, ALL), ap("si", 3, ALL))
+
+    cnt = {"g1": 0, "bb": 0, "rb": 0, "db": 0, "cc": 0, "gt": 0, "gh": 0}
+
+    def nxt(n, m):
+        cnt[n] += 1
+        return (cnt[n] - 1) % m
+
+    def cpp(t, j, e):
+        return P(2 + t % 2, S_(j + 8 * e, L, 16))
+
+    def es_(es):
+        return S_(32 * es[0], 32 * es[-1] + 32)
+
+    def numbers(t, j, es, s):
+        mm([(cpp(t, j, e), IH, ap("cc", s, S_(32 * e, 32 * e + 32))) for e in es], ("c", t))
+
+    def names_static(t, j, es):
+        s = nxt("cc", NCC)
+        prs = []
+        for e in es:
+            g = nxt("g1", NG1)
+            lin(ap("g1", g, ALL), ind(ap("ki", S_(0, B0)), o1(t, j, e)), bias=-CEN)
+            prs.append((ap("cc", s, S_(32 * e, 32 * e + 32)), pap("g1", S_((kof(t, j, e) + t) % 16, 128, 16), g, ALL)))
+        dma(prs)
+        ts(cu(t, j, None if len(es) == 2 else es[0]), ap("cc", s, es_(es)), CEN, A.add)
+        numbers(t, j, es, s)
+
+    def list_pe(t, j, e, src, b):
+        k = kof(t, j, e)
+        mm([(P(b, S_(0, 32)), wsl("ws", k, r), ap(src, S_(r, L, 16))) for r in range(16)])
+        ts(o1(t, j, e), P(b, S_(0, 32)), CEN, A.add)
+
+    def names_dyn(t, j, es, b):
+        s = nxt("gh", 2)
+        for e in es:
+            kr = (kof(t, j, e) + t) % 16
+            lin(ap("gh", s, e, ALL), ind(kk(0, B0 + L * t) if t else ap("ki", ALL), o1(t, j, e)), scale=mk(kr), bias=mk(16 + kr))
+        mm([(P(b, es_(es)), ap("weh", S_(15 - r, 143 - r)), ap("gh", s, S_(es[0], es[-1] + 1), S_(r, L, 16))) for r in range(16)])
+        ts(cu(t, j, None if len(es) == 2 else es[0]), P(b, es_(es)), CEN, A.add)
+        s = nxt("cc", NCC)
+        lin(ap("cc", s, es_(es)), P(b, es_(es)), eng="V")
+        numbers(t, j, es, s)
+
+    def score(t, j, es, dyn):
+        wd = B0 + (L * t if dyn else 0)
+        mode = MODES[t][j if dyn or len(es) == 2 else 8]
+        rs, ds = nxt("rb", NRB), nxt("db", NDB)
+        xw = ap("xx", S_(0, wd))
+        ee = S_(es[0], es[-1] + 1)
+        terms = []
+        if mode == "A":
+            for e in es:
+                g = nxt("gt", 2)
+                act(ap("gt", g, ALL), ind(xw, cu(t, j, e)), F.Identity)
+                mm([(P(4 + g), IB, ap("gt", g, ALL)), (P(4 + g), NIB, ap("xv", t, ALL))])
+                act(ap("rb", rs, ALL, e), P(4 + g), F.Abs)
+            terms.append((E16, "rb", rs))
+        else:
+            bs = nxt("bb", NBB)
+            for e in es:
+                tt(ap("bb", bs, ALL, e), ind(xw, cu(t, j, e)), ap("xv", t, ALL), A.subtract)
+            if mode == "V":
+                ts(ap("rb", rs, ALL, ee), ap("bb", bs, ALL, ee), 0.0, A.max)
+                terms += [(EM16, "bb", bs), (E32, "rb", rs)]
+            else:
+                act(ap("rb", rs, ALL, ee), ap("bb", bs, ALL, ee), F.Abs)
+                terms.append((E16, "rb", rs))
+        for e in es:
+            tt(ap("db", ds, ALL, e), ind(ap("dtab", S_(0, wd)), cu(t, j, e)), ap("dv", t % 2, ALL), A.is_equal)
+        terms.append((EBAR, "db", ds))
+        o = P(t % 2, S_(j, L, 8)) if len(es) == 2 else P(t % 2, S_(j + 8 * es[0], L, 16))
+        for w_, n, s in terms:
+            mm([(o, wsl("we", w_, r), ap(n, s, S_(r, L, 16), ee)) for r in range(16)], ("k", t))
+
+    def opens(t):
+        mm([(P(t % 2), IB, ap("kc", t % 2, ALL))], ("k", t))
+        mm([(P(2 + t % 2), IB, ap("kp", ALL))], ("c", t))
+
+    def sm(i, *ix):
+        return ap("sm", i, *(ix if ix else (ALL,)))
+
+    def su(i, *ix):
+        return ap("su", i, *(ix if ix else (ALL,)))
+
+    MU, GO, SO, RO, ONEW, OVC, MSD, NO = range(3, 11)
+
+    def prepare(t):
+        src = kk(t, 2048, 4)
+        if t:
+            lin(ap("kv16", ALL), src, bias=-CEN)
+            for j, es in DYN[t]:
+                for e in es:
+                    if kof(t, j, e) in (6, 7):
+                        list_pe(t, j, e, "kv16", 6 + e)
+        lin(ap("cb", S_(1024, 1536)), src, eng="G")
+        dma([(ap("cb", S_(1536, 2048)), ap("cb", S_(1024, 1536)))])
+        lin(ap("cn", ALL), ap("lane", ALL), scale=c1(SCN), bias=c1(BCN + t))
+        lin(ap("xq", ALL), ap("xv", t, ALL), scale=4096.0)
+        mm([(P(7), ap("mh", 7 + t, ALL), ap("kv16", ALL)), (P(7), wsl("ws", 7, 9 + t), ap("cn", ALL))])
+        lin(ap("cb", S_(2048, 2560)), P(7), bias=CEN)
+        tt(ap("pkv", ALL), ind(ap("rk%d" % t, ALL), su(t)), ap("xq", ALL), A.add)
+
+    def early(t):
+        lin(ap("kve", ALL), ap("ki", vcols(t)), bias=-CEN)
+        for j, es in DYN[t]:
+            for e in es:
+                if kof(t, j, e) not in (6, 7):
+                    list_pe(t, j, e, "kve", 4 + e)
+
+    def tail(t):
+        n0 = B0 + L * t
+        thr = c1(TH) if t == 0 else c1(THR + t)
+        ends = S_(15, L, 16)
+        kb, cb_ = t % 2, 2 + t % 2
+        scan(ap("sc1", ALL), ap("rstk", ALL), P(kb), A.add, A.min)
+        tt(ap("uu", ALL), P(kb), ap("sc1", ALL), A.not_equal)
+        scan(ap("sc2", ALL), ap("uu", ALL), P(cb_), A.mult, A.max)
+        ts(sm(0), ap("sc1", ends), -131071.0, A.add, 8192.0, A.mult)
+        ts(sm(1), ap("sc1", ends), thr, A.subtract, 8192.0, A.mult)
+        ts(ap("si", 0, ALL), ap("sc2", ends), CEN, A.add)
+        M = ap("si", 1, ALL)
+        ts(M, ap("si", 0, ALL), 4095, A.bitwise_and)
+        tt(sm(2), M, sm(0), A.max)
+        tt(sm(3), sm(2), ap("ia", 1, ALL), A.min)
+        ts(ap("m16", ALL), sm(3), -CEN, A.add)
+        copy(su(MU), M)
+        tt(sm(4), M, sm(1), A.max)
+        ts(su(GO), sm(4), float(DUM + 32), A.min)
+        m16 = ap("m16", ALL)
+        mm([(P(6), IB, ap("dm0", ALL))], ("d0", t))
+        mm([(P(6, S_(r + 1, L, 16)), ap("ll", r, ALL), m16) for r in range(15)], ("d0", t))
+        mm([(P(7, S_(0, 272)), ZB, ap("rs1", ALL))], ("d1", t))
+        mm([x for r in range(16) for x in ((P(7, S_(r + 1, 272, 17)), ap("rr", r, ALL), ap("m16", S_(0, 32, 2))),
+                                           (P(7, S_(r + 1, 272, 17)), NI64, ap("m16", S_(1, 32, 2))))], ("d1", t))
+        act(ap("km16", ALL), ind(kk(0, n0), su(MU)), F.Identity, bias=-CEN)
+        act(ap("xm16", ALL), ind(ap("xx", S_(0, n0)), su(MU)), F.Identity, bias=-0.5)
+        scan(ap("sc2", ALL), P(6), ap("rs0", ALL), A.mult, A.add)
+        scan(ap("sd1", ALL), P(7, S_(0, 272)), ap("rs1", ALL), A.mult, A.add)
+        mm([(P(kb), DN67, ap("kv16", ALL)), (P(kb), wsl("ws", 7, 7), ap("cn", ALL))] +
+           [(P(kb, S_(r, L, 16)), wsl("ws", r, 6), m16) for r in range(16)])
+        act(ap("cb", S_(512, 1024)), P(kb), F.Identity, bias=CEN)
+        mm([(P(cb_), P1, ap("kv16", ALL)), (P(cb_), IH, ap("cn", ALL)), (P(cb_), P2, ap("km16", ALL))] +
+           [(P(cb_, S_(r, L, 16)), wsl("ws", r, 1), m16) for r in range(16)])
+        act(ap("cb", S_(0, 512)), P(cb_), F.Identity, bias=CEN)
+        mm([(P(7), DN67, ap("km16", ALL)), (P(7), wsl("ws", 0, 6), ap("cn", ALL)), (P(7), wsl("ws", 7, 7), ap("cn", ALL))])
+        act(ap("km", ALL), P(7), F.Identity, bias=CEN)
+        mm([(P(kb), HIH, ap("xm16", ALL)), (P(kb), HIB, ap("xv", t, ALL))])
+        ts(ap("nb", S_(0, 512)), P(kb), MAGIC, A.add, -MAGIC, A.add)
+        ts(sm(5), ap("sc2", ends), 0.0, A.is_equal, 8192.0, A.mult)
+        ts(sm(6, S_(0, 16)), ap("sd1", S_(16, 272, 17)), 0.0, A.is_equal, 8192.0, A.mult)
+        tt(sm(7), sm(3), sm(5), A.max)
+        tt(sm(6, S_(16, 32)), sm(7, S_(1, 32, 2)), sm(6, S_(0, 16)), A.max)
+        ts(su(SO, S_(1, 32, 2)), sm(6, S_(16, 32)), c1(DO), A.min)
+        ts(su(SO, S_(0, 32, 2)), sm(7, S_(0, 32, 2)), c1(DE), A.min)
+        tw = ap("tt", ALL)
+        for a in range(15, -1, -1):
+            copy(ind(tw, su(SO, S_(2 * a, 2 * a + 2))), ap("lane", S_(32 * a, 32 * a + 32)))
+        tt(ap("li", 0, ALL), ind(tw, su(GO)), ap("lane", ALL), A.not_equal)
+        scan(ap("li", 1, ALL), ap("scm", ALL), ap("li", 0, ALL), A.mult, A.add)
+        Y, Z = P(6, S_(0, 32)), P(7, S_(32, 64))
+        mm([(Y, wsl("we", EY, r), ap("li", 1, S_(r, L, 16))) for r in range(16)])
+        mm([(Z, IH, ap("itc", ALL))] + [(Z, wsl("we", EZ, r), ap("li", 1, S_(r, L, 16))) for r in range(16)])
+        ts(sm(8), Y, -896.0, A.is_gt, 4096.0, A.mult)
+        tt(sm(9), sm(8), Y, A.add)
+        tt(sm(10), sm(9), Z, A.min)
+        ts(su(RO), sm(10), 1535.0, A.add)
+        ts(su(ONEW), Z, 1535.0, A.add)
+        ts(ap("d1", ALL), Y, 0.0, A.is_lt, 8192.0, A.mult)
+        ts(sm(11), Y, -896.0, A.is_le, 512.0, A.mult)
+        tt(sm(12), sm(11), Z, A.add)
+        ts(su(OVC), sm(12), 1535.0, A.add)
+        tt(sm(13), M, ap("d1", ALL), A.subtract)
+        tt(sm(14), sm(13), ap("ia", 2, ALL), A.max)
+        ts(su(MSD), sm(14), float(L), A.add)
+        copy(ind(ap("tt", S_(0, 1536)), su(RO)), ap("pkv", ALL))
+        lin(kk(t, 2048, 4), ind(ap("cb", S_(512, 2560)), su(OVC)))
+        lin(kk(n0, n0 + L), ind(ap("cb", S_(0, 1536)), su(ONEW)))
+        copy(ind(kk(-L, n0), su(MSD)), ap("km", ALL))
+        if t + 1 < R:
+            mm([(P(7, S_(0, 32)), ONB, ap("d1", ALL))])
+            add([("V", 90.0, ("tensor_reduce", [c1(TOT), P(7, S_(0, 32)), AxisListType.X, A.add], {}))], [P(7, S_(0, 32))], [c1(TOT)])
+            ts(ap("pc", S_(3, 4)), c1(TOT), -1.0, A.mult, 4096.0, A.add)
+            ts(ap("pc", S_(3, 4)), ap("pc", S_(3, 4)), 15, A.bitwise_and)
+            ts(c1(THR + t + 1), ap("pc", S_(3, 4)), 16.0, A.mult, c1(TH + t + 1), A.add)
+            rows06(n0, n0 + L)
+            push(ap("rk%d" % (t + 1), ALL), kk(0, 2048), t + 1)
+        st = [(pap("yk", S_(9 + t, 128, 16), S_(0, B0)), kk(0, B0, 1, S_(9 + t, 128, 16)))]
+        if t + 1 == R:
+            dma(st + [(pap("yk", S_(j, 128, 16), S_(0, n0)), kk(0, n0, 1, S_(j, 128, 16))) for j in (6, 7)])
+            st = []
+        dma(st + [(ap("yk", S_(n0, n0 + L)), kk(n0, n0 + L))])
+        slot = ap("tt", S_(512, 640))
+        ts(ap("ai", 0, ALL), slot, 4095, A.bitwise_and)
+        copy(ap("du", ALL), ap("ai", 0, ALL))
+        ts(ap("ai", 1, ALL), slot, 12, A.arith_shift_right)
+        copy(ap("xa", ALL), ap("ai", 1, ALL))
+        banks = [cb_, kb, 6, 7]
+        for b in range(4):
+            gb = ap("ga", S_(L * b, L * b + L))
+            lin(gb, ind(ap("rx%d" % t, ALL), ap("du", S_(32 * b, 32 * b + 32))))
+            mm([(P(banks[b]), ZB, ap("rs0", ALL))], ("a", t, b))
+            mm([(P(banks[b], S_(k, L, 16)), NIB, ap("xa", S_(32 * b, 32 * b + 32))) for k in range(16)], ("a", t, b))
+            mm([(P(banks[b]), IB, gb)], ("a", t, b))
+            act(ap("ra", S_(2 * b, 2 * b + 2), ALL), P(banks[b]), F.Abs)
+        o = P(cb_, S_(0, 128))
+        for h in range(2):
+            oh = P(cb_, S_(64 * h, 64 * h + 64))
+            mm([(oh, IH, ap("kq", S_(64 * h, 64 * h + 64)))] +
+               [(oh, wsl("we", E2048, r), ap("ra", S_(4 * h, 4 * h + 4), S_(16 * r, 16 * r + 16))) for r in range(16)])
+        scan(ap("sc1", S_(0, 128)), ap("rstk", S_(0, 128)), o, A.add, A.min)
+        copy(ap("si", 4, S_(0, 8)), ap("sc1", S_(15, 128, 16)))
+        ts(ap("si", 5, S_(0, 8)), ap("si", 4, S_(0, 8)), 2047, A.bitwise_and)
+        copy(su(NO, S_(0, 8)), ap("si", 5, S_(0, 8)))
+        tt(ap("nb", S_(512, 640)), ind(ap("ga", ALL), su(NO, S_(0, 8))), ap("xa", ALL), A.subtract)
+        tt(ap("xx", S_(n0, n0 + L)), ind(ap("nb", ALL), su(RO)), ap("xv", t, ALL), A.add)
+        dma([(ap("yx", S_(L * t, L * t + L)), ap("xx", S_(n0, n0 + L)))])
+        for u in range(t + 1, R):
+            push(ap("rx%d" % u, S_(n0, n0 + L)), ap("xx", S_(n0, n0 + L)), u)
+
+    def statics(t):
+        js = STA[t]
+        if t:
+            lin(ap("dv", t % 2, ALL), ap("dtab", vcols(t)), eng="G")
+        for i in range(len(js) + 2):
+            if i < len(js):
+                names_static(t, *js[i])
+            if i >= 2:
+                score(t, js[i - 2][0], js[i - 2][1], False)
+
+    opens(0)
+    lin(ap("kv16", ALL), ap("ki", vcols(0)), bias=-CEN)
+    lin(ap("dv", 0, ALL), ap("dtab", vcols(0)), eng="G")
+    for j, es in DYN[0]:
+        for e in es:
+            list_pe(0, j, e, "kv16", 4 + e)
+        names_dyn(0, j, es, 6 + j % 2)
+    for j, es in DYN[0]:
+        score(0, j, es, True)
+    statics(0)
+    prepare(0)
+    for t in range(R):
+        if t + 1 < R:
+            opens(t + 1)
+            lists(t + 1)
+            early(t + 1)
+            statics(t + 1)
+        tail(t)
+        if t + 1 < R:
+            prepare(t + 1)
+            for i, (j, es) in enumerate(DYN[t + 1]):
+                names_dyn(t + 1, j, es, 6 + i % 2)
+            for j, es in DYN[t + 1]:
+                score(t + 1, j, es, True)
+    return ops
+
+
+def depend(ops):
+    hist = {}
+    for i, o in enumerate(ops):
+        deps = {}
+        fixed = o["alts"][0][0] if len(o["alts"]) == 1 else None
+        for regs, wr in ((o["r"], False), (o["w"], True)):
+            for n, pm, cm, _1, _2 in regs:
+                bank = n[0] == "p" and n[1:].isdigit()
+                for j, pj, cj, wj, ej in hist.get(n, []):
+                    if j == i:
+                        continue
+                    over = (pm & pj) and (cm & cj)
+                    if (over and (wr or wj)) or (bank and (ej is None or ej != fixed)):
+                        deps[j] = deps.get(j, False) or bool(over and wj and not wr)
+        for regs, wr in ((o["r"], False), (o["w"], True)):
+            for n, pm, cm, _1, _2 in regs:
+                h = hist.setdefault(n, [])
+                if wr:
+                    h[:] = [x for x in h if x[0] == i or (x[1] & ~pm) or (x[2] & ~cm)]
+                h.append((i, pm, cm, wr, fixed))
+        o["deps"] = deps
+
+
+def schedule(ops, jit, force):
+    n = len(ops)
+    succ = [[] for _ in range(n)]
+    for i, o in enumerate(ops):
+        for j in o["deps"]:
+            succ[j].append(i)
+    prio = [0.0] * n
+    for i in range(n - 1, -1, -1):
+        o = ops[i]
+        prio[i] = (min(a[1] for a in o["alts"]) + o["lat"] + LAT_X) + jit[i] + max([prio[s] for s in succ[i]] + [0.0])
+        if o["extra"]:
+            prio[i] += o["extra"]
+    busy = {e: [] for e in "VAPGY"}
+    fin, eng, start = [0.0] * n, [None] * n, [0.0] * n
+    for i in sorted(range(n), key=lambda i: -prio[i]):
+        best = None
+        o_g = ops[i]["alts"][0][2][2].get("group")
+        for a in ops[i]["alts"]:
+            e = a[0]
+            if force[i] and e != force[i]:
+                continue
+            s = max([fin[j] - 60.0 if o_g and o_g == ops[j]["alts"][0][2][2].get("group") else fin[j] + (LAT_S if eng[j] == e and ops[j]["kind"] == "c" else LAT_X) for j in ops[i]["deps"]] + [0.0])
+            bz = busy[e]
+            k = len(bz)
+            while k > 0 and bz[k - 1][1] > s:
+                k -= 1
+            while k < len(bz) and s + a[1] > bz[k][0]:
+                s = max(s, bz[k][1])
+                k += 1
+            f = s + a[1] * (PEN if e == "V" else 1.0)
+            if best is None or f < best[0]:
+                best = (f, s, k, a)
+        _f, s, k, a = best
+        busy[a[0]].insert(k, (s, s + a[1]))
+        eng[i], start[i], fin[i] = a[0], s, s + a[1] + ops[i]["lat"]
+        ops[i]["pick"] = a
+    return sorted(range(n), key=lambda i: start[i]), start, fin
+
+
+def search(ops, seed, tries, nj=6, amp=1500.0, temp=50.0):
+    rng = np.random.RandomState(seed)
+    n = len(ops)
+    free = [i for i in range(n) if len(ops[i]["alts"]) > 1]
+    jit, force = [0.0] * n, [None] * n
+    cur = best = max(schedule(ops, jit, force)[2])
+    keep = (jit, force)
+    for k in range(tries):
+        j2, f2 = list(jit), list(force)
+        for i in rng.randint(0, n, nj):
+            j2[i] = max(0.0, j2[i] + amp * float(rng.standard_normal()))
+        for i in rng.randint(0, len(free), 2):
+            f2[free[i]] = (None, "V", "A")[rng.randint(0, 3)]
+        m = max(schedule(ops, j2, f2)[2])
+        if m <= cur + temp * (1 - k / tries) * float(rng.exponential()):
+            cur, jit, force = m, j2, f2
+            if m < best:
+                best, keep = m, (j2, f2)
+    return schedule(ops, *keep)
+
+
+_plan = []
+
+
+def plan():
+    if not _plan:
+        ops = build()
+        depend(ops)
+        _plan.append((ops,) + search(ops, SEED, TRIES))
+    return _plan[0]
+
+
+def rank_program(g, core, T, topo):
+    rank = T.rank_of(core)
+    if rank is None:
+        return
+    ops, order = plan()[0:2]
+    Q = {"V": g.vector, "A": g.scalar, "P": g.tensor, "G": g, "Y": g.sync}
+    calls = {"tensor_copy": g.vector.tensor_copy, "tensor_tensor": g.vector.tensor_tensor, "tensor_scalar": g.vector.tensor_scalar,
+             "memset": g.vector.memset, "tensor_tensor_scan": g.vector.tensor_tensor_scan, "tensor_reduce": g.vector.tensor_reduce,
+             "activation": g.scalar.activation, "iota": g.iota, "affine_select": g.affine_select}
+
+    def real(x):
+        if isinstance(x, tuple):
+            return real(x[1]).indirect(real(x[2])) if x[0] == "*" else T[x[0]][x[1]]
+        return x
+
+    count = {e: 0 for e in "VAPG"}
+    seen = {e: {} for e in Q}
+    done, total, nq, size = {}, {}, [0], {}
+    for o in ops:
+        gr = o["pick"][2][2].get("group")
+        size[gr] = size.get(gr, 0) + 1
+    left = dict(size)
+
+    def fresh():
+        nq[0] += 1
+        return "q%d" % (nq[0] - 1)
+
+    for i in order:
+        o = ops[i]
+        e, _c, (name, args, kw) = o["pick"]
+        need = {}
+        for j, raw in o["deps"].items():
+            if kw.get("group") and kw["group"] == ops[j]["pick"][2][2].get("group"):
+                continue
+            s, v = done[j][1 if raw else 0]
+            need[s] = max(need.get(s, 0), v)
+        for s, v in need.items():
+            if seen[e].get(s, 0) < v:
+                Q[e].wait_ge(T.sem[s], v)
+                seen[e][s] = v
+        if name == "dma":
+            s = fresh()
+            for out, in_ in args:
+                Q[e].dma_start(real(out), real(in_)).then_inc(T.sem[s], 16)
+            total[s] = 16 * len(args)
+            done[i] = ((s, total[s]), (s, total[s]))
+        elif name == "push":
+            dst = T.cores[(rank - 1 - args[2]) % NR]
+            rid, pid, _s = topo.addr(dst)
+            sl, sr = fresh(), fresh()
+            g.remote_dma(real(args[0]), real(args[1]), T.sem[sr], T.sem[sl], pid, rid, topo.mask(core, dst))
+            total[sl] = total[sr] = len(topo.engines(core, dst))
+            done[i] = ((sl, total[sl]), (sr, total[sr]))
+        else:
+            if name == "mm":
+                gr = kw["group"]
+                first = gr is None or left[gr] == size[gr]
+                last = gr is None or left[gr] == 1
+                if gr is not None:
+                    left[gr] -= 1
+                for k, (out, lt, rh) in enumerate(args):
+                    ins = g.tensor.matmul(real(out), real(lt), real(rh), k == 0 and first, k == len(args) - 1 and last)
+            else:
+                ins = calls[name](*[real(x) for x in args], **{k: real(x) for k, x in kw.items()})
+            count[e] += 1
+            ins.then_inc(T.sem["e" + e], 1)
+            total["e" + e] = count[e]
+            done[i] = (("e" + e, count[e]), ("e" + e, count[e]))
+    for s, v in total.items():
+        if seen["G"].get(s, 0) < v:
+            g.wait_ge(T.sem[s], v)

@@ -11,21 +11,21 @@ MAGIC = 12582912.0
 NG1, NBB, NRB, NDB, NCC = 8, 3, 5, 5, 8
 f32, bf, f16, i32, u16 = "float32", "bfloat16", "float16", "int32", "uint16"
 SB = {
-    "ki": ([B0], i32), "kk": ([L + W], f32), "xx": ([W], bf), "dtab": ([DUM], f32), "tt": ([DUM + 48], i32),
+    "ki": ([B0], i32), "kk": ([L + W], f32), "xx": ([W], bf), "dtab": ([DUM], f32), "tt": ([DUM + 48], f32),
     "rk0": ([2048], i32), "rk1": ([2048], f32), "rk2": ([2048], f32),
     "rx0": ([B0], bf), "rx1": ([B0 + L], bf), "rx2": ([B0 + 2 * L], bf),
-    "cb": ([2560], f32), "nb": ([1536], f32), "pkv": ([L], i32),
+    "cb": ([2560], f32), "nb": ([1536], f32), "pkv": ([L], f32),
     "kvr": ([R, L], u16), "of1": ([R * L], u16), "cu": ([R * L], u16), "cc": ([NCC, 64], f16), "kp": ([L], bf),
     "g1": ([NG1, L], f16), "gh": ([2, 2, L], f16), "gt": ([2, L], bf),
     "bb": ([NBB, L, 2], bf), "rb": ([NRB, L, 2], bf), "db": ([NDB, L, 2], bf),
     "xv": ([R, L], bf), "dv": ([2, L], f32), "xq": ([L], bf), "kv16": ([L], f16), "kve": ([L], f16),
     "sc1": ([L], f32), "sc2": ([L], f32), "uu": ([L], bf), "sd1": ([272], f32), "li": ([2, L], bf),
     "km": ([L], f32), "km16": ([L], f16), "xm16": ([L], f16), "cn": ([L], f16),
-    "ga": ([2048], bf), "ra": ([8, 256], bf), "xa": ([128], bf), "ai": ([2, 128], i32), "du": ([128], u16),
+    "ga": ([2048], bf), "ra": ([8, 256], bf), "xa": ([128], bf), "ai": ([128], f32), "xs": ([128], bf), "du": ([128], u16),
     "sm": ([16, 32], f32), "si": ([6, 32], i32), "su": ([12, 32], u16), "m16": ([32], f16), "d1": ([32], bf),
     "pc": ([4], i32), "col": ([48], f32), "ix": ([144], f32), "lane": ([L], f32),
     "we": ([10, 144], bf), "weh": ([144], f16), "ws": ([16, 144], f16), "rr": ([16, 128], f16), "ll": ([16, 128], f16),
-    "mb": ([5, 128], bf), "mh": ([10, 128], f16), "blk": ([128], f32), "mask": ([32], f32),
+    "mb": ([6, 128], bf), "mh": ([10, 128], f16), "blk": ([128], f32), "mask": ([32], f32),
     "kc": ([2, L], bf), "rs0": ([L], bf), "rstk": ([L], bf), "dm0": ([L], bf), "rs1": ([272], bf), "scm": ([L], bf),
     "ia": ([5, 32], f32), "itc": ([32], f16), "kq": ([128], f16),
     "thi": ([4], i32), "thf": ([4], f32), "wi": ([4], i32), "l8": ([128], f32),
@@ -39,10 +39,10 @@ SHAPES = {n: v[1] for n, v in SCRATCH.items()}
 SHAPES.update({"kin": [128, B0], "xf": [128, B0], "th": [8, R], "w": [128, R], "yk": [128, W], "yx": [128, R * L]})
 WIDE = {n: (2 if v[2] in (bf, f16, u16) else 4) for n, v in SCRATCH.items()}
 
-MODES = ["VAVAAVAA", "AAAVAAAA", "AAVAVAAAA"]
-CY, PCY, GAM, SIG = 1.04, 0.52, 1.56, 3.8
-LAT_X, LAT_S = 120.0, 60.0
-SEED, PEN, TRIES = 0, 12.0, 4000
+MODES = ["VAVAVAVA", "VAAAAVAA", "AVAAAAVAA"]
+CY, PCY, GAM, SIG = 0.9, 0.46, 1.56, 3.8
+LAT_X, LAT_S = 250.0, 170.0
+SEED, PEN, TRIES = 0, 12.0, 7000
 S_ = slice
 ALL = slice(None)
 
@@ -98,9 +98,11 @@ STA = [[(j, BOTH) for j in range(2, 8)], [(j, BOTH) for j in (0, 1, 4, 5, 6, 7)]
 def build():
     ops = []
 
-    def add(alts, reads, writes, lat=0.0, kind="c", extra=None):
+    mark = {}
+
+    def add(alts, reads, writes, lat=0.0, kind="c", extra=None, after=None):
         ops.append({"alts": alts, "r": [region(x) for x in flat(reads)], "w": [region(x) for x in flat(writes)],
-                    "lat": lat, "kind": kind, "extra": extra})
+                    "lat": lat, "kind": kind, "extra": extra, "after": [mark[after]] if after else []})
 
     def split(out):
         return ([out[2]], [out[1]]) if out[0] == "*" else ([], [out])
@@ -178,14 +180,14 @@ def build():
         kw = {} if SCRATCH[out[0]][2] == i32 else {"allow_small_or_imprecise_dtypes": True}
         add([("G", 130 + 2 * CY * region(out)[3], ("iota", [out, pat, base, cm], kw))], [], [out], extra=extra)
 
-    def dma(pairs, q="Y"):
+    def dma(pairs, q="Y", after=None):
         by = sum(region(o)[3] * region(o)[4] * WIDE.get(o[0], 2 if o[0] == "yx" else 4) for o, i in pairs)
         add([(q, 60.0 * len(pairs), ("dma", pairs, {}))], [i for o, i in pairs], [o for o, i in pairs],
-            lat=1900 + by / 250.0 + 150 * len(pairs), kind="d")
+            lat=1900 + by / 250.0 + 150 * len(pairs), kind="d", after=after)
 
-    def push(dst, src, t):
+    def push(dst, src, t, after=None):
         by = region(dst)[3] * 128 * WIDE[dst[0]]
-        add([("G", 300.0, ("push", [dst, src, t], {}))], [src], [dst], lat=2000 + by / 200.0, kind="p")
+        add([("G", 300.0, ("push", [dst, src, t], {}))], [src], [dst], lat=2000 + by / 200.0, kind="p", after=after)
 
     def P(b, *ix):
         return ap("p%d" % b, *(ix if ix else (ALL,)))
@@ -226,8 +228,8 @@ def build():
     ts(c1(M06), c1(PM), 6.5, A.is_lt, 131072.0, A.mult)
     ts(c1(WYC), mk(1), -1024.0, A.mult, mk(0), A.add)
     ts(c1(31), mk(1), 1024.0, A.mult)
-    ts(c1(DE), c1(PM), float(DUM), A.add)
-    ts(c1(DO), c1(PM), float(DUM + 16), A.add)
+    ts(c1(DE), c1(PM), DUM - CEN, A.add)
+    ts(c1(DO), c1(PM), DUM + 16 - CEN, A.add)
     ts(c1(GE9), c1(PM), 8.5, A.is_gt)
     ts(c1(32), c1(PM), 16.0, A.mult)
     copy(c1(33), ap("pc", S_(0, 1)))
@@ -250,10 +252,10 @@ def build():
         lin(ap("rr", k, ALL), ap("blk", ALL), scale=mk(k))
     add([("G", 170 + 2 * CY * 2048, ("affine_select", [ap("ll", ALL), ap("rr", ALL), [[0, 16], [-1, 128]], A.not_equal, -1.0 / 64, 0, 1], {}))],
         [ap("rr", ALL)], [ap("ll", ALL)])
-    IB, NIB, HIB, ZB, ONB = [ap("mb", i, ALL) for i in range(5)]
+    IB, NIB, HIB, ZB, ONB, NKB = [ap("mb", i, ALL) for i in range(6)]
     IH, HIH, NI64, DN67, P1, P2, D9 = [ap("mh", i, ALL) for i in range(7)]
     ix128 = ap("ix", S_(0, 128))
-    for m, c in [(IB, 1.0), (NIB, -1.0), (HIB, -0.5), (IH, 1.0), (HIH, 0.5), (NI64, -1.0 / 64), (DN67, c1(N67)), (D9, c1(GE9)),
+    for m, c in [(IB, 1.0), (NIB, -1.0), (NKB, -1024.0), (HIB, -0.5), (IH, 1.0), (HIH, 0.5), (NI64, -1.0 / 64), (DN67, c1(N67)), (D9, c1(GE9)),
                  (ap("mh", 7, ALL), c1(NASK)), (ap("mh", 8, ALL), c1(NASK + 1)), (ap("mh", 9, ALL), c1(NASK + 2))]:
         ts(m, ix128, c1(33), A.is_equal, c, A.mult)
     memset(ZB, 0.0)
@@ -282,7 +284,7 @@ def build():
     iota(ap("ia", 1, ALL), [[0, 16], [16, 2]], 0, 0)
     ts(ap("itc", ALL), ap("ia", 0, ALL), c1(PM), A.add, -1535.0, A.add)
     ts(ap("ia", 1, ALL), ap("ia", 1, ALL), c1(DE), A.add)
-    ts(ap("ia", 2, ALL), ap("ia", 0, ALL), c1(PM), A.add, -float(L), A.add)
+    ts(ap("ia", 2, ALL), ap("ia", 0, ALL), c1(PM), A.add, -L - CEN, A.add)
     iota(ap("blk", ALL), [[256, 8], [1, 16]], 0, 0)
     ts(ap("kq", ALL), ap("blk", ALL), c1(32), A.add)
     iota(ap("nb", S_(512, 1536)), [[0, 1024]], 0, 0)
@@ -291,7 +293,7 @@ def build():
     ts(pap("l8", p8, ALL), pap("l8", p8, ALL), 0.0, A.is_equal)
     copy(pap("thf", p8, S_(0, R)), pap("thi", p8, S_(0, R)))
     mm([(P(7, S_(0, R)), pap("l8", p8, ALL), pap("thf", p8, S_(0, R)))])
-    ts(ap("col", S_(TH, TH + R)), P(7, S_(0, R)), 16.0, A.mult, -1.0, A.add)
+    ts(ap("col", S_(TH, TH + R)), P(7, S_(0, R)), 16.0, A.mult, -0.5, A.add)
 
     def lists(t):
         copy(ap("kvr", t, S_(0, L, 2)), ap("ki", S_(t, 1024, 4)))
@@ -316,11 +318,20 @@ def build():
     lin(kk(0, 1152), ap("ki", S_(0, 1152)))
     lin(kk(1152, B0), ap("ki", S_(1152, B0)))
     rows06(0, B0)
-    push(ap("rk0", ALL), ap("ki", S_(0, 2048)), 0)
     for t in range(R):
-        push(ap("rx%d" % t, S_(0, B0)), ap("xx", S_(0, B0)), t)
         lin(ap("xv", t, ALL), ap("xx", vcols(t)), eng="G" if t else "VA")
-    dma([(pap("yk", S_(j, 128, 16), S_(0, B0)), kk(0, B0, 1, S_(j, 128, 16))) for j in range(16) if j not in (6, 7, 9, 10, 11)])
+
+    def bulk(t):
+        if t == 0:
+            push(ap("rk0", ALL), ap("ki", S_(0, 2048)), 0, ("names", 0))
+            push(ap("rx0", ALL), ap("xx", S_(0, B0)), 0, ("names", 0))
+        if t == 1:
+            push(ap("rx1", S_(0, B0)), ap("xx", S_(0, B0)), 1, ("names", 1))
+        if t == 2:
+            push(ap("rx2", S_(0, B0)), ap("xx", S_(0, B0)), 2, ("names", 2))
+            dma([(pap("yk", S_(j, 128, 16), S_(0, B0)), kk(0, B0, 1, S_(j, 128, 16))) for j in range(16) if j not in (6, 7, 9, 10, 11)],
+                after=("names", 2))
+
     for t in range(R):
         mm([(P(6, S_(0, 32)), wsl("we", EW + t, r), ap("xv", t, S_(r, L, 16))) for r in range(16)])
         copy(ap("si", 2, ALL), P(6, S_(0, 32)))
@@ -350,6 +361,7 @@ def build():
             lin(ap("g1", g, ALL), ind(ap("ki", S_(0, B0)), o1(t, j, e)), bias=-CEN)
             prs.append((ap("cc", s, S_(32 * e, 32 * e + 32)), pap("g1", S_((kof(t, j, e) + t) % 16, 128, 16), g, ALL)))
         dma(prs)
+        mark[("names", t)] = len(ops) - 1
         ts(cu(t, j, None if len(es) == 2 else es[0]), ap("cc", s, es_(es)), CEN, A.add)
         numbers(t, j, es, s)
 
@@ -423,7 +435,7 @@ def build():
         lin(ap("cb", S_(1024, 1536)), src, eng="G")
         dma([(ap("cb", S_(1536, 2048)), ap("cb", S_(1024, 1536)))])
         lin(ap("cn", ALL), ap("lane", ALL), scale=c1(SCN), bias=c1(BCN + t))
-        lin(ap("xq", ALL), ap("xv", t, ALL), scale=4096.0)
+        lin(ap("xq", ALL), ap("xv", t, ALL), scale=1.0 / 1024)
         mm([(P(7), ap("mh", 7 + t, ALL), ap("kv16", ALL)), (P(7), wsl("ws", 7, 9 + t), ap("cn", ALL))])
         lin(ap("cb", S_(2048, 2560)), P(7), bias=CEN)
         tt(ap("pkv", ALL), ind(ap("rk%d" % t, ALL), su(t)), ap("xq", ALL), A.add)
@@ -445,15 +457,14 @@ def build():
         scan(ap("sc2", ALL), ap("uu", ALL), P(cb_), A.mult, A.max)
         ts(sm(0), ap("sc1", ends), -131071.0, A.add, 8192.0, A.mult)
         ts(sm(1), ap("sc1", ends), thr, A.subtract, 8192.0, A.mult)
-        ts(ap("si", 0, ALL), ap("sc2", ends), CEN, A.add)
+        ts(sm(3), ap("sc2", ends), MAGIC * 4096, A.add, -MAGIC * 4096, A.add)
         M = ap("si", 1, ALL)
-        ts(M, ap("si", 0, ALL), 4095, A.bitwise_and)
+        tt(M, ap("sc2", ends), sm(3), A.subtract)
         tt(sm(2), M, sm(0), A.max)
-        tt(sm(3), sm(2), ap("ia", 1, ALL), A.min)
-        ts(ap("m16", ALL), sm(3), -CEN, A.add)
-        copy(su(MU), M)
+        tt(ap("m16", ALL), sm(2), ap("ia", 1, ALL), A.min)
+        ts(su(MU), M, CEN, A.add)
         tt(sm(4), M, sm(1), A.max)
-        ts(su(GO), sm(4), float(DUM + 32), A.min)
+        ts(su(GO), sm(4), DUM + 32 - CEN, A.min, CEN, A.add)
         m16 = ap("m16", ALL)
         mm([(P(6), IB, ap("dm0", ALL))], ("d0", t))
         mm([(P(6, S_(r + 1, L, 16)), ap("ll", r, ALL), m16) for r in range(15)], ("d0", t))
@@ -476,10 +487,10 @@ def build():
         ts(ap("nb", S_(0, 512)), P(kb), MAGIC, A.add, -MAGIC, A.add)
         ts(sm(5), ap("sc2", ends), 0.0, A.is_equal, 8192.0, A.mult)
         ts(sm(6, S_(0, 16)), ap("sd1", S_(16, 272, 17)), 0.0, A.is_equal, 8192.0, A.mult)
-        tt(sm(7), sm(3), sm(5), A.max)
-        tt(sm(6, S_(16, 32)), sm(7, S_(1, 32, 2)), sm(6, S_(0, 16)), A.max)
-        ts(su(SO, S_(1, 32, 2)), sm(6, S_(16, 32)), c1(DO), A.min)
-        ts(su(SO, S_(0, 32, 2)), sm(7, S_(0, 32, 2)), c1(DE), A.min)
+        tt(sm(7), m16, sm(5), A.add)
+        tt(sm(6, S_(16, 32)), sm(7, S_(1, 32, 2)), sm(6, S_(0, 16)), A.add)
+        ts(su(SO, S_(1, 32, 2)), sm(6, S_(16, 32)), c1(DO), A.min, CEN, A.add)
+        ts(su(SO, S_(0, 32, 2)), sm(7, S_(0, 32, 2)), c1(DE), A.min, CEN, A.add)
         tw = ap("tt", ALL)
         for a in range(15, -1, -1):
             copy(ind(tw, su(SO, S_(2 * a, 2 * a + 2))), ap("lane", S_(32 * a, 32 * a + 32)))
@@ -499,7 +510,7 @@ def build():
         ts(su(OVC), sm(12), 1535.0, A.add)
         tt(sm(13), M, ap("d1", ALL), A.subtract)
         tt(sm(14), sm(13), ap("ia", 2, ALL), A.max)
-        ts(su(MSD), sm(14), float(L), A.add)
+        ts(su(MSD), sm(14), L + CEN, A.add)
         copy(ind(ap("tt", S_(0, 1536)), su(RO)), ap("pkv", ALL))
         lin(kk(t, 2048, 4), ind(ap("cb", S_(512, 2560)), su(OVC)))
         lin(kk(n0, n0 + L), ind(ap("cb", S_(0, 1536)), su(ONEW)))
@@ -511,23 +522,24 @@ def build():
             ts(ap("pc", S_(3, 4)), ap("pc", S_(3, 4)), 15, A.bitwise_and)
             ts(c1(THR + t + 1), ap("pc", S_(3, 4)), 16.0, A.mult, c1(TH + t + 1), A.add)
             rows06(n0, n0 + L)
-            push(ap("rk%d" % (t + 1), ALL), kk(0, 2048), t + 1)
+            mark[("rows", t)] = len(ops) - 1
+            push(ap("rk%d" % (t + 1), ALL), kk(0, 2048), t + 1, ("rows", t))
         st = [(pap("yk", S_(9 + t, 128, 16), S_(0, B0)), kk(0, B0, 1, S_(9 + t, 128, 16)))]
         if t + 1 == R:
             dma(st + [(pap("yk", S_(j, 128, 16), S_(0, n0)), kk(0, n0, 1, S_(j, 128, 16))) for j in (6, 7)])
             st = []
-        dma(st + [(ap("yk", S_(n0, n0 + L)), kk(n0, n0 + L))])
+        dma(st + [(ap("yk", S_(n0, n0 + L)), kk(n0, n0 + L))], after=("rows", t) if t + 1 < R else None)
         slot = ap("tt", S_(512, 640))
-        ts(ap("ai", 0, ALL), slot, 4095, A.bitwise_and)
-        copy(ap("du", ALL), ap("ai", 0, ALL))
-        ts(ap("ai", 1, ALL), slot, 12, A.arith_shift_right)
-        copy(ap("xa", ALL), ap("ai", 1, ALL))
+        copy(ap("du", ALL), slot)
+        ts(ap("ai", ALL), slot, MAGIC, A.add, -MAGIC, A.add)
+        tt(ap("xs", ALL), slot, ap("ai", ALL), A.subtract)
+        lin(ap("xa", ALL), ap("xs", ALL), scale=1024.0)
         banks = [cb_, kb, 6, 7]
         for b in range(4):
             gb = ap("ga", S_(L * b, L * b + L))
             lin(gb, ind(ap("rx%d" % t, ALL), ap("du", S_(32 * b, 32 * b + 32))))
             mm([(P(banks[b]), ZB, ap("rs0", ALL))], ("a", t, b))
-            mm([(P(banks[b], S_(k, L, 16)), NIB, ap("xa", S_(32 * b, 32 * b + 32))) for k in range(16)], ("a", t, b))
+            mm([(P(banks[b], S_(k, L, 16)), NKB, ap("xs", S_(32 * b, 32 * b + 32))) for k in range(16)], ("a", t, b))
             mm([(P(banks[b]), IB, gb)], ("a", t, b))
             act(ap("ra", S_(2 * b, 2 * b + 2), ALL), P(banks[b]), F.Abs)
         o = P(cb_, S_(0, 128))
@@ -554,6 +566,7 @@ def build():
                 names_static(t, *js[i])
             if i >= 2:
                 score(t, js[i - 2][0], js[i - 2][1], False)
+        bulk(t)
 
     opens(0)
     lin(ap("kv16", ALL), ap("ki", vcols(0)), bias=-CEN)
@@ -585,7 +598,7 @@ def build():
 def depend(ops):
     hist = {}
     for i, o in enumerate(ops):
-        deps = {}
+        deps = {j: False for j in o["after"]}
         fixed = o["alts"][0][0] if len(o["alts"]) == 1 else None
         for regs, wr in ((o["r"], False), (o["w"], True)):
             for n, pm, cm, _1, _2 in regs:

@@ -6,43 +6,50 @@ F = ActivationFunctionType
 B0, L, R, NR = 2304, 512, 3, 8
 W = B0 + R * L
 DUM = B0 + 2 * L
+OFF = L
 CEN = 1920.0
 MAGIC = 12582912.0
-NG1, NBB, NRB, NDB, NCC = 8, 3, 5, 5, 8
+BAR = 131072.0
+NG1, NGD, NBB, NRB, NDB, NCC, LATE = 4, 6, 3, 5, 3, 4, 2
 f32, bf, f16, i32, u16 = "float32", "bfloat16", "float16", "int32", "uint16"
 SB = {
-    "ki": ([B0], i32), "kk": ([L + W], f32), "xx": ([W], bf), "dtab": ([DUM], f32), "tt": ([DUM + 48], f32),
-    "rk0": ([2048], i32), "rk1": ([2048], f32), "rk2": ([2048], f32),
+    "ki": ([B0], i32), "kk": ([OFF + W + 32], f32), "xx": ([W], bf), "dtab": ([B0], i32), "st": ([1024], f32),
+    "rk": ([R, L], f32), "qa": ([R, 32], u16), "of2": ([16, 64], u16), "kw2": ([16, 2, 32], u16),
     "rx0": ([B0], bf), "rx1": ([B0 + L], bf), "rx2": ([B0 + 2 * L], bf),
-    "cb": ([2560], f32), "nb": ([1536], f32), "pkv": ([L], f32),
-    "kvr": ([R, L], u16), "of1": ([R * L], u16), "cu": ([R * L], u16), "cc": ([NCC, 64], f16), "kp": ([L], bf),
-    "g1": ([NG1, L], f16), "gh": ([2, 2, L], f16), "gt": ([2, L], bf),
-    "bb": ([NBB, L, 2], bf), "rb": ([NRB, L, 2], bf), "db": ([NDB, L, 2], bf),
-    "xv": ([R, L], bf), "dv": ([2, L], f32), "xq": ([L], bf), "kv16": ([L], f16), "kve": ([L], f16),
-    "sc1": ([L], f32), "sc2": ([L], f32), "uu": ([L], bf), "sd1": ([272], f32), "li": ([2, L], bf),
-    "km": ([L], f32), "km16": ([L], f16), "xm16": ([L], f16), "cn": ([L], f16),
-    "ga": ([2048], bf), "ra": ([8, 256], bf), "xa": ([128], bf), "ai": ([128], f32), "xs": ([128], bf), "du": ([128], u16),
-    "sm": ([16, 32], f32), "si": ([6, 32], i32), "su": ([12, 32], u16), "m16": ([32], f16), "d1": ([32], bf),
-    "pc": ([4], i32), "col": ([48], f32), "ix": ([144], f32), "lane": ([L], f32),
-    "we": ([10, 144], bf), "weh": ([144], f16), "ws": ([16, 144], f16), "rr": ([16, 128], f16), "ll": ([16, 128], f16),
-    "mb": ([6, 128], bf), "mh": ([10, 128], f16), "blk": ([128], f32), "mask": ([32], f32),
-    "kc": ([2, L], bf), "rs0": ([L], bf), "rstk": ([L], bf), "dm0": ([L], bf), "rs1": ([272], bf), "scm": ([L], bf),
-    "ia": ([5, 32], f32), "itc": ([32], f16), "kq": ([128], f16),
+    "cb": ([2048], f32), "nb": ([R, 1152], bf), "pkv": ([L], f32), "nv": ([R, L], f32), "vv": ([L], f32),
+    "kvr": ([L], u16), "of1": ([R * L], u16), "cu": ([R * L], u16), "cc": ([NCC + 3, 128], f16), "kp": ([L], bf),
+    "g1": ([NG1 + 1, 2 * L], f16), "gh": ([3, 2, L], f16), "gt": ([2, L], bf), "gd": ([NGD + LATE + 1, L, 2], f16),
+    "bb": ([NBB, L, 2], bf), "rb": ([NRB + LATE, L, 2], bf), "db": ([NDB + LATE, L, 2], bf),
+    "dv": ([2, L], f32), "xq": ([L], f32), "kv16": ([L], f16),
+    "sc1": ([L], f32), "sc2": ([L], f32), "uu": ([L], bf), "sd1": ([272], f32), "li": ([2, L], f16),
+    "km": ([L], f32), "val": ([L], f32), "xm16": ([L], f16),
+    "ga": ([2048], bf), "ra": ([8, 16, 16], bf), "ai": ([128], f32), "xs": ([128], bf), "du": ([128], u16),
+    "sm": ([16, 32], f32), "si": ([2, 8], i32), "sa": ([2, 96], i32), "su": ([12, 32], u16), "m16": ([32], f16),
+    "pc": ([6], i32), "col": ([48], f32), "ix": ([144], f32), "sxc": ([144], i32), "mi": ([2, 160], i32), "mf": ([160], bf), "sxv": ([R, 32], f16),
+    "we": ([7, 144], bf), "weh": ([2, 144], f16), "ws": ([16, 144], f16), "rr": ([16, 128], f16), "ll": ([16, 128], f16),
+    "mb": ([5, 128], bf), "mh": ([9, 128], f16), "p2f": ([128], f32), "blk": ([128], f32), "bl16": ([128], f16), "mask": ([32], f32),
+    "kc": ([2, L], bf), "rs0": ([L], bf), "rstk": ([L], bf), "dm0": ([L], bf), "rs1": ([272], bf),
+    "ia": ([2, 32], f32), "itc": ([2, 32], f16), "kq": ([128], f16),
     "thi": ([4], i32), "thf": ([4], f32), "wi": ([4], i32), "l8": ([128], f32),
 }
 SCRATCH = {n: ("sbuf", [128] + s, d) for n, (s, d) in SB.items()}
 for _b in range(8):
     SCRATCH["p%d" % _b] = ("psum", [128, 512], f32)
-NDS = 80
+NDS = 140
 SEMAPHORES = ["eV", "eA", "eP", "eG"] + ["q%d" % i for i in range(NDS)]
 SHAPES = {n: v[1] for n, v in SCRATCH.items()}
 SHAPES.update({"kin": [128, B0], "xf": [128, B0], "th": [8, R], "w": [128, R], "yk": [128, W], "yx": [128, R * L]})
 WIDE = {n: (2 if v[2] in (bf, f16, u16) else 4) for n, v in SCRATCH.items()}
 
-MODES = ["VAVAVAVA", "VAAAAVAA", "AVAAAAVAA"]
-CY, PCY, GAM, SIG = 0.9, 0.46, 1.56, 3.8
-LAT_X, LAT_S = 250.0, 170.0
-SEED, PEN, TRIES = 0, 12.0, 7000
+MODELS = [(0.9, 1.56, 3.8, 1000.0, 500.0, 300.0, 3.0, 250.0, 170.0),
+          (1.15, 2.0, 3.0, 1000.0, 500.0, 300.0, 3.0, 250.0, 170.0),
+          (1.1, 1.15, 5.5, 1000.0, 500.0, 300.0, 3.0, 250.0, 170.0),
+          (0.9, 1.8, 3.8, 1500.0, 700.0, 200.0, 5.0, 350.0, 250.0)]
+DPRE, DPOST = MODELS[0][3:5]
+LAT_X, LAT_S = MODELS[0][7:9]
+SEED, TRIES, SHY, TOL, DEL = 0, 7000, 4000.0, 200.0, 600.0
+KK2 = "G"
+LEAD = [0.0, 0.0, 0.0]
 S_ = slice
 ALL = slice(None)
 
@@ -57,6 +64,10 @@ def pap(n, ps, *ix):
 
 def ind(win, off):
     return ("*", win, off)
+
+
+def row(j):
+    return S_(j, 128, 16)
 
 
 _cache = {}
@@ -91,14 +102,20 @@ def kof(t, j, e):
 
 
 BOTH = (0, 1)
-DYN = [[(0, BOTH), (1, BOTH)], [(2, BOTH), (3, BOTH)], [(2, BOTH), (4, (0,)), (3, BOTH)]]
-STA = [[(j, BOTH) for j in range(2, 8)], [(j, BOTH) for j in (0, 1, 4, 5, 6, 7)], [(j, BOTH) for j in (0, 1, 5, 6, 7)] + [(4, (1,))]]
+QUADS = [[(2, 3), (4, 5), (6, 7)], [(0, 1), (4, 5), (6, 7)], [(0, 1), (6, 7), (5,)]]
+DYN = [[(j, BOTH, "") for j in range(2)], [(2, BOTH, "WW"), (3, BOTH, "WW")], [(2, BOTH, "WW"), (3, BOTH, "WW"), (4, (0,), "WM")]]
+LONE = [[], [], [(4, (1,), "")]]
+PIECES = ["11111111", "44114411", "44111411"]
+PIECES = [[int(c) for c in x] for x in PIECES]
 
 
-def build():
+def build(model=None):
+    CY, GAM, SIG, DPRE, DPOST, DBW, DROW = (model or MODELS[0])[:7]
+    PCY = CY * 0.51
     ops = []
 
     mark = {}
+    lead = [0.0]
 
     def add(alts, reads, writes, lat=0.0, kind="c", extra=None, after=None):
         ops.append({"alts": alts, "r": [region(x) for x in flat(reads)], "w": [region(x) for x in flat(writes)],
@@ -174,20 +191,22 @@ def build():
 
     def mm(lst, group=None):
         cost = sum(max(64, region(x[2])[3]) * (WIDE[x[2][0]] ** 2 / 4) * PCY for x in lst)
-        add([("P", cost, ("mm", lst, {"group": group}))], [x[1] for x in lst] + [x[2] for x in lst], [x[0] for x in lst], lat=60.0)
+        add([("P", cost, ("mm", lst, {"group": group}))], [x[1] for x in lst] + [x[2] for x in lst], [x[0] for x in lst], lat=60.0,
+            extra=lead[0] if group and group[0] == "k" else None)
 
     def iota(out, pat, base, cm, extra=None):
         kw = {} if SCRATCH[out[0]][2] == i32 else {"allow_small_or_imprecise_dtypes": True}
         add([("G", 130 + 2 * CY * region(out)[3], ("iota", [out, pat, base, cm], kw))], [], [out], extra=extra)
 
-    def dma(pairs, q="Y", after=None):
+    def dma(pairs, q="Y", after=None, extra=None):
         by = sum(region(o)[3] * region(o)[4] * WIDE.get(o[0], 2 if o[0] == "yx" else 4) for o, i in pairs)
+        rows = sum(max(16, region(o)[4], region(i)[4]) for o, i in pairs)
         add([(q, 60.0 * len(pairs), ("dma", pairs, {}))], [i for o, i in pairs], [o for o, i in pairs],
-            lat=1900 + by / 250.0 + 150 * len(pairs), kind="d", after=after)
+            lat=DPRE + DPOST + by / DBW + rows * DROW, kind="d", after=after, extra=extra)
 
     def push(dst, src, t, after=None):
         by = region(dst)[3] * 128 * WIDE[dst[0]]
-        add([("G", 300.0, ("push", [dst, src, t], {}))], [src], [dst], lat=2000 + by / 200.0, kind="p", after=after)
+        add([("G", 300.0, ("push", [dst, src, t], {}))], [src], [dst], lat=DPRE + DPOST + by / DBW + 128 * DROW, kind="p", after=after)
 
     def P(b, *ix):
         return ap("p%d" % b, *(ix if ix else (ALL,)))
@@ -205,212 +224,317 @@ def build():
         return S_(t, 2048, 4)
 
     def kk(a, b, step=1, ps=ALL):
-        return pap("kk", ps, S_(L + a, L + b, step))
+        return pap("kk", ps, S_(OFF + a, OFF + b, step))
 
-    dma([(ap("ki", S_(0, 1152)), ap("kin", S_(0, 1152))), (ap("ki", S_(1152, B0)), ap("kin", S_(1152, B0)))])
-    dma([(ap("xx", S_(0, B0)), ap("xf", ALL))])
-    dma([(pap("thi", S_(0, 8), S_(0, R)), ap("th", ALL)), (ap("wi", S_(0, R)), ap("w", ALL))])
+    def xv(t):
+        return ap("nb", t, S_(0, L))
 
-    PM, PG, C15, M67, N67, SCN, SVN, M06, WYC, DE, DO, GE9 = range(12)
-    BCN, BVN, NASK, WF, TH, THR = 12, 15, 18, 21, 24, 27
-    TOT = 30
-    iota(ap("pc", S_(0, 1)), [[0, 1]], 0, 1, 1e6)
+    def pc(i):
+        return ap("pc", S_(i, i + 1))
+
+    dma([(ap("ki", S_(0, 1152)), ap("kin", S_(0, 1152))), (ap("ki", S_(1152, B0)), ap("kin", S_(1152, B0)))], extra=4e6)
+    dma([(ap("xx", S_(0, B0)), ap("xf", ALL))], extra=3e6)
+    dma([(pap("thi", S_(0, 8), S_(0, R)), ap("th", ALL)), (ap("wi", S_(0, R)), ap("w", ALL))], extra=8e6)
+
+
+    PM, PG, Q8, PP, C15, N67, DE, DO, H0, H1, H1B, BAR0, BAR1, CCOL, GB, GS, SXW, CHB, P16, TMP = range(20)
+    WF, TH, THR, GS2 = 24, 27, 30, 33
+    iota(pc(0), [[0, 1]], 0, 1, 1e6)
     iota(ap("ix", ALL), [[1, 144]], 0, 0, 1e6)
-    ts(ap("pc", S_(1, 2)), ap("pc", S_(0, 1)), 15, A.bitwise_and)
-    ts(ap("pc", S_(2, 3)), ap("pc", S_(0, 1)), 4, A.arith_shift_right)
-    copy(ap("col", S_(0, 2)), ap("pc", S_(1, 3)))
+    ts(pc(1), pc(0), 15, A.bitwise_and)
+    ts(pc(2), pc(0), 4, A.arith_shift_right)
+    ts(pc(3), pc(0), 7, A.bitwise_and)
+    copy(ap("col", S_(0, 3)), ap("pc", S_(1, 4)))
+    copy(c1(PP), pc(0))
     ts(c1(C15), c1(PG), 16.0, A.mult, 15.0, A.add)
     ts(ap("mask", S_(0, 16)), ap("ix", S_(0, 16)), c1(PM), A.is_equal)
     ts(ap("mask", S_(16, 32)), ap("mask", S_(0, 16)), -CEN, A.mult)
-    ts(c1(M67), mk(6), 1.0, A.mult, mk(7), A.add)
-    ts(c1(N67), c1(M67), -1.0, A.mult, 1.0, A.add)
-    ts(c1(SCN), mk(0), 4.0, A.mult, c1(M67), A.add)
-    ts(c1(M06), c1(PM), 6.5, A.is_lt, 131072.0, A.mult)
-    ts(c1(WYC), mk(1), -1024.0, A.mult, mk(0), A.add)
-    ts(c1(31), mk(1), 1024.0, A.mult)
-    ts(c1(DE), c1(PM), DUM - CEN, A.add)
-    ts(c1(DO), c1(PM), DUM + 16 - CEN, A.add)
-    ts(c1(GE9), c1(PM), 8.5, A.is_gt)
-    ts(c1(32), c1(PM), 16.0, A.mult)
-    copy(c1(33), ap("pc", S_(0, 1)))
-    for t in range(R):
-        n0 = B0 + L * t
-        ts(c1(34 + t), mk(0), t - CEN, A.mult)
-        ts(c1(BCN + t), c1(M67), n0 - CEN, A.mult, c1(34 + t), A.add)
-        ts(c1(NASK + t), mk(9 + t), -1.0, A.mult, 1.0, A.add)
+    ts(c1(TMP), mk(6), -1.0, A.mult, mk(7), A.subtract)
+    ts(c1(N67), c1(TMP), 1.0, A.add)
+    ts(c1(DE), c1(PM), W - CEN, A.add)
+    ts(c1(DO), c1(PM), W + 16 - CEN, A.add)
+    ts(c1(H0), c1(PM), 7.5, A.is_lt)
+    ts(c1(H1B), c1(PM), 7.5, A.is_gt, BAR, A.mult)
+    ts(c1(BAR0), c1(PM), 6.5, A.is_lt, BAR, A.mult)
+    ts(c1(BAR1), c1(Q8), 6.5, A.is_lt, c1(H1B), A.mult)
+    ts(c1(CCOL), c1(Q8), 5.5, A.is_lt, 0.5, A.mult)
+    ts(c1(TMP + 1), c1(Q8), 6.0, A.not_equal, -2040.0, A.mult)
+    ts(c1(GB), mk(15), 6120.0, A.mult, c1(TMP + 1), A.add)
+    ts(c1(GS), c1(PM), 14.5, A.is_lt)
+    ts(c1(GS2), c1(PM), 14.5, A.is_lt, mk(6), A.subtract)
+    ts(c1(SXW), c1(Q8), 6.5, A.is_gt, 16.0, A.mult)
+    ts(c1(TMP + 2), c1(PM), 3.5, A.is_lt, mk(0), A.subtract)
+    ts(c1(CHB), c1(TMP + 2), mk(8), A.add, CEN, A.mult)
+    ts(c1(P16), c1(PM), 16.0, A.mult)
     copy(ap("col", S_(WF, WF + R)), ap("wi", S_(0, R)))
-    E32, EM16, E16, EBAR, E2048, EY, EZ, EW = range(8)
-    for i, c in [(E32, 32.0), (EM16, -16.0), (E16, 16.0), (EBAR, c1(M06)), (E2048, 2048.0), (EY, c1(WYC)), (EZ, c1(31)),
+    E16, EM32, EBAR0, EBAR1, EW = range(5)
+    for i, c in [(E16, 16.0), (EM32, -32.0), (EBAR0, c1(BAR0)), (EBAR1, c1(BAR1)),
                  (EW, c1(WF)), (EW + 1, c1(WF + 1)), (EW + 2, c1(WF + 2))]:
         ts(ap("we", i, ALL), ap("ix", ALL), c1(C15), A.is_equal, c, A.mult)
-    ts(ap("weh", ALL), ap("ix", ALL), c1(C15), A.is_equal)
+    ts(ap("weh", 0, ALL), ap("ix", ALL), c1(C15), A.is_equal)
+    lin(ap("weh", 1, ALL), ap("weh", 0, ALL), scale=c1(SXW))
     for k in range(16):
-        lin(ap("ws", k, ALL), ap("weh", ALL), scale=mk(k))
+        lin(ap("ws", k, ALL), ap("weh", 0, ALL), scale=mk(k))
     iota(ap("blk", ALL), [[1, 8], [0, 16]], 0, 0, 1e6)
-    ts(ap("blk", ALL), ap("blk", ALL), c1(PG), A.is_equal, 1.0 / 64, A.mult)
+    ts(ap("bl16", ALL), ap("blk", ALL), c1(PG), A.is_equal, 1.0 / 64, A.mult)
     for k in range(16):
-        lin(ap("rr", k, ALL), ap("blk", ALL), scale=mk(k))
+        lin(ap("rr", k, ALL), ap("bl16", ALL), scale=mk(k))
     add([("G", 170 + 2 * CY * 2048, ("affine_select", [ap("ll", ALL), ap("rr", ALL), [[0, 16], [-1, 128]], A.not_equal, -1.0 / 64, 0, 1], {}))],
         [ap("rr", ALL)], [ap("ll", ALL)])
-    IB, NIB, HIB, ZB, ONB, NKB = [ap("mb", i, ALL) for i in range(6)]
-    IH, HIH, NI64, DN67, P1, P2, D9 = [ap("mh", i, ALL) for i in range(7)]
+    IB, NIB, HIB, ZB = [ap("mb", i, ALL) for i in range(4)]
+    IH, HIH, NI64, I16H, C0, C1, P1, W7, C1S = [ap("mh", i, ALL) for i in range(9)]
     ix128 = ap("ix", S_(0, 128))
-    for m, c in [(IB, 1.0), (NIB, -1.0), (NKB, -1024.0), (HIB, -0.5), (IH, 1.0), (HIH, 0.5), (NI64, -1.0 / 64), (DN67, c1(N67)), (D9, c1(GE9)),
-                 (ap("mh", 7, ALL), c1(NASK)), (ap("mh", 8, ALL), c1(NASK + 1)), (ap("mh", 9, ALL), c1(NASK + 2))]:
-        ts(m, ix128, c1(33), A.is_equal, c, A.mult)
-    memset(ZB, 0.0)
-    memset(ONB, 1.0 / 8192)
-    tt(P1, wsl("ws", 0, 2), wsl("ws", 1, 3), A.add)
-    tt(P1, P1, wsl("ws", 7, 8), A.add)
-    tt(P2, wsl("ws", 0, 4), wsl("ws", 1, 5), A.add)
-    tt(P2, P2, D9, A.add)
+    ts(IB, ix128, c1(PP), A.is_equal)
+    ts(IH, ix128, c1(PP), A.is_equal)
+    ts(c1(TMP + 3), c1(PP), 8.0, A.add)
+    ts(C1S, ix128, c1(TMP + 3), A.is_equal, c1(H0), A.mult)
+    for m, c in [(NIB, -1.0), (HIB, 0.5), (ZB, 0.0)]:
+        lin(m, IB, scale=c)
+    for m, c in [(HIH, 0.5), (NI64, -1.0 / 64), (I16H, 16.0), (C0, c1(H0)), (P1, c1(CCOL))]:
+        lin(m, IH, scale=c)
+    lin(W7, ix128, scale=0.0, bias=mk(7))
+    mm([(P(3, S_(144, 272)), IH, C0), (P(3, S_(144, 272)), wsl("weh", 0, 15), P1)])
+    lin(C0, P(3, S_(144, 272)))
+    mm([(P(3, S_(256, 384)), IH, wsl("ws", a, b)) for a, b in ((0, 2), (1, 3), (7, 8))])
+    lin(P1, P(3, S_(256, 384)))
+    mm([(P(3, S_(384, 512)), IH, wsl("ws", a, b)) for a, b in [(0, 4), (1, 5)] + [(k, k) for k in range(9, 16)]])
+    lin(ap("p2f", ALL), P(3, S_(384, 512)))
     iota(ap("kc", 0, ALL), [[0, 32], [1, 2], [2, 8]], 0, 0)
-    iota(ap("dtab", S_(0, B0)), [[0, B0 // 4], [1, 4]], 0, 0)
-    iota(ap("dtab", S_(B0, DUM)), [[0, 2 * L // 4], [1, 4]], 0, 0)
     iota(ap("uu", ALL), [[0, 32], [1, 16]], 0, 0)
     iota(ap("kc", 1, ALL), [[0, 32], [1, 2], [2, 8]], 1, 0)
     memset(ap("kc", 1, S_(15, L, 16)), 0.0)
     ts(ap("rs0", ALL), ap("uu", ALL), 0.0, A.is_equal)
     ts(ap("rstk", ALL), ap("uu", ALL), 0.0, A.is_equal, 16777216.0, A.mult)
-    ts(ap("dm0", ALL), ap("uu", ALL), c1(PM), A.is_gt, 61.0, A.mult)
-    ts(ap("scm", ALL), ap("uu", ALL), 0.0, A.mult, mk(0), A.add)
+    ts(ap("dm0", ALL), ap("uu", ALL), c1(PM), A.is_gt, 128.0, A.mult)
     ts(ap("kp", ALL), ap("uu", ALL), -4096.0, A.mult, 65536.0, A.add)
     memset(ap("rs1", ALL), 0.0)
     memset(ap("rs1", S_(0, 272, 17)), 1.0)
-    iota(ap("lane", ALL), [[1, L]], 0, 0)
-    iota(ap("tt", S_(0, DUM + 32)), [[0, DUM + 32]], 0, 0)
-    iota(ap("tt", S_(DUM + 32, DUM + 48)), [[0, 16]], -1, 0)
+    for t in range(R):
+        iota(ap("nv", t, ALL), [[1, L]], B0 + L * t, 0)
+    iota(ap("st", S_(512, 640)), [[0, 128]], 0, 0)
+    iota(ap("kk", S_(0, OFF)), [[0, OFF]], 0, 0)
     iota(ap("ia", 0, ALL), [[16, 32]], 0, 0)
-    iota(ap("ia", 1, ALL), [[0, 16], [16, 2]], 0, 0)
-    ts(ap("itc", ALL), ap("ia", 0, ALL), c1(PM), A.add, -1535.0, A.add)
-    ts(ap("ia", 1, ALL), ap("ia", 1, ALL), c1(DE), A.add)
-    ts(ap("ia", 2, ALL), ap("ia", 0, ALL), c1(PM), A.add, -L - CEN, A.add)
+    ts(ap("itc", 0, ALL), ap("ia", 0, ALL), c1(PM), A.add, 1.0 / 512, A.mult)
+    ts(ap("itc", 1, ALL), ap("ia", 0, ALL), 0.0, A.mult, 511.0, A.add)
+    ts(ap("ia", 1, ALL), ap("ia", 0, ALL), c1(PM), A.add, -OFF - CEN, A.add)
     iota(ap("blk", ALL), [[256, 8], [1, 16]], 0, 0)
-    ts(ap("kq", ALL), ap("blk", ALL), c1(32), A.add)
-    iota(ap("nb", S_(512, 1536)), [[0, 1024]], 0, 0)
+    ts(ap("kq", ALL), ap("blk", ALL), c1(P16), A.add)
     p8 = S_(0, 8)
     iota(pap("l8", p8, ALL), [[1, 8], [0, 16]], 0, -1)
     ts(pap("l8", p8, ALL), pap("l8", p8, ALL), 0.0, A.is_equal)
     copy(pap("thf", p8, S_(0, R)), pap("thi", p8, S_(0, R)))
-    mm([(P(7, S_(0, R)), pap("l8", p8, ALL), pap("thf", p8, S_(0, R)))])
-    ts(ap("col", S_(TH, TH + R)), P(7, S_(0, R)), 16.0, A.mult, -0.5, A.add)
+    mm([(P(1, S_(300, 300 + R)), pap("l8", p8, ALL), pap("thf", p8, S_(0, R)))])
+    ts(ap("col", S_(TH, TH + R)), P(1, S_(300, 300 + R)), 16.0, A.mult, -0.5, A.add)
+
+    def o1(t, j, e=None):
+        if t and kof(t, j, e) not in (6, 7):
+            return ap("of2", kof(t, j, e), S_(32 * t - 32, 32 * t))
+        c = t * L + 64 * j
+        return ap("of1", S_(c, c + 64)) if e is None else ap("of1", S_(c + 32 * e, c + 32 * e + 32))
+
+    def cu(t, j, e):
+        c = t * L + 64 * j + 32 * e
+        return ap("cu", S_(c, c + 32))
 
     def lists(t):
-        copy(ap("kvr", t, S_(0, L, 2)), ap("ki", S_(t, 1024, 4)))
-        copy(ap("kvr", t, S_(1, L, 2)), ap("ki", S_(1024 + t, 2048, 4)))
-        js = STA[t]
-        groups = [[x] for x in js] if t == 0 else [js[:2], js[2:]]
-        for gr in groups:
-            dma([(o1(t, j, e), pap("kvr", S_(kof(t, j, e), 128, 16), t, ALL)) for j, es in gr for e in es])
-
-    def o1(t, j, e):
-        c = t * L + 64 * j + 32 * e
-        return ap("of1", S_(c, c + 32))
-
-    def cu(t, j, e=None):
-        c = t * L + 64 * j
-        return ap("cu", S_(c, c + 64)) if e is None else ap("cu", S_(c + 32 * e, c + 32 * e + 32))
-
-    def rows06(c0, c1_):
-        dma([(pap("dtab", S_(j, 128, 16), S_(c0, c1_)), kk(c0, c1_, 1, S_(j, 128, 16))) for j in range(6)])
+        if t == 0:
+            copy(ap("kvr", S_(0, L, 2)), ap("ki", S_(0, 1024, 4)))
+            copy(ap("kvr", S_(1, L, 2)), ap("ki", S_(1024, 2048, 4)))
+            mark["kvr"] = len(ops) - 1
+            for q in QUADS[0]:
+                for j in q:
+                    dma([(o1(0, j, e), pap("kvr", row(kof(0, j, e)), ALL)) for e in BOTH])
+        if t == 1:
+            for u in (1, 2):
+                for h in BOTH:
+                    copy(ap("kw2", ALL, u - 1, S_(h, 32, 2)), ap("ki", S_(1024 * h + u, 1024 * h + 1024, 4)))
+            for ks in ((1, 2), (3, 4), (9, 10), (11, 12), (13, 14), (15, 0), (5, 8)):
+                dma([(ap("of2", k, ALL), pap("kw2", row(k), ALL, ALL, ALL)) for k in ks])
 
     lists(0)
-    lin(kk(0, 1152), ap("ki", S_(0, 1152)))
-    lin(kk(1152, B0), ap("ki", S_(1152, B0)))
-    rows06(0, B0)
+    lin(kk(0, 1152), ap("ki", S_(0, 1152)), eng="G")
+    lin(kk(1152, B0), ap("ki", S_(1152, B0)), eng=KK2)
+    iota(ap("dtab", ALL), [[0, B0 // 4], [1, 4]], 0, 0)
+    dma([(pap("dtab", row(j), ALL), pap("kin", row(j), ALL)) for j in range(6)], after="kvr")
+    mm([(P(3, S_(0, 144)), wsl("we", E16, r), ap("xx", S_(144 * r, 144 * r + 144))) for r in range(16)])
+    lin(ap("sxc", ALL), P(3, S_(0, 144)), scale=1.0 / 16, eng="V")
+    dma([(pap("dtab", row(7), S_(0, B0)), ap("sxc", ALL))])
     for t in range(R):
-        lin(ap("xv", t, ALL), ap("xx", vcols(t)), eng="G" if t else "VA")
+        lin(xv(t), ap("xx", vcols(t)), eng="G" if t else "VA")
+    for t in range(R):
+        mm([(P(1, S_(32 * t, 32 * t + 32)), wsl("we", EW + t, r), ap("nb", t, S_(r, L, 16))) for r in range(16)])
+    mm([(P(1, S_(128, 224)), wsl("we", E16, r), ap("nb", ALL, S_(r, L, 16))) for r in range(16)])
+    copy(ap("sa", 0, ALL), P(1, S_(0, 96)))
+    ts(ap("sxv", ALL), P(1, S_(128, 224)), 1.0 / 16, A.mult, -2040.0, A.add)
+    ts(ap("sa", 1, ALL), ap("sa", 0, ALL), 2047, A.bitwise_and)
+    copy(ap("su", S_(0, R), ALL), ap("sa", 1, ALL))
+    for t in range(R):
+        push(ap("qa", t, ALL), ap("su", t, ALL), 1 + t)
 
     def bulk(t):
         if t == 0:
-            push(ap("rk0", ALL), ap("ki", S_(0, 2048)), 0, ("names", 0))
-            push(ap("rx0", ALL), ap("xx", S_(0, B0)), 0, ("names", 0))
+            push(ap("rx0", ALL), ap("xx", S_(0, B0)), -1, ("names", 0))
+            dma([(pap("yk", row(j), S_(0, B0)), kk(0, B0, 1, row(j))) for j in range(16) if j not in (6, 7, 9, 10, 11)], after=("names", 0))
         if t == 1:
-            push(ap("rx1", S_(0, B0)), ap("xx", S_(0, B0)), 1, ("names", 1))
+            push(ap("rx1", S_(0, B0)), ap("xx", S_(0, B0)), -2, ("names", 1))
         if t == 2:
-            push(ap("rx2", S_(0, B0)), ap("xx", S_(0, B0)), 2, ("names", 2))
-            dma([(pap("yk", S_(j, 128, 16), S_(0, B0)), kk(0, B0, 1, S_(j, 128, 16))) for j in range(16) if j not in (6, 7, 9, 10, 11)],
-                after=("names", 2))
+            push(ap("rx2", S_(0, B0)), ap("xx", S_(0, B0)), -3, ("names", 2))
 
-    for t in range(R):
-        mm([(P(6, S_(0, 32)), wsl("we", EW + t, r), ap("xv", t, S_(r, L, 16))) for r in range(16)])
-        copy(ap("si", 2, ALL), P(6, S_(0, 32)))
-        ts(ap("si", 3, ALL), ap("si", 2, ALL), 2047, A.bitwise_and)
-        copy(ap("su", t, ALL), ap("si", 3, ALL))
+    cnt = {}
 
-    cnt = {"g1": 0, "bb": 0, "rb": 0, "db": 0, "cc": 0, "gt": 0, "gh": 0}
+    def nxt(n, m, late=0):
+        k = cnt.get((n, late), 0)
+        cnt[(n, late)] = k + 1
+        return m + k % late if late else k % m
 
-    def nxt(n, m):
-        cnt[n] += 1
-        return (cnt[n] - 1) % m
-
-    def cpp(t, j, e):
-        return P(2 + t % 2, S_(j + 8 * e, L, 16))
+    def pos(t, b, j, es):
+        return P(b + t % 2, S_(j, L, 8)) if len(es) == 2 else P(b + t % 2, S_(j + 8 * es[0], L, 16))
 
     def es_(es):
         return S_(32 * es[0], 32 * es[-1] + 32)
 
-    def numbers(t, j, es, s):
-        mm([(cpp(t, j, e), IH, ap("cc", s, S_(32 * e, 32 * e + 32))) for e in es], ("c", t))
-
-    def names_static(t, j, es):
-        s = nxt("cc", NCC)
-        prs = []
-        for e in es:
-            g = nxt("g1", NG1)
-            lin(ap("g1", g, ALL), ind(ap("ki", S_(0, B0)), o1(t, j, e)), bias=-CEN)
-            prs.append((ap("cc", s, S_(32 * e, 32 * e + 32)), pap("g1", S_((kof(t, j, e) + t) % 16, 128, 16), g, ALL)))
-        dma(prs)
-        mark[("names", t)] = len(ops) - 1
-        ts(cu(t, j, None if len(es) == 2 else es[0]), ap("cc", s, es_(es)), CEN, A.add)
-        numbers(t, j, es, s)
-
-    def list_pe(t, j, e, src, b):
-        k = kof(t, j, e)
-        mm([(P(b, S_(0, 32)), wsl("ws", k, r), ap(src, S_(r, L, 16))) for r in range(16)])
-        ts(o1(t, j, e), P(b, S_(0, 32)), CEN, A.add)
-
-    def names_dyn(t, j, es, b):
-        s = nxt("gh", 2)
-        for e in es:
-            kr = (kof(t, j, e) + t) % 16
-            lin(ap("gh", s, e, ALL), ind(kk(0, B0 + L * t) if t else ap("ki", ALL), o1(t, j, e)), scale=mk(kr), bias=mk(16 + kr))
-        mm([(P(b, es_(es)), ap("weh", S_(15 - r, 143 - r)), ap("gh", s, S_(es[0], es[-1] + 1), S_(r, L, 16))) for r in range(16)])
-        ts(cu(t, j, None if len(es) == 2 else es[0]), P(b, es_(es)), CEN, A.add)
-        s = nxt("cc", NCC)
-        lin(ap("cc", s, es_(es)), P(b, es_(es)), eng="V")
-        numbers(t, j, es, s)
-
-    def score(t, j, es, dyn):
-        wd = B0 + (L * t if dyn else 0)
-        mode = MODES[t][j if dyn or len(es) == 2 else 8]
-        rs, ds = nxt("rb", NRB), nxt("db", NDB)
-        xw = ap("xx", S_(0, wd))
-        ee = S_(es[0], es[-1] + 1)
-        terms = []
-        if mode == "A":
-            for e in es:
-                g = nxt("gt", 2)
-                act(ap("gt", g, ALL), ind(xw, cu(t, j, e)), F.Identity)
-                mm([(P(4 + g), IB, ap("gt", g, ALL)), (P(4 + g), NIB, ap("xv", t, ALL))])
-                act(ap("rb", rs, ALL, e), P(4 + g), F.Abs)
-            terms.append((E16, "rb", rs))
-        else:
-            bs = nxt("bb", NBB)
-            for e in es:
-                tt(ap("bb", bs, ALL, e), ind(xw, cu(t, j, e)), ap("xv", t, ALL), A.subtract)
-            if mode == "V":
-                ts(ap("rb", rs, ALL, ee), ap("bb", bs, ALL, ee), 0.0, A.max)
-                terms += [(EM16, "bb", bs), (E32, "rb", rs)]
+    def names_static(t, js, es, late=False):
+        s = nxt("cc", NCC, 3 * late)
+        prs, nums = [], []
+        for i, j in enumerate(js):
+            g = nxt("g1", NG1, 1 * late)
+            if t:
+                for e in es:
+                    lin(ap("g1", g, S_(L * e, L * e + L)), ind(kk(0, B0 + L * t) if late else ap("ki", ALL), o1(t, j, e)), bias=-CEN)
             else:
-                act(ap("rb", rs, ALL, ee), ap("bb", bs, ALL, ee), F.Abs)
-                terms.append((E16, "rb", rs))
-        for e in es:
-            tt(ap("db", ds, ALL, e), ind(ap("dtab", S_(0, wd)), cu(t, j, e)), ap("dv", t % 2, ALL), A.is_equal)
-        terms.append((EBAR, "db", ds))
-        o = P(t % 2, S_(j, L, 8)) if len(es) == 2 else P(t % 2, S_(j + 8 * es[0], L, 16))
-        for w_, n, s in terms:
-            mm([(o, wsl("we", w_, r), ap(n, s, S_(r, L, 16), ee)) for r in range(16)], ("k", t))
+                lin(ap("g1", g, ALL), ind(ap("ki", ALL), o1(t, j)), bias=-CEN)
+            pj = [(ap("cc", s, S_(64 * i + 32 * e, 64 * i + 32 * e + 32)), pap("g1", row((kof(t, j, e) + t) % 16), g, S_(L * e, L * e + L))) for e in es]
+            dma(pj)
+            nums += [(pos(t, 2, j, (e,)), IH, pj[n][0]) for n, e in enumerate(es)]
+        mark[("late" if late else "names", t)] = len(ops) - 1
+        c, n = t * L + 64 * js[0] + 32 * es[0], 32 * len(es) * len(js)
+        ts(ap("cu", S_(c, c + n)), ap("cc", s, S_(32 * es[0], 32 * es[0] + n)), CEN, A.add)
+        mm(nums, ("c", t))
+
+    def list_pe(t, two, b):
+        for i, (j, e) in enumerate(two):
+            mm([(P(b, S_(32 * i, 32 * i + 32)), wsl("ws", kof(t, j, e), r), ap("kv16", S_(r, L, 16))) for r in range(16)])
+        c = t * L + 64 * two[0][0] + 32 * two[0][1]
+        ts(ap("of1", S_(c, c + 64)), P(b, S_(0, 64)), CEN, A.add)
+
+    def names_pe(t, two, b):
+        s = nxt("gh", 3)
+        for i, (j, e) in enumerate(two):
+            kr = (kof(t, j, e) + t) % 16
+            lin(ap("gh", s, i, ALL), ind(kk(0, B0 + L * t) if t else ap("ki", ALL), o1(t, j, e)), scale=mk(kr), bias=mk(16 + kr))
+        mm([(P(b, S_(0, 64)), wsl("weh", 0, r), ap("gh", s, ALL, S_(r, L, 16))) for r in range(16)])
+        c = t * L + 64 * two[0][0] + 32 * two[0][1]
+        ts(ap("cu", S_(c, c + 64)), P(b, S_(0, 64)), CEN, A.add)
+        s = nxt("cc", NCC, 3)
+        lin(ap("cc", s, S_(0, 64)), P(b, S_(0, 64)))
+        mm([(pos(t, 2, j, (e,)), IH, ap("cc", s, S_(32 * i, 32 * i + 32))) for i, (j, e) in enumerate(two)], ("c", t))
+
+    def names_late(t):
+        late = [(j, e) for j, es, _m in DYN[t] for e in es]
+        for j, es, _m in DYN[t]:
+            es = tuple(e for e in es if kof(t, j, e) not in (6, 7))
+            if es:
+                names_static(t, (j,), es, True)
+        names_pe(t, sorted(x for x in late if kof(t, *x) in (6, 7)), 6)
+
+    def terms(t, j, es, lst):
+        ee = S_(es[0], es[-1] + 1)
+        for w_, i, n, s in lst:
+            mm([(pos(t, 0, j, es), wsl(w_, i, r), ap(n, s, S_(r, L, 16), ee)) for r in range(16)], ("k", t))
+
+    def by_scalar(t, j, e, rs, wd):
+        s, b = nxt("gt", 2), 4 + nxt("pb", 2)
+        lin(ap("gt", s, ALL), ind(ap("xx", S_(0, wd)), cu(t, j, e)))
+        mm([(P(b), NIB, xv(t)), (P(b), IB, ap("gt", s, ALL))])
+        act(ap("rb", rs, ALL, e), P(b), F.Abs)
+
+    def score_quad(t, js):
+        gs = []
+        lead[0] = LEAD[t] * (7 - js[-1])
+        for j in js:
+            rs, g = nxt("rb", NRB), nxt("gd", NGD)
+            gs.append(g)
+            for e in BOTH:
+                lin(ap("gd", g, ALL, e), ind(ap("dtab", S_(0, B0)), cu(t, j, e)), scale=c1(GS), bias=c1(GB))
+            if PIECES[t][j] == 0:
+                for e in BOTH:
+                    by_scalar(t, j, e, rs, B0)
+                terms(t, j, BOTH, [("we", E16, "rb", rs)])
+                continue
+            for e in BOTH:
+                n = PIECES[t][j]
+                for q in range(n):
+                    c = t * L + 64 * j + 32 * e + 32 // n * q
+                    ls = S_(L // n * q, L // n * (q + 1))
+                    tt(ap("rb", rs, ls, e), ind(ap("xx", S_(0, B0)), ap("cu", S_(c, c + 32 // n))), ap("nb", t, ls), A.min)
+            terms(t, j, BOTH, [("we", EM32, "rb", rs), ("weh", 1, "gd", g)])
+            mm([(pos(t, 0, j, (e,)), I16H, ap("sxv", t, ALL)) for e in BOTH], ("k", t))
+        blood(t, js, gs, 0)
+        lead[0] = 0.0
+
+    def blood(t, js, gs, late):
+        ds = nxt("db", NDB, late)
+        two = [(ap("gd", gs[0], ALL, q), ap("gd", gs[1], ALL, q)) for q in BOTH] if len(js) == 2 else [(ap("gd", gs[0], ALL, 0), ap("gd", gs[0], ALL, 1))]
+        for q, (g0, g1) in enumerate(two):
+            b = 4 + nxt("pb", 2)
+            mm([(P(b), C0, g0), (P(b), C1S, g1)])
+            tt(ap("db", ds, ALL, q), P(b), ap("dv", t % 2, ALL), A.is_equal)
+        if len(js) == 2:
+            terms(t, js[0], BOTH, [("we", EBAR0, "db", ds)])
+            terms(t, js[1], BOTH, [("we", EBAR1, "db", ds)])
+        else:
+            for e in BOTH:
+                mm([(pos(t, 0, js[0], (e,)), wsl("we", EBAR0 + e, r), ap("db", ds, S_(r, L, 16), 0)) for r in range(16)], ("k", t))
+
+    def score_late(t):
+        gs = {}
+        for part in (DYN[t][:2], DYN[t][2:]):
+            for j, es, mode in part:
+                gs[j] = nxt("gd", NGD, LATE + 1)
+                for e in BOTH:
+                    if mode[e] == "M":
+                        lin(ap("gd", gs[j], ALL, e), ind(ap("dtab", ALL), cu(t, j, e)), scale=c1(GS), bias=c1(GB))
+                    else:
+                        lin(ap("gd", gs[j], ALL, e), ind(kk(0, B0 + L * t), cu(t, j, e)), scale=c1(GS2), bias=c1(GB))
+            if part:
+                blood(t, [x[0] for x in part], [gs[x[0]] for x in part], LATE)
+        late = sorted((j, e) for j, es, _m in DYN[t] for e in es)
+        c, n = t * L + 64 * late[0][0], 32 * len(late)
+        copy(ap("mi", 0, S_(0, n)), ap("cu", S_(c, c + n)))
+        ts(ap("mi", 1, S_(0, n)), ap("mi", 0, S_(0, n)), 3, A.bitwise_and)
+        ts(ap("mf", S_(0, n)), ap("mi", 1, S_(0, n)), float(t), A.is_equal, BAR, A.mult)
+        mm([(pos(t, 0, j, (e,)), IB, ap("mf", S_(32 * i, 32 * i + 32))) for i, (j, e) in enumerate(late)], ("k", t))
+        for j, es, mode in DYN[t]:
+            score(t, j, mode, gs[j])
+
+    def score(t, j, mode, g):
+        rs = nxt("rb", NRB, LATE)
+        wd = [B0 if m == "M" else B0 + L * t for m in mode[:2]]
+        for es in ([BOTH] if mode[0] == mode[1] else [(0,), (1,)]):
+            m = mode[es[0]]
+            xw = ap("xx", S_(0, wd[es[0]]))
+            ee = S_(es[0], es[-1] + 1)
+            if m == "A":
+                for e in es:
+                    by_scalar(t, j, e, rs, wd[e])
+                terms(t, j, es, [("we", E16, "rb", rs)])
+            elif m == "W":
+                bs = nxt("bb", NBB)
+                for e in es:
+                    tt(ap("bb", bs, ALL, e), ind(xw, cu(t, j, e)), xv(t), A.subtract)
+                    act(ap("rb", rs, ALL, e), ap("bb", bs, ALL, e), F.Abs)
+                terms(t, j, es, [("we", E16, "rb", rs)])
+            elif m == "V":
+                bs = nxt("bb", NBB)
+                for e in es:
+                    tt(ap("bb", bs, ALL, e), ind(xw, cu(t, j, e)), xv(t), A.subtract)
+                ts(ap("rb", rs, ALL, ee), ap("bb", bs, ALL, ee), 0.0, A.min)
+                terms(t, j, es, [("we", E16, "bb", bs), ("we", EM32, "rb", rs)])
+            else:
+                for e in es:
+                    tt(ap("rb", rs, ALL, e), ind(xw, cu(t, j, e)), xv(t), A.min)
+                terms(t, j, es, [("we", EM32, "rb", rs), ("weh", 1, "gd", g)])
+                mm([(pos(t, 0, j, (e,)), I16H, ap("sxv", t, ALL)) for e in es], ("k", t))
 
     def opens(t):
         mm([(P(t % 2), IB, ap("kc", t % 2, ALL))], ("k", t))
@@ -422,176 +546,172 @@ def build():
     def su(i, *ix):
         return ap("su", i, *(ix if ix else (ALL,)))
 
-    MU, GO, SO, RO, ONEW, OVC, MSD, NO = range(3, 11)
+    MU, I1, SO, RO, ONEW, OVC, NO, XI = range(3, 11)
+    CHILD, KV, WEDV, ASKV = [S_(L * i, L * i + L) for i in range(4)]
 
     def prepare(t):
         src = kk(t, 2048, 4)
         if t:
             lin(ap("kv16", ALL), src, bias=-CEN)
-            for j, es in DYN[t]:
-                for e in es:
-                    if kof(t, j, e) in (6, 7):
-                        list_pe(t, j, e, "kv16", 6 + e)
-        lin(ap("cb", S_(1024, 1536)), src, eng="G")
-        dma([(ap("cb", S_(1536, 2048)), ap("cb", S_(1024, 1536)))])
-        lin(ap("cn", ALL), ap("lane", ALL), scale=c1(SCN), bias=c1(BCN + t))
-        lin(ap("xq", ALL), ap("xv", t, ALL), scale=1.0 / 1024)
-        mm([(P(7), ap("mh", 7 + t, ALL), ap("kv16", ALL)), (P(7), wsl("ws", 7, 9 + t), ap("cn", ALL))])
-        lin(ap("cb", S_(2048, 2560)), P(7), bias=CEN)
-        tt(ap("pkv", ALL), ind(ap("rk%d" % t, ALL), su(t)), ap("xq", ALL), A.add)
+            list_pe(t, sorted((j, e) for j, es, _m in DYN[t] for e in es if kof(t, j, e) in (6, 7)), 7)
+        for c in (KV, WEDV, ASKV):
+            lin(ap("cb", c), src, eng="G")
+        iota(ap("vv", ALL), [[4, L]], t, 0)
+        dma([(pap("kk", row(7), S_(0, OFF)), pap("nv", row(7), t, ALL)), (pap("kk", row(6), S_(0, OFF)), pap("vv", row(6), ALL))])
+        dma([(pap("cb", row(7), WEDV), pap("nv", row(7), t, ALL)), (pap("cb", row(9 + t), ASKV), pap("nv", row(7), t, ALL))])
 
-    def early(t):
-        lin(ap("kve", ALL), ap("ki", vcols(t)), bias=-CEN)
-        for j, es in DYN[t]:
-            for e in es:
-                if kof(t, j, e) not in (6, 7):
-                    list_pe(t, j, e, "kve", 4 + e)
+    def answer(t):
+        lin(ap("pkv", ALL), ind(kk(0, 2048) if t else ap("ki", S_(0, 2048)), ap("qa", t, ALL)), scale=1024.0)
+        push(ap("rk", t, ALL), ap("pkv", ALL), -1 - t)
 
     def tail(t):
         n0 = B0 + L * t
         thr = c1(TH) if t == 0 else c1(THR + t)
         ends = S_(15, L, 16)
         kb, cb_ = t % 2, 2 + t % 2
+        lin(ap("xq", ALL), xv(t), eng="G")
         scan(ap("sc1", ALL), ap("rstk", ALL), P(kb), A.add, A.min)
         tt(ap("uu", ALL), P(kb), ap("sc1", ALL), A.not_equal)
         scan(ap("sc2", ALL), ap("uu", ALL), P(cb_), A.mult, A.max)
-        ts(sm(0), ap("sc1", ends), -131071.0, A.add, 8192.0, A.mult)
+        ts(sm(0), ap("sc1", ends), 100000.0, A.is_gt, 4096.0, A.mult)
         ts(sm(1), ap("sc1", ends), thr, A.subtract, 8192.0, A.mult)
+        tt(sm(2), sm(1), ap("ia", 1, ALL), A.max)
         ts(sm(3), ap("sc2", ends), MAGIC * 4096, A.add, -MAGIC * 4096, A.add)
-        M = ap("si", 1, ALL)
+        M = sm(15)
         tt(M, ap("sc2", ends), sm(3), A.subtract)
-        tt(sm(2), M, sm(0), A.max)
-        tt(ap("m16", ALL), sm(2), ap("ia", 1, ALL), A.min)
-        ts(su(MU), M, CEN, A.add)
-        tt(sm(4), M, sm(1), A.max)
-        ts(su(GO), sm(4), DUM + 32 - CEN, A.min, CEN, A.add)
         m16 = ap("m16", ALL)
+        tt(m16, M, sm(0), A.add)
+        ts(su(MU), M, CEN, A.add)
+        tt(sm(4), M, sm(2), A.min)
+        ts(su(I1), sm(4), OFF + CEN, A.add)
         mm([(P(6), IB, ap("dm0", ALL))], ("d0", t))
         mm([(P(6, S_(r + 1, L, 16)), ap("ll", r, ALL), m16) for r in range(15)], ("d0", t))
-        mm([(P(7, S_(0, 272)), ZB, ap("rs1", ALL))], ("d1", t))
+        mm([(P(7, S_(0, 272, 17)), ZB, ap("rs1", S_(0, 16)))], ("d1", t))
         mm([x for r in range(16) for x in ((P(7, S_(r + 1, 272, 17)), ap("rr", r, ALL), ap("m16", S_(0, 32, 2))),
                                            (P(7, S_(r + 1, 272, 17)), NI64, ap("m16", S_(1, 32, 2))))], ("d1", t))
-        act(ap("km16", ALL), ind(kk(0, n0), su(MU)), F.Identity, bias=-CEN)
-        act(ap("xm16", ALL), ind(ap("xx", S_(0, n0)), su(MU)), F.Identity, bias=-0.5)
+        lin(ap("km", ALL), ind(kk(0, n0), su(MU)), scale=c1(N67))
+        lin(ap("val", ALL), ind(kk(-OFF, n0), su(I1)))
+        lin(ap("xm16", ALL), ind(ap("xx", S_(0, n0)), su(MU)), bias=-0.5)
         scan(ap("sc2", ALL), P(6), ap("rs0", ALL), A.mult, A.add)
         scan(ap("sd1", ALL), P(7, S_(0, 272)), ap("rs1", ALL), A.mult, A.add)
-        mm([(P(kb), DN67, ap("kv16", ALL)), (P(kb), wsl("ws", 7, 7), ap("cn", ALL))] +
-           [(P(kb, S_(r, L, 16)), wsl("ws", r, 6), m16) for r in range(16)])
-        act(ap("cb", S_(512, 1024)), P(kb), F.Identity, bias=CEN)
-        mm([(P(cb_), P1, ap("kv16", ALL)), (P(cb_), IH, ap("cn", ALL)), (P(cb_), P2, ap("km16", ALL))] +
+        mm([(P(cb_), P1, ap("kv16", ALL)), (P(cb_), ap("p2f", ALL), ap("km", ALL))] +
            [(P(cb_, S_(r, L, 16)), wsl("ws", r, 1), m16) for r in range(16)])
-        act(ap("cb", S_(0, 512)), P(cb_), F.Identity, bias=CEN)
-        mm([(P(7), DN67, ap("km16", ALL)), (P(7), wsl("ws", 0, 6), ap("cn", ALL)), (P(7), wsl("ws", 7, 7), ap("cn", ALL))])
-        act(ap("km", ALL), P(7), F.Identity, bias=CEN)
-        mm([(P(kb), HIH, ap("xm16", ALL)), (P(kb), HIB, ap("xv", t, ALL))])
-        ts(ap("nb", S_(0, 512)), P(kb), MAGIC, A.add, -MAGIC, A.add)
+        lin(ap("cb", CHILD), P(cb_), bias=c1(CHB))
+        dma([(pap("cb", row(6), WEDV), pap("cb", row(1), CHILD)), (pap("cb", row(0), CHILD), pap("vv", row(0), ALL))] +
+            [(pap("cb", row(j), CHILD), pap("nv", row(j), t, ALL)) for j in (6, 7)])
+        mm([(P(kb), HIH, ap("xm16", ALL)), (P(kb), HIB, xv(t))])
+        ts(ap("nb", t, S_(512, 1024)), P(kb), MAGIC, A.add, -MAGIC, A.add)
         ts(sm(5), ap("sc2", ends), 0.0, A.is_equal, 8192.0, A.mult)
         ts(sm(6, S_(0, 16)), ap("sd1", S_(16, 272, 17)), 0.0, A.is_equal, 8192.0, A.mult)
         tt(sm(7), m16, sm(5), A.add)
         tt(sm(6, S_(16, 32)), sm(7, S_(1, 32, 2)), sm(6, S_(0, 16)), A.add)
         ts(su(SO, S_(1, 32, 2)), sm(6, S_(16, 32)), c1(DO), A.min, CEN, A.add)
         ts(su(SO, S_(0, 32, 2)), sm(7, S_(0, 32, 2)), c1(DE), A.min, CEN, A.add)
-        tw = ap("tt", ALL)
         for a in range(15, -1, -1):
-            copy(ind(tw, su(SO, S_(2 * a, 2 * a + 2))), ap("lane", S_(32 * a, 32 * a + 32)))
-        tt(ap("li", 0, ALL), ind(tw, su(GO)), ap("lane", ALL), A.not_equal)
-        scan(ap("li", 1, ALL), ap("scm", ALL), ap("li", 0, ALL), A.mult, A.add)
-        Y, Z = P(6, S_(0, 32)), P(7, S_(32, 64))
-        mm([(Y, wsl("we", EY, r), ap("li", 1, S_(r, L, 16))) for r in range(16)])
-        mm([(Z, IH, ap("itc", ALL))] + [(Z, wsl("we", EZ, r), ap("li", 1, S_(r, L, 16))) for r in range(16)])
-        ts(sm(8), Y, -896.0, A.is_gt, 4096.0, A.mult)
-        tt(sm(9), sm(8), Y, A.add)
-        tt(sm(10), sm(9), Z, A.min)
-        ts(su(RO), sm(10), 1535.0, A.add)
-        ts(su(ONEW), Z, 1535.0, A.add)
-        ts(ap("d1", ALL), Y, 0.0, A.is_lt, 8192.0, A.mult)
-        ts(sm(11), Y, -896.0, A.is_le, 512.0, A.mult)
-        tt(sm(12), sm(11), Z, A.add)
-        ts(su(OVC), sm(12), 1535.0, A.add)
-        tt(sm(13), M, ap("d1", ALL), A.subtract)
-        tt(sm(14), sm(13), ap("ia", 2, ALL), A.max)
-        ts(su(MSD), sm(14), L + CEN, A.add)
-        copy(ind(ap("tt", S_(0, 1536)), su(RO)), ap("pkv", ALL))
-        lin(kk(t, 2048, 4), ind(ap("cb", S_(512, 2560)), su(OVC)))
-        lin(kk(n0, n0 + L), ind(ap("cb", S_(0, 1536)), su(ONEW)))
-        copy(ind(kk(-L, n0), su(MSD)), ap("km", ALL))
+            tt(ind(kk(0, W + 32), su(SO, S_(2 * a, 2 * a + 2))), ap("val", S_(32 * a, 32 * a + 32)), ap("km", S_(32 * a, 32 * a + 32)), A.max)
+        tt(ap("li", 0, ALL), ind(kk(0, n0), su(MU)), ap("nv", t, ALL), A.not_equal)
+        scan(ap("li", 1, ALL), ap("li", 0, ALL), ap("li", 0, ALL), A.add, A.max)
+        Z, Y = P(7, S_(320, 352)), P(7, S_(352, 384))
+        mm([(P(7, S_(320, 384)), IH, ap("itc", ALL, ALL))] + [(P(7, S_(320, 384)), wsl("ws", 7, r), ap("li", ALL, S_(r, L, 16))) for r in range(16)])
+        ts(sm(8), Z, 512.0, A.mult)
+        tt(sm(9), Y, sm(8), A.min)
+        copy(su(RO), sm(9))
+        ts(su(ONEW), Z, 512.0, A.mult)
+        ts(sm(10), sm(9), 639.5, A.is_gt, -1024.0, A.mult)
+        tt(sm(11), sm(10), sm(8), A.add)
+        ts(su(OVC), sm(11), 1024.0, A.add)
+        tt(sm(12), sm(11), sm(9), A.min)
+        ts(su(XI), sm(12), 512.0, A.add)
+        tt(ind(ap("st", ALL), su(RO)), ap("rk", t, ALL), ap("xq", ALL), A.add)
+        lin(kk(t, 2048, 4), ind(ap("cb", ALL), su(OVC)))
+        lin(kk(n0, n0 + L), ind(ap("cb", S_(0, 1024)), su(ONEW)))
         if t + 1 < R:
-            mm([(P(7, S_(0, 32)), ONB, ap("d1", ALL))])
-            add([("V", 90.0, ("tensor_reduce", [c1(TOT), P(7, S_(0, 32)), AxisListType.X, A.add], {}))], [P(7, S_(0, 32))], [c1(TOT)])
-            ts(ap("pc", S_(3, 4)), c1(TOT), -1.0, A.mult, 4096.0, A.add)
-            ts(ap("pc", S_(3, 4)), ap("pc", S_(3, 4)), 15, A.bitwise_and)
-            ts(c1(THR + t + 1), ap("pc", S_(3, 4)), 16.0, A.mult, c1(TH + t + 1), A.add)
-            rows06(n0, n0 + L)
-            mark[("rows", t)] = len(ops) - 1
-            push(ap("rk%d" % (t + 1), ALL), kk(0, 2048), t + 1, ("rows", t))
-        st = [(pap("yk", S_(9 + t, 128, 16), S_(0, B0)), kk(0, B0, 1, S_(9 + t, 128, 16)))]
+            mm([(P(6, S_(0, 1)), W7, ap("li", 1, S_(L - 1, L)))])
+            ts(pc(4), P(6, S_(0, 1)), -1.0, A.mult, 4096.0, A.add)
+            ts(pc(5), pc(4), 15, A.bitwise_and)
+            ts(c1(THR + t + 1), pc(5), 16.0, A.mult, c1(TH + t + 1), A.add)
+
+    def stores(t):
+        n0 = B0 + L * t
+        if t + 1 < R:
+            answer(t + 1)
+        st = [(pap("yk", row(9 + t), S_(0, B0)), kk(0, B0, 1, row(9 + t)))]
         if t + 1 == R:
-            dma(st + [(pap("yk", S_(j, 128, 16), S_(0, n0)), kk(0, n0, 1, S_(j, 128, 16))) for j in (6, 7)])
+            dma(st + [(pap("yk", row(j), S_(0, n0)), kk(0, n0, 1, row(j))) for j in (6, 7)])
             st = []
-        dma(st + [(ap("yk", S_(n0, n0 + L)), kk(n0, n0 + L))], after=("rows", t) if t + 1 < R else None)
-        slot = ap("tt", S_(512, 640))
-        copy(ap("du", ALL), slot)
-        ts(ap("ai", ALL), slot, MAGIC, A.add, -MAGIC, A.add)
+        dma(st + [(ap("yk", S_(n0, n0 + L)), kk(n0, n0 + L))], after=("late", t + 1) if t + 1 < R else None)
+
+    def ask(t):
+        n0 = B0 + L * t
+        kb, cb_ = t % 2, 2 + t % 2
+        slot = ap("st", S_(512, 640))
+        ts(ap("du", ALL), slot, 1.0 / 1024, A.mult)
+        ts(ap("ai", ALL), slot, MAGIC * 1024, A.add, -MAGIC * 1024, A.add)
         tt(ap("xs", ALL), slot, ap("ai", ALL), A.subtract)
-        lin(ap("xa", ALL), ap("xs", ALL), scale=1024.0)
-        banks = [cb_, kb, 6, 7]
+        banks = [cb_, kb, cb_, kb] if t + 1 < R else [cb_, kb, 4, 5]
         for b in range(4):
-            gb = ap("ga", S_(L * b, L * b + L))
-            lin(gb, ind(ap("rx%d" % t, ALL), ap("du", S_(32 * b, 32 * b + 32))))
-            mm([(P(banks[b]), ZB, ap("rs0", ALL))], ("a", t, b))
-            mm([(P(banks[b], S_(k, L, 16)), NKB, ap("xs", S_(32 * b, 32 * b + 32))) for k in range(16)], ("a", t, b))
-            mm([(P(banks[b]), IB, gb)], ("a", t, b))
-            act(ap("ra", S_(2 * b, 2 * b + 2), ALL), P(banks[b]), F.Abs)
-        o = P(cb_, S_(0, 128))
+            lin(ap("ga", S_(L * b, L * b + L)), ind(ap("rx%d" % t, ALL), ap("du", S_(32 * b, 32 * b + 32))))
+        for b in range(4):
+            h, q = b // 2, b % 2
+            mm([(P(banks[b], S_(k, L, 8)), NIB, ap("xs", S_(64 * h, 64 * h + 64))) for k in range(8)], ("a", t, b))
+            mm([(P(banks[b], S_(k, L, 8)), IB, ap("ga", S_(1024 * h + 8 * q + k, 1024 * h + 1024, 16))) for k in range(8)], ("a", t, b))
+            act(ap("ra", S_(4 * h, 4 * h + 4), ALL, S_(8 * q, 8 * q + 8)), P(banks[b]), F.Abs, scale=128.0)
+        o = P(7, S_(0, 128))
         for h in range(2):
-            oh = P(cb_, S_(64 * h, 64 * h + 64))
+            oh = P(7, S_(64 * h, 64 * h + 64))
             mm([(oh, IH, ap("kq", S_(64 * h, 64 * h + 64)))] +
-               [(oh, wsl("we", E2048, r), ap("ra", S_(4 * h, 4 * h + 4), S_(16 * r, 16 * r + 16))) for r in range(16)])
+               [(oh, wsl("we", E16, r), ap("ra", S_(4 * h, 4 * h + 4), r, ALL)) for r in range(16)])
         scan(ap("sc1", S_(0, 128)), ap("rstk", S_(0, 128)), o, A.add, A.min)
-        copy(ap("si", 4, S_(0, 8)), ap("sc1", S_(15, 128, 16)))
-        ts(ap("si", 5, S_(0, 8)), ap("si", 4, S_(0, 8)), 2047, A.bitwise_and)
-        copy(su(NO, S_(0, 8)), ap("si", 5, S_(0, 8)))
-        tt(ap("nb", S_(512, 640)), ind(ap("ga", ALL), su(NO, S_(0, 8))), ap("xa", ALL), A.subtract)
-        tt(ap("xx", S_(n0, n0 + L)), ind(ap("nb", ALL), su(RO)), ap("xv", t, ALL), A.add)
+        copy(ap("si", 0, ALL), ap("sc1", S_(15, 128, 16)))
+        ts(ap("si", 1, ALL), ap("si", 0, ALL), 2047, A.bitwise_and)
+        copy(su(NO, S_(0, 8)), ap("si", 1, ALL))
+        lin(ap("nb", t, S_(1024, 1152)), ind(ap("ga", ALL), su(NO, S_(0, 8))))
+        lin(ap("xx", S_(n0, n0 + L)), ind(ap("nb", t, ALL), su(XI)))
         dma([(ap("yx", S_(L * t, L * t + L)), ap("xx", S_(n0, n0 + L)))])
         for u in range(t + 1, R):
-            push(ap("rx%d" % u, S_(n0, n0 + L)), ap("xx", S_(n0, n0 + L)), u)
+            push(ap("rx%d" % u, S_(n0, n0 + L)), ap("xx", S_(n0, n0 + L)), -1 - u)
+
+    def suitors(t):
+        lin(ap("dv", t % 2, ALL), ap("dtab", vcols(t)), eng="G")
+        dma([(pap("dv", row(j + 8), t % 2, ALL), pap("dv", row(j), t % 2, ALL)) for j in range(6)])
 
     def statics(t):
-        js = STA[t]
+        js = QUADS[t]
         if t:
-            lin(ap("dv", t % 2, ALL), ap("dtab", vcols(t)), eng="G")
-        for i in range(len(js) + 2):
+            suitors(t)
+        for i in range(len(js) + 1):
             if i < len(js):
-                names_static(t, *js[i])
-            if i >= 2:
-                score(t, js[i - 2][0], js[i - 2][1], False)
+                names_static(t, js[i], BOTH)
+            if i >= 1:
+                score_quad(t, js[i - 1])
+        for j, es, mode in LONE[t]:
+            names_static(t, (j,), es)
         bulk(t)
 
     opens(0)
     lin(ap("kv16", ALL), ap("ki", vcols(0)), bias=-CEN)
-    lin(ap("dv", 0, ALL), ap("dtab", vcols(0)), eng="G")
-    for j, es in DYN[0]:
-        for e in es:
-            list_pe(0, j, e, "kv16", 4 + e)
-        names_dyn(0, j, es, 6 + j % 2)
-    for j, es in DYN[0]:
-        score(0, j, es, True)
+    suitors(0)
+    for j, es, _m in DYN[0]:
+        list_pe(0, [(j, e) for e in es], 4 + j % 2)
+        names_pe(0, [(j, e) for e in es], 6 + j % 2)
+    for i in range(0, len(DYN[0]), 2):
+        score_quad(0, [j for j, es, _m in DYN[0][i:i + 2]])
     statics(0)
+    answer(0)
     prepare(0)
     for t in range(R):
         if t + 1 < R:
             opens(t + 1)
             lists(t + 1)
-            early(t + 1)
             statics(t + 1)
         tail(t)
         if t + 1 < R:
             prepare(t + 1)
-            for i, (j, es) in enumerate(DYN[t + 1]):
-                names_dyn(t + 1, j, es, 6 + i % 2)
-            for j, es in DYN[t + 1]:
-                score(t + 1, j, es, True)
+            names_late(t + 1)
+        stores(t)
+        ask(t)
+        if t + 1 < R:
+            score_late(t + 1)
     return ops
 
 
@@ -613,69 +733,149 @@ def depend(ops):
             for n, pm, cm, _1, _2 in regs:
                 h = hist.setdefault(n, [])
                 if wr:
-                    h[:] = [x for x in h if x[0] == i or (x[1] & ~pm) or (x[2] & ~cm)]
+                    bank = n[0] == "p" and n[1:].isdigit()
+                    h[:] = [x for x in h if x[0] == i or (x[1] & ~pm) or (x[2] & ~cm) or (bank and x[4] != fixed and cm + 1 != 1 << 512)]
                 h.append((i, pm, cm, wr, fixed))
         o["deps"] = deps
 
 
-def schedule(ops, jit, force):
+def search(ops, seed, tries, nj=4, amp=1500.0, temp=100.0):
     n = len(ops)
-    succ = [[] for _ in range(n)]
+    succ, dep = [[] for _ in range(n)], []
     for i, o in enumerate(ops):
+        gr = o["alts"][0][2][2].get("group")
+        dep.append([(j, bool(gr) and gr == ops[j]["alts"][0][2][2].get("group"), ops[j]["kind"] == "c") for j in o["deps"]])
         for j in o["deps"]:
             succ[j].append(i)
-    prio = [0.0] * n
-    for i in range(n - 1, -1, -1):
-        o = ops[i]
-        prio[i] = (min(a[1] for a in o["alts"]) + o["lat"] + LAT_X) + jit[i] + max([prio[s] for s in succ[i]] + [0.0])
-        if o["extra"]:
-            prio[i] += o["extra"]
-    busy = {e: [] for e in "VAPGY"}
-    fin, eng, start = [0.0] * n, [None] * n, [0.0] * n
-    for i in sorted(range(n), key=lambda i: -prio[i]):
-        best = None
-        o_g = ops[i]["alts"][0][2][2].get("group")
-        for a in ops[i]["alts"]:
-            e = a[0]
-            if force[i] and e != force[i]:
+    base = [min(a[1] for a in o["alts"]) + o["lat"] + LAT_X + (o["extra"] or 0.0) for o in ops]
+    cost = [{a[0]: a[1] for a in o["alts"]} for o in ops]
+    lat = [o["lat"] for o in ops]
+    moves = [o["kind"] != "c" for o in ops]
+
+    queues = "VAPGY"
+
+    def schedule(jit, shy):
+        prio = [0.0] * n
+        for i in range(n - 1, -1, -1):
+            m = 0.0
+            for s in succ[i]:
+                if prio[s] > m:
+                    m = prio[s]
+            prio[i] = base[i] + jit[i] + m
+        left = [len(d) for d in dep]
+        pool, free, wake = {e: [] for e in queues}, {e: 0.0 for e in queues}, {e: 0.0 for e in queues}
+        fin, start, eng = [0.0] * n, [0.0] * n, [None] * n
+        dfree = 0.0
+
+        def arrive(i, now):
+            for e in cost[i]:
+                s = 0.0
+                for j, same, cj in dep[i]:
+                    x = fin[j] - 60.0 if same else fin[j] + (LAT_S if cj and eng[j] == e else LAT_X)
+                    if x > s:
+                        s = x
+                p = -prio[i] + (shy[i] if e == "V" and len(cost[i]) > 1 else 0.0)
+                pl = pool[e]
+                k = len(pl)
+                while k and pl[k - 1][0] > p:
+                    k -= 1
+                pl.insert(k, (p, s, cost[i][e], i))
+                w = max(s, free[e], now)
+                if w < wake[e]:
+                    wake[e] = w
+
+        for i in range(n):
+            if not left[i]:
+                arrive(i, 0.0)
+        order = []
+        while len(order) < n:
+            e = min(queues, key=wake.get)
+            t = wake[e]
+            if e == "Y" and t < dfree - DPRE - 100.0:
+                wake[e] = dfree - DPRE - 100.0
                 continue
-            s = max([fin[j] - 60.0 if o_g and o_g == ops[j]["alts"][0][2][2].get("group") else fin[j] + (LAT_S if eng[j] == e and ops[j]["kind"] == "c" else LAT_X) for j in ops[i]["deps"]] + [0.0])
-            bz = busy[e]
-            k = len(bz)
-            while k > 0 and bz[k - 1][1] > s:
-                k -= 1
-            while k < len(bz) and s + a[1] > bz[k][0]:
-                s = max(s, bz[k][1])
+            pl = pool[e]
+            lim, top, pick, soon, k = 1e18, None, None, 1e18, 0
+            while k < len(pl):
+                p, s, c, i = pl[k]
+                if eng[i]:
+                    pl.pop(k)
+                    continue
+                if s <= t:
+                    if t + c <= lim or p - top < DEL:
+                        pick = k
+                        break
+                else:
+                    soon, lim = min(soon, s), min(lim, s + TOL)
+                    if top is None:
+                        top = p
                 k += 1
-            f = s + a[1] * (PEN if e == "V" else 1.0)
-            if best is None or f < best[0]:
-                best = (f, s, k, a)
-        _f, s, k, a = best
-        busy[a[0]].insert(k, (s, s + a[1]))
-        eng[i], start[i], fin[i] = a[0], s, s + a[1] + ops[i]["lat"]
-        ops[i]["pick"] = a
-    return sorted(range(n), key=lambda i: start[i]), start, fin
+            if pick is None:
+                wake[e] = soon
+                continue
+            p, s, c, i = pl.pop(pick)
+            eng[i], start[i] = e, t
+            wake[e] = free[e] = t + c
+            fin[i] = t + c + lat[i]
+            if moves[i]:
+                dfree = max(t + c + DPRE, dfree) + lat[i] - DPRE - DPOST
+                fin[i] = dfree + DPOST
+            order.append(i)
+            for s in succ[i]:
+                left[s] -= 1
+                if not left[s]:
+                    arrive(s, t)
+        return order, start, fin, eng
 
+    others = [build(m) for m in MODELS]
+    others = [([{a[0]: a[1] for a in o["alts"]} for o in x], [o["lat"] for o in x]) for x in others]
 
-def search(ops, seed, tries, nj=6, amp=1500.0, temp=50.0):
+    def replay(order, eng, k):
+        cs, lt = others[k]
+        pre, post, lx, ls = MODELS[k][3], MODELS[k][4], MODELS[k][7], MODELS[k][8]
+        free, fin, dfree = {e: 0.0 for e in queues}, [0.0] * n, 0.0
+        for i in order:
+            e = eng[i]
+            s = free[e]
+            for j, same, cj in dep[i]:
+                x = fin[j] - 60.0 if same else fin[j] + (ls if cj and eng[j] == e else lx)
+                if x > s:
+                    s = x
+            s = free[e] = s + cs[i][e]
+            if moves[i]:
+                dfree = max(s + pre, dfree) + lt[i] - pre - post
+                fin[i] = dfree + post
+            else:
+                fin[i] = s + lt[i]
+        return max(fin)
+
+    def times(jit, shy):
+        order, start, fin, eng = schedule(jit, shy)
+        return [replay(order, eng, k) for k in range(len(MODELS))]
+
     rng = np.random.RandomState(seed)
-    n = len(ops)
-    free = [i for i in range(n) if len(ops[i]["alts"]) > 1]
-    jit, force = [0.0] * n, [None] * n
-    cur = best = max(schedule(ops, jit, force)[2])
-    keep = (jit, force)
+    both = [i for i in range(n) if len(cost[i]) > 1]
+    jit, shy = [0.0] * n, [SHY] * n
+    norm = times(jit, shy)
+    norm = [norm[0] / x / len(norm) for x in norm]
+    cur = best = norm[0] * len(norm) * 1e9
+    keep = (jit, shy)
     for k in range(tries):
-        j2, f2 = list(jit), list(force)
+        j2, s2 = list(jit), list(shy)
         for i in rng.randint(0, n, nj):
             j2[i] = max(0.0, j2[i] + amp * float(rng.standard_normal()))
-        for i in rng.randint(0, len(free), 2):
-            f2[free[i]] = (None, "V", "A")[rng.randint(0, 3)]
-        m = max(schedule(ops, j2, f2)[2])
+        if k % 2:
+            s2[both[rng.randint(0, len(both))]] = (0.0, SHY, 1e5)[rng.randint(0, 3)]
+        m = sum(a * b for a, b in zip(times(j2, s2), norm))
         if m <= cur + temp * (1 - k / tries) * float(rng.exponential()):
-            cur, jit, force = m, j2, f2
+            cur, jit, shy = m, j2, s2
             if m < best:
-                best, keep = m, (j2, f2)
-    return schedule(ops, *keep)
+                best, keep = m, (j2, s2)
+    order, start, fin, eng = schedule(*keep)
+    for o, e in zip(ops, eng):
+        o["pick"] = [a for a in o["alts"] if a[0] == e][0]
+    ops[0]["times"] = times(*keep)
+    return order, start, fin
 
 
 _plan = []
@@ -736,7 +936,7 @@ def rank_program(g, core, T, topo):
             total[s] = 16 * len(args)
             done[i] = ((s, total[s]), (s, total[s]))
         elif name == "push":
-            dst = T.cores[(rank - 1 - args[2]) % NR]
+            dst = T.cores[(rank + args[2]) % NR]
             rid, pid, _s = topo.addr(dst)
             sl, sr = fresh(), fresh()
             g.remote_dma(real(args[0]), real(args[1]), T.sem[sr], T.sem[sl], pid, rid, topo.mask(core, dst))

@@ -9,25 +9,27 @@ DUM = B0 + 2 * L
 OFF = L
 CEN = 1920.0
 MAGIC = 12582912.0
-BAR = 131072.0
-NG1, NGD, NBB, NRB, NDB, NCC, LATE = 4, 6, 3, 5, 3, 4, 2
+BAR = 262144.0
+NG1, NGD, NRB, NDB, NCC, LATE = 4, 7, 5, 3, 10, 2
 f32, bf, f16, i32, u16 = "float32", "bfloat16", "float16", "int32", "uint16"
 SB = {
-    "ki": ([B0], i32), "kk": ([OFF + W + 32], f32), "xx": ([W], bf), "dtab": ([B0], i32), "st": ([1024], f32),
-    "rk": ([R, L], f32), "qa": ([R, 32], u16), "of2": ([16, 64], u16), "kw2": ([16, 2, 32], u16),
+    "ki": ([B0], i32), "kk": ([OFF + W + 32], f32), "xx": ([W], bf), "dtab": ([B0 + 2 * L], f32),
+    "rk": ([R, L], f32), "qa": ([R, 32], u16), "of3": ([16, 96], u16), "kw3": ([16, R, 32], u16), "kv16": ([L], f16), "ws": ([8, 144], f16), "m4": ([144], f32),
     "rx0": ([B0], bf), "rx1": ([B0 + L], bf), "rx2": ([B0 + 2 * L], bf),
     "cb": ([2048], f32), "nb": ([R, 1152], bf), "pkv": ([L], f32), "nv": ([R, L], f32), "vv": ([L], f32),
-    "kvr": ([L], u16), "of1": ([R * L], u16), "cu": ([R * L], u16), "cc": ([NCC + 3, 128], f16), "kp": ([L], bf),
-    "g1": ([NG1 + 1, 2 * L], f16), "gh": ([3, 2, L], f16), "gt": ([2, L], bf), "gd": ([NGD + LATE + 1, L, 2], f16),
-    "bb": ([NBB, L, 2], bf), "rb": ([NRB + LATE, L, 2], bf), "db": ([NDB + LATE, L, 2], bf),
-    "dv": ([2, L], f32), "xq": ([L], f32), "kv16": ([L], f16),
-    "sc1": ([L], f32), "sc2": ([L], f32), "uu": ([L], bf), "sd1": ([272], f32), "li": ([2, L], f16),
+    "kvf": ([L], f32), "l67": ([2, 32], f32),
+    "cu": ([R * 16, 32], u16), "cc": ([NCC + 3, 128], f16), "kp": ([L], bf),
+    "g1": ([NG1, 2 * L], f16), "gh": ([3, 2, L], f16), "gd": ([NGD + 2 * LATE, L, 2], f16),
+    "bb": ([2, L], bf), "rb": ([NRB + LATE + 2, L, 2], bf), "db": ([NDB + 2 * LATE, 256, 2], bf),
+    "dv": ([3, 256, 2], f32), "barc": ([32], bf), "sc0": ([128], f32), "sc1": ([L], f32), "sc2": ([L], f32), "uu": ([L], bf), "sd1": ([272], f32), "li": ([2, L], f16),
     "km": ([L], f32), "val": ([L], f32), "xm16": ([L], f16),
-    "ga": ([2048], bf), "ra": ([8, 16, 16], bf), "ai": ([128], f32), "xs": ([128], bf), "du": ([128], u16),
-    "sm": ([16, 32], f32), "si": ([2, 8], i32), "sa": ([2, 96], i32), "su": ([12, 32], u16), "m16": ([32], f16),
-    "pc": ([6], i32), "col": ([48], f32), "ix": ([144], f32), "sxc": ([144], i32), "mi": ([2, 160], i32), "mf": ([160], bf), "sxv": ([R, 32], f16),
-    "we": ([7, 144], bf), "weh": ([2, 144], f16), "ws": ([16, 144], f16), "rr": ([16, 128], f16), "ll": ([16, 128], f16),
-    "mb": ([5, 128], bf), "mh": ([9, 128], f16), "p2f": ([128], f32), "blk": ([128], f32), "bl16": ([128], f16), "mask": ([32], f32),
+    "ga": ([2048], bf), "ra": ([128, 16], bf), "xs": ([128], bf), "du": ([128], u16),
+    "sm": ([22, 32], f32), "si": ([2, 8], i32), "sa": ([2, 96], i32), "su": ([12, 32], u16), "m16": ([32], f16),
+    "pc": ([8], i32), "col": ([48], f32), "ix": ([144], f32), "sxc": ([144], f32), "sxn": ([2, 32], f32),
+    "mi": ([2, 32], i32), "mf": ([32], bf), "sxw": ([R, 32], f32),
+    "ns": ([256], bf), "seg": ([256], bf), "bs": ([256], f16), "srow": ([128], f32), "fl": ([128], f16),
+    "we": ([8, 144], bf), "weh": ([2, 144], f16), "rr": ([16, 128], f16), "ll": ([16, 128], f16),
+    "mb": ([5, 128], bf), "mh": ([8, 128], f16), "blk": ([128], f32), "mask": ([32], f32),
     "kc": ([2, L], bf), "rs0": ([L], bf), "rstk": ([L], bf), "dm0": ([L], bf), "rs1": ([272], bf),
     "ia": ([2, 32], f32), "itc": ([2, 32], f16), "kq": ([128], f16),
     "thi": ([4], i32), "thf": ([4], f32), "wi": ([4], i32), "l8": ([128], f32),
@@ -41,15 +43,16 @@ SHAPES = {n: v[1] for n, v in SCRATCH.items()}
 SHAPES.update({"kin": [128, B0], "xf": [128, B0], "th": [8, R], "w": [128, R], "yk": [128, W], "yx": [128, R * L]})
 WIDE = {n: (2 if v[2] in (bf, f16, u16) else 4) for n, v in SCRATCH.items()}
 
-MODELS = [(0.9, 1.56, 3.8, 1000.0, 500.0, 300.0, 3.0, 250.0, 170.0),
-          (1.15, 2.0, 3.0, 1000.0, 500.0, 300.0, 3.0, 250.0, 170.0),
-          (1.1, 1.15, 5.5, 1000.0, 500.0, 300.0, 3.0, 250.0, 170.0),
-          (0.9, 1.8, 3.8, 1500.0, 700.0, 200.0, 5.0, 350.0, 250.0)]
+MODELS = [(0.9, 1.56, 3.8, 900.0, 400.0, 280.0, 3.5, 260.0, 170.0, 0.52, 100.0, 4000.0),
+          (1.1, 2.0, 3.0, 800.0, 400.0, 300.0, 2.5, 240.0, 160.0, 0.51, 60.0, 2000.0),
+          (1.1, 1.2, 5.5, 1000.0, 500.0, 300.0, 3.0, 300.0, 200.0, 0.55, 100.0, 6000.0),
+          (0.9, 1.3, 2.5, 1300.0, 600.0, 220.0, 4.5, 290.0, 200.0, 0.51, 150.0, 8000.0)]
 DPRE, DPOST = MODELS[0][3:5]
 LAT_X, LAT_S = MODELS[0][7:9]
-SEED, TRIES, SHY, TOL, DEL = 0, 7000, 4000.0, 200.0, 600.0
-KK2 = "G"
+SEED, TRIES, POLISH, SHY, TOL, DEL = 0, 600, 55000, 4000.0, 200.0, 600.0
+KK2 = [(0, 1024, "VA"), (1024, 2048, "VA"), (2048, B0, "VA")]
 LEAD = [0.0, 0.0, 0.0]
+SOON = 15000.0
 S_ = slice
 ALL = slice(None)
 
@@ -102,20 +105,23 @@ def kof(t, j, e):
 
 
 BOTH = (0, 1)
-QUADS = [[(2, 3), (4, 5), (6, 7)], [(0, 1), (4, 5), (6, 7)], [(0, 1), (6, 7), (5,)]]
-DYN = [[(j, BOTH, "") for j in range(2)], [(2, BOTH, "WW"), (3, BOTH, "WW")], [(2, BOTH, "WW"), (3, BOTH, "WW"), (4, (0,), "WM")]]
-LONE = [[], [], [(4, (1,), "")]]
-PIECES = ["11111111", "44114411", "44111411"]
-PIECES = [[int(c) for c in x] for x in PIECES]
+QUADS = [[(0, 1), (2, 3), (4, 5), (6, 7)], [(0, 1), (4, 5), (6, 7)], [(0, 1), (6, 7)]]
+NAMES_PE = [(0, 2), (), ()]
+BATCH = [(0, 1), (1, 2), (2, 4), (4, 6), (6, 8)]
+ASK_V = [(), (), (0,)]
+DYN = [[], [((3, "LW"), (2, "LL"))], [((2, "LL"), (3, "LL")), ((4, "WM"), (5, "MM"))]]
+PIECES = [[1] * 8, [1, 1, 1, 1, 4, 4, 4, 4], [1, 1, 1, 1, 4, 4, 4, 4]]
+KVF = "G"
+HOLD, HALVES, MEAN = True, (1, 1, 1), 256
 
 
 def build(model=None):
     CY, GAM, SIG, DPRE, DPOST, DBW, DROW = (model or MODELS[0])[:7]
-    PCY = CY * 0.51
+    PCY = CY * (model or MODELS[0])[9]
+    ISSUE, FIRST = (tuple(model or MODELS[0]) + (60.0, 0.0))[10:12]
     ops = []
 
     mark = {}
-    lead = [0.0]
 
     def add(alts, reads, writes, lat=0.0, kind="c", extra=None, after=None):
         ops.append({"alts": alts, "r": [region(x) for x in flat(reads)], "w": [region(x) for x in flat(writes)],
@@ -191,8 +197,7 @@ def build(model=None):
 
     def mm(lst, group=None):
         cost = sum(max(64, region(x[2])[3]) * (WIDE[x[2][0]] ** 2 / 4) * PCY for x in lst)
-        add([("P", cost, ("mm", lst, {"group": group}))], [x[1] for x in lst] + [x[2] for x in lst], [x[0] for x in lst], lat=60.0,
-            extra=lead[0] if group and group[0] == "k" else None)
+        add([("P", cost, ("mm", lst, {"group": group}))], [x[1] for x in lst] + [x[2] for x in lst], [x[0] for x in lst], lat=60.0)
 
     def iota(out, pat, base, cm, extra=None):
         kw = {} if SCRATCH[out[0]][2] == i32 else {"allow_small_or_imprecise_dtypes": True}
@@ -201,12 +206,14 @@ def build(model=None):
     def dma(pairs, q="Y", after=None, extra=None):
         by = sum(region(o)[3] * region(o)[4] * WIDE.get(o[0], 2 if o[0] == "yx" else 4) for o, i in pairs)
         rows = sum(max(16, region(o)[4], region(i)[4]) for o, i in pairs)
-        add([(q, 60.0 * len(pairs), ("dma", pairs, {}))], [i for o, i in pairs], [o for o, i in pairs],
+        add([(q, ISSUE * len(pairs), ("dma", pairs, {}))], [i for o, i in pairs], [o for o, i in pairs],
             lat=DPRE + DPOST + by / DBW + rows * DROW, kind="d", after=after, extra=extra)
 
     def push(dst, src, t, after=None):
         by = region(dst)[3] * 128 * WIDE[dst[0]]
-        add([("G", 300.0, ("push", [dst, src, t], {}))], [src], [dst], lat=DPRE + DPOST + by / DBW + 128 * DROW, kind="p", after=after)
+        add([("G", 300.0 + ("push" not in mark) * FIRST, ("push", [dst, src, t], {"group": "push"}))], [src], [dst],
+            lat=DPRE + DPOST + by / DBW + 128 * DROW, kind="p", after=after, extra=None if "push" in mark else SOON)
+        mark["push"] = True
 
     def P(b, *ix):
         return ap("p%d" % b, *(ix if ix else (ALL,)))
@@ -232,13 +239,13 @@ def build(model=None):
     def pc(i):
         return ap("pc", S_(i, i + 1))
 
-    dma([(ap("ki", S_(0, 1152)), ap("kin", S_(0, 1152))), (ap("ki", S_(1152, B0)), ap("kin", S_(1152, B0)))], extra=4e6)
-    dma([(ap("xx", S_(0, B0)), ap("xf", ALL))], extra=3e6)
-    dma([(pap("thi", S_(0, 8), S_(0, R)), ap("th", ALL)), (ap("wi", S_(0, R)), ap("w", ALL))], extra=8e6)
+    for a, b in ((0, 1024), (1024, 2048), (2048, B0)):
+        dma([(ap("ki", S_(a, b)), ap("kin", S_(a, b)))], extra=6e6 - 100.0 * a)
+    dma([(ap("xx", S_(0, B0)), ap("xf", ALL))])
+    dma([(pap("thi", S_(0, 8), S_(0, R)), ap("th", ALL)), (ap("wi", S_(0, R)), ap("w", ALL))])
 
-
-    PM, PG, Q8, PP, C15, N67, DE, DO, H0, H1, H1B, BAR0, BAR1, CCOL, GB, GS, SXW, CHB, P16, TMP = range(20)
-    WF, TH, THR, GS2 = 24, 27, 30, 33
+    PM, PG, Q8, PP, C15, N67, DE, DO, H0, H1, H1B, BAR0, BAR1, CCOL, GB, GS, _a, _b, P16, TMP = range(20)
+    WF, TH, THR, GS2, P64 = 24, 27, 30, 33, 34
     iota(pc(0), [[0, 1]], 0, 1, 1e6)
     iota(ap("ix", ALL), [[1, 144]], 0, 0, 1e6)
     ts(pc(1), pc(0), 15, A.bitwise_and)
@@ -254,35 +261,33 @@ def build(model=None):
     ts(c1(DE), c1(PM), W - CEN, A.add)
     ts(c1(DO), c1(PM), W + 16 - CEN, A.add)
     ts(c1(H0), c1(PM), 7.5, A.is_lt)
-    ts(c1(H1B), c1(PM), 7.5, A.is_gt, BAR, A.mult)
-    ts(c1(BAR0), c1(PM), 6.5, A.is_lt, BAR, A.mult)
-    ts(c1(BAR1), c1(Q8), 6.5, A.is_lt, c1(H1B), A.mult)
+    ts(c1(H1B), c1(PM), 7.5, A.is_gt, c1(C15), A.add)
+    ts(c1(BAR0), c1(Q8), 6.5, A.is_lt, BAR, A.mult)
     ts(c1(CCOL), c1(Q8), 5.5, A.is_lt, 0.5, A.mult)
     ts(c1(TMP + 1), c1(Q8), 6.0, A.not_equal, -2040.0, A.mult)
     ts(c1(GB), mk(15), 6120.0, A.mult, c1(TMP + 1), A.add)
     ts(c1(GS), c1(PM), 14.5, A.is_lt)
-    ts(c1(GS2), c1(PM), 14.5, A.is_lt, mk(6), A.subtract)
-    ts(c1(SXW), c1(Q8), 6.5, A.is_gt, 16.0, A.mult)
-    ts(c1(TMP + 2), c1(PM), 3.5, A.is_lt, mk(0), A.subtract)
-    ts(c1(CHB), c1(TMP + 2), mk(8), A.add, CEN, A.mult)
-    ts(c1(P16), c1(PM), 16.0, A.mult)
+    ts(c1(GS2), c1(PM), 5.5, A.is_lt)
+    ts(c1(P64), c1(PM), 64.0, A.mult)
     copy(ap("col", S_(WF, WF + R)), ap("wi", S_(0, R)))
-    E16, EM32, EBAR0, EBAR1, EW = range(5)
-    for i, c in [(E16, 16.0), (EM32, -32.0), (EBAR0, c1(BAR0)), (EBAR1, c1(BAR1)),
+    E16, EM32, EBAR, EMX, EY, EW = range(6)
+    ts(ap("we", EBAR, ALL), ap("ix", ALL), c1(H1B), A.is_equal, c1(BAR0), A.mult)
+    for i, c in [(E16, 16.0), (EM32, -32.0), (EMX, 4096.0), (EY, -2048.0),
                  (EW, c1(WF)), (EW + 1, c1(WF + 1)), (EW + 2, c1(WF + 2))]:
         ts(ap("we", i, ALL), ap("ix", ALL), c1(C15), A.is_equal, c, A.mult)
     ts(ap("weh", 0, ALL), ap("ix", ALL), c1(C15), A.is_equal)
-    lin(ap("weh", 1, ALL), ap("weh", 0, ALL), scale=c1(SXW))
-    for k in range(16):
-        lin(ap("ws", k, ALL), ap("weh", 0, ALL), scale=mk(k))
-    iota(ap("blk", ALL), [[1, 8], [0, 16]], 0, 0, 1e6)
-    ts(ap("bl16", ALL), ap("blk", ALL), c1(PG), A.is_equal, 1.0 / 64, A.mult)
-    for k in range(16):
-        lin(ap("rr", k, ALL), ap("bl16", ALL), scale=mk(k))
+    memset(ap("ws", ALL), 0.0)
+    one = ap("ws", ALL, S_(15, 144, 16))
+    memset(one, 1.0)
+    add([("G", 170 + 2 * CY * 72, ("affine_select", [one, one, [[-1, 8], [-16, 9]], A.is_equal, 0.0, 0, 1], {}))], [one], [one], extra=2e4)
+    lin(ap("weh", 1, ALL), ap("ws", 7, ALL), scale=16.0)
+    memset(ap("rr", ALL), 1.0 / 64)
+    add([("G", 170 + 2 * CY * 2048, ("affine_select", [ap("rr", ALL), ap("rr", ALL), [[-1, 16], [-16, 8], [0, 16]], A.is_equal, 0.0, 0, 1], {}))],
+        [ap("rr", ALL)], [ap("rr", ALL)])
     add([("G", 170 + 2 * CY * 2048, ("affine_select", [ap("ll", ALL), ap("rr", ALL), [[0, 16], [-1, 128]], A.not_equal, -1.0 / 64, 0, 1], {}))],
         [ap("rr", ALL)], [ap("ll", ALL)])
     IB, NIB, HIB, ZB = [ap("mb", i, ALL) for i in range(4)]
-    IH, HIH, NI64, I16H, C0, C1, P1, W7, C1S = [ap("mh", i, ALL) for i in range(9)]
+    IH, HIH, NI64, I16H, C0, R7, W7, C1S = [ap("mh", i, ALL) for i in range(8)]
     ix128 = ap("ix", S_(0, 128))
     ts(IB, ix128, c1(PP), A.is_equal)
     ts(IH, ix128, c1(PP), A.is_equal)
@@ -290,74 +295,78 @@ def build(model=None):
     ts(C1S, ix128, c1(TMP + 3), A.is_equal, c1(H0), A.mult)
     for m, c in [(NIB, -1.0), (HIB, 0.5), (ZB, 0.0)]:
         lin(m, IB, scale=c)
-    for m, c in [(HIH, 0.5), (NI64, -1.0 / 64), (I16H, 16.0), (C0, c1(H0)), (P1, c1(CCOL))]:
+    for m, c in [(HIH, 0.5), (NI64, -1.0 / 64), (I16H, 16.0), (C0, c1(H0)), (R7, c1(CCOL))]:
         lin(m, IH, scale=c)
-    lin(W7, ix128, scale=0.0, bias=mk(7))
-    mm([(P(3, S_(144, 272)), IH, C0), (P(3, S_(144, 272)), wsl("weh", 0, 15), P1)])
+    mm([(P(3, S_(144, 272)), IH, C0), (P(3, S_(144, 272)), wsl("weh", 0, 15), R7)])
     lin(C0, P(3, S_(144, 272)))
-    mm([(P(3, S_(256, 384)), IH, wsl("ws", a, b)) for a, b in ((0, 2), (1, 3), (7, 8))])
-    lin(P1, P(3, S_(256, 384)))
-    mm([(P(3, S_(384, 512)), IH, wsl("ws", a, b)) for a, b in [(0, 4), (1, 5)] + [(k, k) for k in range(9, 16)]])
-    lin(ap("p2f", ALL), P(3, S_(384, 512)))
+    lin(W7, ix128, scale=0.0, bias=mk(7))
+    lin(R7, ap("rr", 7, ALL), scale=-4096.0)
+    memset(ap("barc", ALL), BAR)
     iota(ap("kc", 0, ALL), [[0, 32], [1, 2], [2, 8]], 0, 0)
     iota(ap("uu", ALL), [[0, 32], [1, 16]], 0, 0)
     iota(ap("kc", 1, ALL), [[0, 32], [1, 2], [2, 8]], 1, 0)
     memset(ap("kc", 1, S_(15, L, 16)), 0.0)
-    ts(ap("rs0", ALL), ap("uu", ALL), 0.0, A.is_equal)
-    ts(ap("rstk", ALL), ap("uu", ALL), 0.0, A.is_equal, 16777216.0, A.mult)
     ts(ap("dm0", ALL), ap("uu", ALL), c1(PM), A.is_gt, 128.0, A.mult)
-    ts(ap("kp", ALL), ap("uu", ALL), -4096.0, A.mult, 65536.0, A.add)
-    memset(ap("rs1", ALL), 0.0)
-    memset(ap("rs1", S_(0, 272, 17)), 1.0)
+    iota(ap("kp", ALL), [[0, 32], [-4096, 16]], 65536, 0)
+    for n, w_, step, c in (("rs0", L, 16, 1), ("rstk", L, 16, (1 << 24) - 1), ("rs1", 272, 17, 1)):
+        iota(ap(n, ALL), [[0, w_]], 0, 0)
+        iota(ap(n, S_(0, w_, step)), [[0, w_ // step]], c, 0)
     for t in range(R):
         iota(ap("nv", t, ALL), [[1, L]], B0 + L * t, 0)
-    iota(ap("st", S_(512, 640)), [[0, 128]], 0, 0)
+    iota(ap("seg", ALL), [[0, 8], [1, 32]], 0, 0)
+    iota(ap("ns", ALL), [[4096, 2], [256, 4], [0, 32]], 0, 0)
+    ts(pc(6), pc(1), 3, A.bitwise_and)
+    ts(c1(P64 + 1), pc(6), 1008.0, A.mult, 32.0, A.add)
+    ts(c1(P64 + 2), c1(PM), 16.0, A.mult, c1(P64 + 1), A.add)
+    ts(ap("ns", ALL), ap("ns", ALL), c1(P64 + 2), A.add)
+    iota(ap("srow", ALL), [[64, 2], [1, 16], [16, 4]], 511, 0)
+    lin(ap("srow", ALL), ap("srow", ALL), scale=1.0 / 512)
     iota(ap("kk", S_(0, OFF)), [[0, OFF]], 0, 0)
     iota(ap("ia", 0, ALL), [[16, 32]], 0, 0)
     ts(ap("itc", 0, ALL), ap("ia", 0, ALL), c1(PM), A.add, 1.0 / 512, A.mult)
     ts(ap("itc", 1, ALL), ap("ia", 0, ALL), 0.0, A.mult, 511.0, A.add)
-    ts(ap("ia", 1, ALL), ap("ia", 0, ALL), c1(PM), A.add, -OFF - CEN, A.add)
-    iota(ap("blk", ALL), [[256, 8], [1, 16]], 0, 0)
-    ts(ap("kq", ALL), ap("blk", ALL), c1(P16), A.add)
+    ts(ap("ia", 1, ALL), ap("ia", 0, ALL), c1(PM), A.add, -float(OFF), A.add)
+    iota(ap("blk", ALL), [[1024, 2], [1, 64]], 0, 0)
+    lin(ap("kq", ALL), ap("blk", ALL), bias=c1(P64))
     p8 = S_(0, 8)
     iota(pap("l8", p8, ALL), [[1, 8], [0, 16]], 0, -1)
     ts(pap("l8", p8, ALL), pap("l8", p8, ALL), 0.0, A.is_equal)
     copy(pap("thf", p8, S_(0, R)), pap("thi", p8, S_(0, R)))
     mm([(P(1, S_(300, 300 + R)), pap("l8", p8, ALL), pap("thf", p8, S_(0, R)))])
-    ts(ap("col", S_(TH, TH + R)), P(1, S_(300, 300 + R)), 16.0, A.mult, -0.5, A.add)
+    ts(c1(TH), P(1, S_(300, 301)), 16.0, A.mult, -0.5, A.add)
+    ts(ap("col", S_(TH + 1, TH + R)), P(1, S_(301, 300 + R)), 16.0, A.mult, -8.5, A.add)
 
-    def o1(t, j, e=None):
-        if t and kof(t, j, e) not in (6, 7):
-            return ap("of2", kof(t, j, e), S_(32 * t - 32, 32 * t))
-        c = t * L + 64 * j
-        return ap("of1", S_(c, c + 64)) if e is None else ap("of1", S_(c + 32 * e, c + 32 * e + 32))
+    def o1(t, j, e):
+        return ap("of3", kof(t, j, e), S_(32 * t, 32 * t + 32))
 
     def cu(t, j, e):
-        c = t * L + 64 * j + 32 * e
-        return ap("cu", S_(c, c + 32))
+        return ap("cu", 16 * t + 2 * j + e, ALL)
 
-    def lists(t):
-        if t == 0:
-            copy(ap("kvr", S_(0, L, 2)), ap("ki", S_(0, 1024, 4)))
-            copy(ap("kvr", S_(1, L, 2)), ap("ki", S_(1024, 2048, 4)))
-            mark["kvr"] = len(ops) - 1
-            for q in QUADS[0]:
-                for j in q:
-                    dma([(o1(0, j, e), pap("kvr", row(kof(0, j, e)), ALL)) for e in BOTH])
-        if t == 1:
-            for u in (1, 2):
-                for h in BOTH:
-                    copy(ap("kw2", ALL, u - 1, S_(h, 32, 2)), ap("ki", S_(1024 * h + u, 1024 * h + 1024, 4)))
-            for ks in ((1, 2), (3, 4), (9, 10), (11, 12), (13, 14), (15, 0), (5, 8)):
-                dma([(ap("of2", k, ALL), pap("kw2", row(k), ALL, ALL, ALL)) for k in ks])
+    def lists():
+        for h in BOTH:
+            lin(ap("kv16", S_(h, L, 2)), ap("ki", S_(1024 * h, 1024 * h + 1024, 4)), bias=-CEN)
+        for i, (a, b) in enumerate(BATCH):
+            for k in range(a, b):
+                o = P(4 + i % 2, S_(32 * (k - a), 32 * (k - a) + 32))
+                mm([(o, wsl("ws", k, r), ap("kv16", S_(32 * r, 32 * r + 32))) for r in range(16)])
+            ts(ap("of3", S_(a, b), S_(0, 32)), P(4 + i % 2, S_(0, 32 * (b - a))), CEN, A.add)
+        for u in range(R):
+            for h in BOTH:
+                copy(ap("kw3", ALL, u, S_(h, 32, 2)), ap("ki", S_(1024 * h + u, 1024 * h + 1024, 4)))
+        for k in range(16):
+            a, b = 1 if k < BATCH[-1][1] else 0, 1 if k in (6, 7) else R
+            if a < b:
+                dma([(ap("of3", k, S_(32 * a, 32 * b)), pap("kw3", row(k), ALL, S_(a, b), ALL))])
 
-    lists(0)
-    lin(kk(0, 1152), ap("ki", S_(0, 1152)), eng="G")
-    lin(kk(1152, B0), ap("ki", S_(1152, B0)), eng=KK2)
-    iota(ap("dtab", ALL), [[0, B0 // 4], [1, 4]], 0, 0)
-    dma([(pap("dtab", row(j), ALL), pap("kin", row(j), ALL)) for j in range(6)], after="kvr")
+    lists()
+    for a, b, eng in KK2:
+        lin(kk(a, b), ap("ki", S_(a, b)), eng="G")
+        lin(ap("dtab", S_(a, b)), ap("ki", S_(a, b)), scale=c1(GS2), eng=eng)
+    iota(ap("m4", ALL), [[0, 36], [1, 4]], 0, 0)
+    iota(ap("dtab", S_(B0, B0 + 2 * L)), [[0, L // 2], [1, 4]], 0, 0)
+    dma([(pap("dtab", row(6), S_(0, B0)), ap("m4", ALL))])
     mm([(P(3, S_(0, 144)), wsl("we", E16, r), ap("xx", S_(144 * r, 144 * r + 144))) for r in range(16)])
-    lin(ap("sxc", ALL), P(3, S_(0, 144)), scale=1.0 / 16, eng="V")
+    lin(ap("sxc", ALL), P(3, S_(0, 144)), scale=1.0 / 16)
     dma([(pap("dtab", row(7), S_(0, B0)), ap("sxc", ALL))])
     for t in range(R):
         lin(xv(t), ap("xx", vcols(t)), eng="G" if t else "VA")
@@ -365,7 +374,8 @@ def build(model=None):
         mm([(P(1, S_(32 * t, 32 * t + 32)), wsl("we", EW + t, r), ap("nb", t, S_(r, L, 16))) for r in range(16)])
     mm([(P(1, S_(128, 224)), wsl("we", E16, r), ap("nb", ALL, S_(r, L, 16))) for r in range(16)])
     copy(ap("sa", 0, ALL), P(1, S_(0, 96)))
-    ts(ap("sxv", ALL), P(1, S_(128, 224)), 1.0 / 16, A.mult, -2040.0, A.add)
+    ts(ap("sxw", 0, ALL), P(1, S_(128, 160)), 32640.0, A.add)
+    ts(ap("sxw", S_(1, R), ALL), P(1, S_(160, 224)), 32632.0, A.add)
     ts(ap("sa", 1, ALL), ap("sa", 0, ALL), 2047, A.bitwise_and)
     copy(ap("su", S_(0, R), ALL), ap("sa", 1, ALL))
     for t in range(R):
@@ -398,147 +408,147 @@ def build(model=None):
         prs, nums = [], []
         for i, j in enumerate(js):
             g = nxt("g1", NG1, 1 * late)
-            if t:
-                for e in es:
-                    lin(ap("g1", g, S_(L * e, L * e + L)), ind(kk(0, B0 + L * t) if late else ap("ki", ALL), o1(t, j, e)), bias=-CEN)
-            else:
-                lin(ap("g1", g, ALL), ind(ap("ki", ALL), o1(t, j)), bias=-CEN)
+            for e in es:
+                lin(ap("g1", g, S_(L * e, L * e + L)), ind(ap("ki", ALL), o1(t, j, e)), bias=-CEN)
+                ops[-1]["extra"] = LEAD[t] * (PIECES[t][j] > 1)
             pj = [(ap("cc", s, S_(64 * i + 32 * e, 64 * i + 32 * e + 32)), pap("g1", row((kof(t, j, e) + t) % 16), g, S_(L * e, L * e + L))) for e in es]
             dma(pj)
             nums += [(pos(t, 2, j, (e,)), IH, pj[n][0]) for n, e in enumerate(es)]
         mark[("late" if late else "names", t)] = len(ops) - 1
-        c, n = t * L + 64 * js[0] + 32 * es[0], 32 * len(es) * len(js)
-        ts(ap("cu", S_(c, c + n)), ap("cc", s, S_(32 * es[0], 32 * es[0] + n)), CEN, A.add)
-        mm(nums, ("c", t))
+        c, n = 16 * t + 2 * js[0] + es[0], 32 * len(es) * len(js)
+        ts(ap("cu", S_(c, c + n // 32), ALL), ap("cc", s, S_(32 * es[0], 32 * es[0] + n)), CEN, A.add)
+        numbers(t, nums)
 
-    def list_pe(t, two, b):
-        for i, (j, e) in enumerate(two):
-            mm([(P(b, S_(32 * i, 32 * i + 32)), wsl("ws", kof(t, j, e), r), ap("kv16", S_(r, L, 16))) for r in range(16)])
-        c = t * L + 64 * two[0][0] + 32 * two[0][1]
-        ts(ap("of1", S_(c, c + 64)), P(b, S_(0, 64)), CEN, A.add)
-
-    def names_pe(t, two, b):
-        s = nxt("gh", 3)
-        for i, (j, e) in enumerate(two):
+    def names_pe(t, j, es, late=True):
+        s, b, n = nxt("gh", 3), 7 if t == 1 else 6 + j % 2, 32 * len(es)
+        for i, e in enumerate(es):
             kr = (kof(t, j, e) + t) % 16
-            lin(ap("gh", s, i, ALL), ind(kk(0, B0 + L * t) if t else ap("ki", ALL), o1(t, j, e)), scale=mk(kr), bias=mk(16 + kr))
-        mm([(P(b, S_(0, 64)), wsl("weh", 0, r), ap("gh", s, ALL, S_(r, L, 16))) for r in range(16)])
-        c = t * L + 64 * two[0][0] + 32 * two[0][1]
-        ts(ap("cu", S_(c, c + 64)), P(b, S_(0, 64)), CEN, A.add)
-        s = nxt("cc", NCC, 3)
-        lin(ap("cc", s, S_(0, 64)), P(b, S_(0, 64)))
-        mm([(pos(t, 2, j, (e,)), IH, ap("cc", s, S_(32 * i, 32 * i + 32))) for i, (j, e) in enumerate(two)], ("c", t))
+            lin(ap("gh", s, i, ALL), ind(kk(0, B0 + L * t) if late else ap("ki", ALL), o1(t, j, e)), scale=mk(kr), bias=mk(16 + kr))
+        mm([(P(b, S_(0, n)), wsl("weh", 0, r), ap("gh", s, S_(0, len(es)), S_(32 * r, 32 * r + 32))) for r in range(16)])
+        c = 16 * t + 2 * j + es[0]
+        ts(ap("cu", S_(c, c + len(es)), ALL), P(b, S_(0, n)), CEN, A.add)
+        mark[("late" if late else "names", t)] = len(ops) - 1
+        s = nxt("cc", NCC, 3 * late)
+        lin(ap("cc", s, S_(0, n)), P(b, S_(0, n)))
+        nums = []
+        for i, e in enumerate(es):
+            c = ap("cc", s, S_(32 * i, 32 * i + 32))
+            if t and kof(t, j, e) == 8:
+                mark[("c8", t)] = c
+            else:
+                nums.append((pos(t, 2, j, (e,)), IH, c))
+        numbers(t, nums)
 
-    def names_late(t):
-        late = [(j, e) for j, es, _m in DYN[t] for e in es]
-        for j, es, _m in DYN[t]:
-            es = tuple(e for e in es if kof(t, j, e) not in (6, 7))
-            if es:
-                names_static(t, (j,), es, True)
-        names_pe(t, sorted(x for x in late if kof(t, *x) in (6, 7)), 6)
+    def halves(t, kinds):
+        return [(j, tuple(e for e in BOTH if m[e] in kinds)) for q in DYN[t] for j, m in q if set(m) & set(kinds)]
 
     def terms(t, j, es, lst):
         ee = S_(es[0], es[-1] + 1)
         for w_, i, n, s in lst:
             mm([(pos(t, 0, j, es), wsl(w_, i, r), ap(n, s, S_(r, L, 16), ee)) for r in range(16)], ("k", t))
 
-    def by_scalar(t, j, e, rs, wd):
-        s, b = nxt("gt", 2), 4 + nxt("pb", 2)
-        lin(ap("gt", s, ALL), ind(ap("xx", S_(0, wd)), cu(t, j, e)))
-        mm([(P(b), NIB, xv(t)), (P(b), IB, ap("gt", s, ALL))])
-        act(ap("rb", rs, ALL, e), P(b), F.Abs)
+    place = {}
 
-    def score_quad(t, js):
-        gs = []
-        lead[0] = LEAD[t] * (7 - js[-1])
-        for j in js:
-            rs, g = nxt("rb", NRB), nxt("gd", NGD)
-            gs.append(g)
-            for e in BOTH:
-                lin(ap("gd", g, ALL, e), ind(ap("dtab", S_(0, B0)), cu(t, j, e)), scale=c1(GS), bias=c1(GB))
-            if PIECES[t][j] == 0:
+    def score_quad(t, js, parts):
+        late = not isinstance(js[0], int)
+        quad = js if late else [(j, "MM") for j in js]
+        wd = {"M": B0, "L": B0 + L * t}
+        if parts in "fpF":
+            for j, m in quad:
+                if parts != "F" and (PIECES[t][j] > 1 and HOLD) != (parts == "p"):
+                    continue
+                if (t, j) not in place:
+                    place[(t, j)] = nxt("rb", NRB, 2 * LATE * late)
+                rs = place[(t, j)]
                 for e in BOTH:
-                    by_scalar(t, j, e, rs, B0)
-                terms(t, j, BOTH, [("we", E16, "rb", rs)])
+                    if m[e] == ("L" if parts == "F" else "M"):
+                        for ls, off in pieces(t, j, e, PIECES[t][j]):
+                            tt(ap("rb", rs, ls, e), ind(ap("xx", S_(0, wd[m[e]])), off), ap("nb", t, ls), A.min)
+                            if parts == "p":
+                                ops[-1]["after"].append(mark["named"])
+                if ("L" in m) == ("F" in parts):
+                    terms(t, j, tuple(e for e in BOTH if m[e] != "W"), [("we", EM32, "rb", rs)])
+            return
+        for j, m in quad:
+            es = tuple(e for e in BOTH if (m[e] == "M") == (parts == "b"))
+            if not es:
                 continue
-            for e in BOTH:
-                n = PIECES[t][j]
-                for q in range(n):
-                    c = t * L + 64 * j + 32 * e + 32 // n * q
-                    ls = S_(L // n * q, L // n * (q + 1))
-                    tt(ap("rb", rs, ls, e), ind(ap("xx", S_(0, B0)), ap("cu", S_(c, c + 32 // n))), ap("nb", t, ls), A.min)
-            terms(t, j, BOTH, [("we", EM32, "rb", rs), ("weh", 1, "gd", g)])
-            mm([(pos(t, 0, j, (e,)), I16H, ap("sxv", t, ALL)) for e in BOTH], ("k", t))
-        blood(t, js, gs, 0)
-        lead[0] = 0.0
+            if (t, j, "b") not in place:
+                place[(t, j, "b")] = nxt("gd", NGD, 2 * LATE * late), nxt("db", NDB, 2 * LATE * late)
+            g, ds = place[(t, j, "b")]
+            for e in es:
+                if m[e] == "W":
+                    lin(ap("gd", g, ALL, e), ind(kk(0, B0 + L * t), cu(t, j, e)), scale=c1(GS2), bias=c1(GB))
+                    mark[("d8", t)] = (j, e, ds)
+                else:
+                    lin(ap("gd", g, ALL, e), ind(ap("dtab", S_(0, wd[m[e]])), cu(t, j, e)), scale=c1(GS), bias=c1(GB))
+            b, ee, w_ = 4 + nxt("pb", 2), S_(es[0], es[-1] + 1), 256 * len(es)
+            mm([(P(b, S_(0, w_)), c, ap("gd", g, S_(h, L, 2), ee)) for h, c in enumerate((C0, C1S))])
+            n = HALVES[t] if parts == "b" and len(es) == 2 else 1
+            for q in range(n):
+                ls = S_(256 // n * q, 256 // n * (q + 1))
+                tt(ap("db", ds, ls, ee), P(b, S_(w_ // n * q, w_ // n * (q + 1))), ap("dv", t % 2, ls, ee), A.is_equal)
+            es = tuple(e for e in es if m[e] != "W")
+            if es:
+                terms(t, j, es, [("weh", 1, "gd", g)])
+                mm(barred(pos(t, 0, j, es), ds, es), ("k", t))
 
-    def blood(t, js, gs, late):
-        ds = nxt("db", NDB, late)
-        two = [(ap("gd", gs[0], ALL, q), ap("gd", gs[1], ALL, q)) for q in BOTH] if len(js) == 2 else [(ap("gd", gs[0], ALL, 0), ap("gd", gs[0], ALL, 1))]
-        for q, (g0, g1) in enumerate(two):
-            b = 4 + nxt("pb", 2)
-            mm([(P(b), C0, g0), (P(b), C1S, g1)])
-            tt(ap("db", ds, ALL, q), P(b), ap("dv", t % 2, ALL), A.is_equal)
-        if len(js) == 2:
-            terms(t, js[0], BOTH, [("we", EBAR0, "db", ds)])
-            terms(t, js[1], BOTH, [("we", EBAR1, "db", ds)])
+    def barred(o, ds, es):
+        return [(o, wsl("we", EBAR, 2 * r), ap("db", ds, S_(r, 256, 8), S_(es[0], es[-1] + 1))) for r in range(8)]
+
+    def pieces(t, j, e, n):
+        return [(S_(L // n * q, L // n * (q + 1)), ap("cu", 16 * t + 2 * j + e, S_(32 // n * q, 32 // n * (q + 1)))) for q in range(n)]
+
+    def least(t):
+        kb, cb_ = t % 2, 2 + t % 2
+        ends = S_(15, L, 16)
+        scan(ap("sc1", ALL), ap("rstk", ALL), P(kb), A.add, A.min)
+        mark["named"] = len(ops) - 1
+        tt(ap("uu", ALL), P(kb), ap("sc1", ALL), A.not_equal)
+        scan(ap("sc2", ALL), ap("uu", ALL), P(cb_), A.mult, A.max)
+        tt(sm(13), ap("sc1", ends), ap("sxw", t, ALL), A.add)
+        ts(sm(3), ap("sc2", ends), MAGIC * 4096, A.add, -MAGIC * 4096, A.add)
+        ts(sm(0), sm(13), 100000.0, A.is_gt, 4096.0, A.mult)
+        tt(sm(15), ap("sc2", ends), sm(3), A.subtract)
+        tt(sm(14) if t else ap("m16", ALL), sm(15), sm(0), A.add)
+        if t:
+            j, e, ds = mark[("d8", t)]
+            ts(sm(3), sm(13), 100000.0, A.min)
+            tt(sm(16), mark[("c8", t)], sm(14), A.subtract)
+            copy(ap("mi", 0, ALL), cu(t, j, e))
+            ts(ap("mi", 1, ALL), ap("mi", 0, ALL), 3, A.bitwise_and)
+            ts(ap("mf", ALL), ap("mi", 1, ALL), float(t), A.is_equal, BAR, A.mult)
+
+    def score_asked(t):
+        j, e, ds = mark[("d8", t)]
+        o = P(2 + (t - 1) % 2, S_(0, 32))
+        mm([(o, IB, ap("mf", ALL))] + barred(o, ds, (e,)), ("x", t))
+        tt(ap("bb", 0, ALL), ind(ap("xx", S_(0, B0 + L * t)), cu(t, j, e)), xv(t), A.subtract)
+        ts(ap("bb", 1, ALL), ap("bb", 0, ALL), 0.0, A.min)
+        for i, w_ in enumerate((E16, EM32)):
+            mm([(o, wsl("we", w_, r), ap("bb", i, S_(r, L, 16))) for r in range(16)], ("x", t))
+        tt(sm(17), o, sm(3), A.is_lt)
+        tt(sm(19), o, sm(13), A.min)
+        tt(sm(18), sm(17), sm(16), A.mult)
+        tt(ap("m16", ALL), sm(14), sm(18), A.add)
+
+    def opens(t, which):
+        if which == "k":
+            mm([(P(t % 2), IB, ap("kc", t % 2, ALL))] + [(pos(t, 0, j, es), IB, ap("barc", ALL)) for j, es in halves(t, "W")], ("k", t))
         else:
-            for e in BOTH:
-                mm([(pos(t, 0, js[0], (e,)), wsl("we", EBAR0 + e, r), ap("db", ds, S_(r, L, 16), 0)) for r in range(16)], ("k", t))
+            mm([(P(2 + t % 2), IB, ap("kp", ALL))], ("c", t))
+            mark[("open", t)] = True
+            numbers(t, [])
 
-    def score_late(t):
-        gs = {}
-        for part in (DYN[t][:2], DYN[t][2:]):
-            for j, es, mode in part:
-                gs[j] = nxt("gd", NGD, LATE + 1)
-                for e in BOTH:
-                    if mode[e] == "M":
-                        lin(ap("gd", gs[j], ALL, e), ind(ap("dtab", ALL), cu(t, j, e)), scale=c1(GS), bias=c1(GB))
-                    else:
-                        lin(ap("gd", gs[j], ALL, e), ind(kk(0, B0 + L * t), cu(t, j, e)), scale=c1(GS2), bias=c1(GB))
-            if part:
-                blood(t, [x[0] for x in part], [gs[x[0]] for x in part], LATE)
-        late = sorted((j, e) for j, es, _m in DYN[t] for e in es)
-        c, n = t * L + 64 * late[0][0], 32 * len(late)
-        copy(ap("mi", 0, S_(0, n)), ap("cu", S_(c, c + n)))
-        ts(ap("mi", 1, S_(0, n)), ap("mi", 0, S_(0, n)), 3, A.bitwise_and)
-        ts(ap("mf", S_(0, n)), ap("mi", 1, S_(0, n)), float(t), A.is_equal, BAR, A.mult)
-        mm([(pos(t, 0, j, (e,)), IB, ap("mf", S_(32 * i, 32 * i + 32))) for i, (j, e) in enumerate(late)], ("k", t))
-        for j, es, mode in DYN[t]:
-            score(t, j, mode, gs[j])
+    held = [[], [], []]
 
-    def score(t, j, mode, g):
-        rs = nxt("rb", NRB, LATE)
-        wd = [B0 if m == "M" else B0 + L * t for m in mode[:2]]
-        for es in ([BOTH] if mode[0] == mode[1] else [(0,), (1,)]):
-            m = mode[es[0]]
-            xw = ap("xx", S_(0, wd[es[0]]))
-            ee = S_(es[0], es[-1] + 1)
-            if m == "A":
-                for e in es:
-                    by_scalar(t, j, e, rs, wd[e])
-                terms(t, j, es, [("we", E16, "rb", rs)])
-            elif m == "W":
-                bs = nxt("bb", NBB)
-                for e in es:
-                    tt(ap("bb", bs, ALL, e), ind(xw, cu(t, j, e)), xv(t), A.subtract)
-                    act(ap("rb", rs, ALL, e), ap("bb", bs, ALL, e), F.Abs)
-                terms(t, j, es, [("we", E16, "rb", rs)])
-            elif m == "V":
-                bs = nxt("bb", NBB)
-                for e in es:
-                    tt(ap("bb", bs, ALL, e), ind(xw, cu(t, j, e)), xv(t), A.subtract)
-                ts(ap("rb", rs, ALL, ee), ap("bb", bs, ALL, ee), 0.0, A.min)
-                terms(t, j, es, [("we", E16, "bb", bs), ("we", EM32, "rb", rs)])
-            else:
-                for e in es:
-                    tt(ap("rb", rs, ALL, e), ind(xw, cu(t, j, e)), xv(t), A.min)
-                terms(t, j, es, [("we", EM32, "rb", rs), ("weh", 1, "gd", g)])
-                mm([(pos(t, 0, j, (e,)), I16H, ap("sxv", t, ALL)) for e in es], ("k", t))
-
-    def opens(t):
-        mm([(P(t % 2), IB, ap("kc", t % 2, ALL))], ("k", t))
-        mm([(P(2 + t % 2), IB, ap("kp", ALL))], ("c", t))
+    def numbers(t, nums):
+        held[t].append(nums)
+        if ("open", t) in mark:
+            for x in held[t]:
+                if x:
+                    mm(x, ("c", t))
+            del held[t][:]
 
     def sm(i, *ix):
         return ap("sm", i, *(ix if ix else (ALL,)))
@@ -552,38 +562,35 @@ def build(model=None):
     def prepare(t):
         src = kk(t, 2048, 4)
         if t:
-            lin(ap("kv16", ALL), src, bias=-CEN)
-            list_pe(t, sorted((j, e) for j, es, _m in DYN[t] for e in es if kof(t, j, e) in (6, 7)), 7)
+            for h in BOTH:
+                lin(ap("kvf", S_(h, L, 2)), kk(1024 * h + t, 1024 * h + 1024, 4), eng=KVF)
+            dma([(ap("l67", i, ALL), pap("kvf", row(6 + i), ALL)) for i in BOTH])
+            copy(ap("of3", S_(6, 8), S_(32 * t, 32 * t + 32)), ap("l67", ALL, ALL))
         for c in (KV, WEDV, ASKV):
             lin(ap("cb", c), src, eng="G")
         iota(ap("vv", ALL), [[4, L]], t, 0)
         dma([(pap("kk", row(7), S_(0, OFF)), pap("nv", row(7), t, ALL)), (pap("kk", row(6), S_(0, OFF)), pap("vv", row(6), ALL))])
         dma([(pap("cb", row(7), WEDV), pap("nv", row(7), t, ALL)), (pap("cb", row(9 + t), ASKV), pap("nv", row(7), t, ALL))])
+        dma([(pap("cb", row(0), CHILD), pap("vv", row(0), ALL))] + [(pap("cb", row(j), CHILD), pap("nv", row(j), t, ALL)) for j in (6, 7)] +
+            [(pap("cb", row(b), CHILD), pap("cb", row(a), KV)) for a, b in ((0, 2), (1, 3), (7, 8))])
 
     def answer(t):
-        lin(ap("pkv", ALL), ind(kk(0, 2048) if t else ap("ki", S_(0, 2048)), ap("qa", t, ALL)), scale=1024.0)
+        lin(ap("pkv", ALL), ind(kk(0, 2048) if t else ap("ki", S_(0, 2048)), ap("qa", t, ALL)))
         push(ap("rk", t, ALL), ap("pkv", ALL), -1 - t)
 
     def tail(t):
         n0 = B0 + L * t
         thr = c1(TH) if t == 0 else c1(THR + t)
         ends = S_(15, L, 16)
-        kb, cb_ = t % 2, 2 + t % 2
-        lin(ap("xq", ALL), xv(t), eng="G")
-        scan(ap("sc1", ALL), ap("rstk", ALL), P(kb), A.add, A.min)
-        tt(ap("uu", ALL), P(kb), ap("sc1", ALL), A.not_equal)
-        scan(ap("sc2", ALL), ap("uu", ALL), P(cb_), A.mult, A.max)
-        ts(sm(0), ap("sc1", ends), 100000.0, A.is_gt, 4096.0, A.mult)
-        ts(sm(1), ap("sc1", ends), thr, A.subtract, 8192.0, A.mult)
+        kb, cb_ = t % 2 if t else 6, 2 + t % 2
+        key = sm(19 if t else 13)
+        ts(sm(1), key, thr, A.subtract, 8192.0, A.mult)
         tt(sm(2), sm(1), ap("ia", 1, ALL), A.max)
-        ts(sm(3), ap("sc2", ends), MAGIC * 4096, A.add, -MAGIC * 4096, A.add)
-        M = sm(15)
-        tt(M, ap("sc2", ends), sm(3), A.subtract)
         m16 = ap("m16", ALL)
-        tt(m16, M, sm(0), A.add)
-        ts(su(MU), M, CEN, A.add)
-        tt(sm(4), M, sm(2), A.min)
-        ts(su(I1), sm(4), OFF + CEN, A.add)
+        ts(su(MU), m16, n0 - 1 - CEN, A.min, CEN, A.add)
+        ts(sm(20), m16, n0 - 1 - CEN, A.min, CEN, A.add)
+        tt(sm(4), sm(20), sm(2), A.min)
+        ts(su(I1), sm(4), float(OFF), A.add)
         mm([(P(6), IB, ap("dm0", ALL))], ("d0", t))
         mm([(P(6, S_(r + 1, L, 16)), ap("ll", r, ALL), m16) for r in range(15)], ("d0", t))
         mm([(P(7, S_(0, 272, 17)), ZB, ap("rs1", S_(0, 16)))], ("d1", t))
@@ -594,13 +601,16 @@ def build(model=None):
         lin(ap("xm16", ALL), ind(ap("xx", S_(0, n0)), su(MU)), bias=-0.5)
         scan(ap("sc2", ALL), P(6), ap("rs0", ALL), A.mult, A.add)
         scan(ap("sd1", ALL), P(7, S_(0, 272)), ap("rs1", ALL), A.mult, A.add)
-        mm([(P(cb_), P1, ap("kv16", ALL)), (P(cb_), ap("p2f", ALL), ap("km", ALL))] +
-           [(P(cb_, S_(r, L, 16)), wsl("ws", r, 1), m16) for r in range(16)])
-        lin(ap("cb", CHILD), P(cb_), bias=c1(CHB))
-        dma([(pap("cb", row(6), WEDV), pap("cb", row(1), CHILD)), (pap("cb", row(0), CHILD), pap("vv", row(0), ALL))] +
-            [(pap("cb", row(j), CHILD), pap("nv", row(j), t, ALL)) for j in (6, 7)])
+        dma([(pap("cb", row(b), CHILD), pap("km", row(a), ALL)) for a, b in [(0, 4), (1, 5)] + [(k, k) for k in range(9, 16)]])
+        vop("transpose", sm(21), [sm(20)], [sm(20)])
+        dma([(pap("cb", S_(16 * h + 1, 128, 32), CHILD), sm(21, S_(16 * h, 16 * h + 16))) for h in BOTH])
+        dma([(pap("cb", row(6), WEDV), pap("cb", row(1), CHILD))])
         mm([(P(kb), HIH, ap("xm16", ALL)), (P(kb), HIB, xv(t))])
-        ts(ap("nb", t, S_(512, 1024)), P(kb), MAGIC, A.add, -MAGIC, A.add)
+        for a in range(0, L, MEAN):
+            ts(ap("nb", t, S_(512 + a, 512 + a + MEAN)), P(kb, S_(a, a + MEAN)), MAGIC, A.add, -MAGIC, A.add)
+        if t + 1 < R:
+            dma([(ap("xx", S_(n0, n0 + L)), ap("nb", t, S_(512, 1024)))])
+            blood_rows(t, [pap("cb", row(j), CHILD) for j in range(6)], lambda a, b: ap("nb", t, S_(512 + a, 512 + b)))
         ts(sm(5), ap("sc2", ends), 0.0, A.is_equal, 8192.0, A.mult)
         ts(sm(6, S_(0, 16)), ap("sd1", S_(16, 272, 17)), 0.0, A.is_equal, 8192.0, A.mult)
         tt(sm(7), m16, sm(5), A.add)
@@ -613,16 +623,24 @@ def build(model=None):
         scan(ap("li", 1, ALL), ap("li", 0, ALL), ap("li", 0, ALL), A.add, A.max)
         Z, Y = P(7, S_(320, 352)), P(7, S_(352, 384))
         mm([(P(7, S_(320, 384)), IH, ap("itc", ALL, ALL))] + [(P(7, S_(320, 384)), wsl("ws", 7, r), ap("li", ALL, S_(r, L, 16))) for r in range(16)])
-        ts(sm(8), Z, 512.0, A.mult)
-        tt(sm(9), Y, sm(8), A.min)
-        copy(su(RO), sm(9))
+        ts(sm(8), Y, 1.0 / 512, A.mult)
+        tt(sm(9), Z, sm(8), A.min)
         ts(su(ONEW), Z, 512.0, A.mult)
-        ts(sm(10), sm(9), 639.5, A.is_gt, -1024.0, A.mult)
-        tt(sm(11), sm(10), sm(8), A.add)
-        ts(su(OVC), sm(11), 1024.0, A.add)
+        ts(sm(10), sm(9), 639.5 / 512, A.is_gt, -2.0, A.mult)
+        tt(sm(11), Z, sm(10), A.add)
+        ts(su(OVC), sm(11), 512.0, A.mult, 1024.0, A.add)
         tt(sm(12), sm(11), sm(9), A.min)
-        ts(su(XI), sm(12), 512.0, A.add)
-        tt(ind(ap("st", ALL), su(RO)), ap("rk", t, ALL), ap("xq", ALL), A.add)
+        ts(su(XI), sm(12), 512.0, A.mult, 512.0, A.add)
+        mm([(P(kb, S_(0, 256)), IB, ap("ns", ALL))] +
+           [(P(kb, S_(32 * a + 1, 32 * a + 32)), R7, ap("li", 1, S_(15, 496, 16))) for a in range(8)])
+        scan(ap("bs", ALL), P(kb, S_(0, 256)), ap("seg", ALL), A.max, A.min)
+        copy(su(RO, S_(0, 8)), ap("bs", S_(31, 256, 32)))
+        tt(ap("fl", ALL), ind(sm(8), su(RO, S_(0, 8))), ap("srow", ALL), A.is_le)
+        mm([(P(cb_, S_(0, 8)), I16H, ap("bs", S_(31, 256, 32)))] +
+           [(P(cb_, S_(0, 8)), wsl("weh", 0, r), ap("fl", S_(r, 128, 16))) for r in range(16)])
+        ts(su(RO, S_(8, 16)), P(cb_, S_(0, 8)), 511.0, A.min)
+        copy(ap("du", ALL), ind(ap("rk", t, ALL), su(RO, S_(8, 16))))
+        lin(ap("xs", ALL), ind(xv(t), su(RO, S_(8, 16))))
         lin(kk(t, 2048, 4), ind(ap("cb", ALL), su(OVC)))
         lin(kk(n0, n0 + L), ind(ap("cb", S_(0, 1024)), su(ONEW)))
         if t + 1 < R:
@@ -630,6 +648,13 @@ def build(model=None):
             ts(pc(4), P(6, S_(0, 1)), -1.0, A.mult, 4096.0, A.add)
             ts(pc(5), pc(4), 15, A.bitwise_and)
             ts(c1(THR + t + 1), pc(5), 16.0, A.mult, c1(TH + t + 1), A.add)
+
+    def blood_rows(t, rows, feats):
+        n0, s = B0 + L * t, nxt("sxn", 2)
+        dma([(pap("dtab", row(j), S_(n0, n0 + L)), rows[j]) for j in range(6)])
+        mm([(P(6, S_(64, 96)), wsl("we", E16, r), feats(32 * r, 32 * r + 32)) for r in range(16)])
+        lin(ap("sxn", s, ALL), P(6, S_(64, 96)), scale=1.0 / 16)
+        dma([(pap("dtab", row(7), S_(n0, n0 + L)), ap("sxn", s, ALL))])
 
     def stores(t):
         n0 = B0 + L * t
@@ -643,88 +668,111 @@ def build(model=None):
 
     def ask(t):
         n0 = B0 + L * t
-        kb, cb_ = t % 2, 2 + t % 2
-        slot = ap("st", S_(512, 640))
-        ts(ap("du", ALL), slot, 1.0 / 1024, A.mult)
-        ts(ap("ai", ALL), slot, MAGIC * 1024, A.add, -MAGIC * 1024, A.add)
-        tt(ap("xs", ALL), slot, ap("ai", ALL), A.subtract)
+        kb, cb_ = t % 2 if t else 6, 2 + t % 2
         banks = [cb_, kb, cb_, kb] if t + 1 < R else [cb_, kb, 4, 5]
         for b in range(4):
             lin(ap("ga", S_(L * b, L * b + L)), ind(ap("rx%d" % t, ALL), ap("du", S_(32 * b, 32 * b + 32))))
         for b in range(4):
             h, q = b // 2, b % 2
+            if h in ASK_V[t]:
+                mm([(P(banks[b], S_(k, L, 16)), IB, ap("xs", S_(32 * b, 32 * b + 32))) for k in range(16)])
+                tt(ap("ra", S_(32 * b, 32 * b + 32), ALL), ap("ga", S_(L * b, L * b + L)), P(banks[b]), A.max)
+                continue
             mm([(P(banks[b], S_(k, L, 8)), NIB, ap("xs", S_(64 * h, 64 * h + 64))) for k in range(8)], ("a", t, b))
             mm([(P(banks[b], S_(k, L, 8)), IB, ap("ga", S_(1024 * h + 8 * q + k, 1024 * h + 1024, 16))) for k in range(8)], ("a", t, b))
-            act(ap("ra", S_(4 * h, 4 * h + 4), ALL, S_(8 * q, 8 * q + 8)), P(banks[b]), F.Abs, scale=128.0)
+            act(ap("ra", S_(64 * h, 64 * h + 64), S_(8 * q, 8 * q + 8)), P(banks[b]), F.Abs, scale=128.0)
         o = P(7, S_(0, 128))
+        mm([(o, IH, ap("kq", ALL))], ("o", t))
         for h in range(2):
-            oh = P(7, S_(64 * h, 64 * h + 64))
-            mm([(oh, IH, ap("kq", S_(64 * h, 64 * h + 64)))] +
-               [(oh, wsl("we", E16, r), ap("ra", S_(4 * h, 4 * h + 4), r, ALL)) for r in range(16)])
-        scan(ap("sc1", S_(0, 128)), ap("rstk", S_(0, 128)), o, A.add, A.min)
-        copy(ap("si", 0, ALL), ap("sc1", S_(15, 128, 16)))
+            oh, byv = P(7, S_(64 * h, 64 * h + 64)), h in ASK_V[t]
+            if byv:
+                mm([(oh, wsl("we", EY, r), ap("ga", S_(1024 * h + 64 * r, 1024 * h + 64 * r + 64))) for r in range(16)], ("o", t))
+            for rs in ((range(8), range(8, 16)) if byv else (range(16),)):
+                mm([(oh, wsl("we", EMX if byv else E16, r), ap("ra", S_(64 * h + 4 * r, 64 * h + 4 * r + 4), ALL)) for r in rs], ("o", t))
+        scan(ap("sc0", ALL), ap("rstk", S_(0, 128)), o, A.add, A.min)
+        copy(ap("si", 0, ALL), ap("sc0", S_(15, 128, 16)))
         ts(ap("si", 1, ALL), ap("si", 0, ALL), 2047, A.bitwise_and)
         copy(su(NO, S_(0, 8)), ap("si", 1, ALL))
         lin(ap("nb", t, S_(1024, 1152)), ind(ap("ga", ALL), su(NO, S_(0, 8))))
-        lin(ap("xx", S_(n0, n0 + L)), ind(ap("nb", t, ALL), su(XI)))
+        n = 1 if t + 1 < R else 2
+        for a, b in [(L // n * h, L // n * (h + 1)) for h in range(n)]:
+            lin(ap("xx", S_(n0 + a, n0 + b)), ind(ap("nb", t, ALL), su(XI, S_(a // 16, b // 16))))
         dma([(ap("yx", S_(L * t, L * t + L)), ap("xx", S_(n0, n0 + L)))])
         for u in range(t + 1, R):
             push(ap("rx%d" % u, S_(n0, n0 + L)), ap("xx", S_(n0, n0 + L)), -1 - u)
 
     def suitors(t):
-        lin(ap("dv", t % 2, ALL), ap("dtab", vcols(t)), eng="G")
-        dma([(pap("dv", row(j + 8), t % 2, ALL), pap("dv", row(j), t % 2, ALL)) for j in range(6)])
+        for s, c in ((2, 4), (t % 2, 0)):
+            for e in BOTH:
+                lin(ap("dv", s, ALL, e), ap("dtab", S_(t + c, 2048, 8)), eng="G")
+        dma([(pap("dv", row(j + 8), t % 2, ALL, ALL), pap("dv", row(j), 2, ALL, ALL)) for j in range(7)])
 
-    def statics(t):
-        js = QUADS[t]
-        if t:
+    def statics(t, parts):
+        if "f" in parts:
+            opens(t, "k")
+            for js in QUADS[t]:
+                if js[0] in NAMES_PE[t]:
+                    for j in js:
+                        names_pe(t, j, BOTH, False)
+                else:
+                    names_static(t, js, BOTH)
+            for j, es in halves(t, "M"):
+                names_static(t, (j,), es)
+            bulk(t)
+        if "b" in parts:
             suitors(t)
-        for i in range(len(js) + 1):
-            if i < len(js):
-                names_static(t, js[i], BOTH)
-            if i >= 1:
-                score_quad(t, js[i - 1])
-        for j, es, mode in LONE[t]:
-            names_static(t, (j,), es)
-        bulk(t)
+            opens(t, "c")
+        for js in QUADS[t] + DYN[t]:
+            for x in parts:
+                score_quad(t, js, x)
 
-    opens(0)
-    lin(ap("kv16", ALL), ap("ki", vcols(0)), bias=-CEN)
-    suitors(0)
-    for j, es, _m in DYN[0]:
-        list_pe(0, [(j, e) for e in es], 4 + j % 2)
-        names_pe(0, [(j, e) for e in es], 6 + j % 2)
-    for i in range(0, len(DYN[0]), 2):
-        score_quad(0, [j for j, es, _m in DYN[0][i:i + 2]])
-    statics(0)
+    statics(0, "fb")
     answer(0)
     prepare(0)
+    least(0)
     for t in range(R):
+        if t == 0:
+            statics(1, "fb")
+            statics(2, "f")
+        if t == 1:
+            statics(2, "b")
         if t + 1 < R:
-            opens(t + 1)
-            lists(t + 1)
-            statics(t + 1)
+            statics(t + 1, "p")
         tail(t)
         if t + 1 < R:
             prepare(t + 1)
-            names_late(t + 1)
+            for j, es in halves(t + 1, "LW"):
+                names_pe(t + 1, j, es)
+            for q in DYN[t + 1]:
+                score_quad(t + 1, q, "B")
+                score_quad(t + 1, q, "F")
+            least(t + 1)
         stores(t)
         ask(t)
         if t + 1 < R:
-            score_late(t + 1)
+            score_asked(t + 1)
+        if t + 2 < R:
+            n0 = B0 + L * t
+            blood_rows(t, [kk(n0, n0 + L, 1, row(j)) for j in range(6)], lambda a, b: ap("xx", S_(n0 + a, n0 + b)))
     return ops
 
 
 def depend(ops):
-    hist = {}
+    hist, head = {}, {}
+    group = [o["alts"][0][2][2].get("group") for o in ops]
     for i, o in enumerate(ops):
         deps = {j: False for j in o["after"]}
         fixed = o["alts"][0][0] if len(o["alts"]) == 1 else None
+        gr = group[i]
+        if gr:
+            if gr in head:
+                deps[head[gr]] = False
+            head.setdefault(gr, i)
         for regs, wr in ((o["r"], False), (o["w"], True)):
             for n, pm, cm, _1, _2 in regs:
                 bank = n[0] == "p" and n[1:].isdigit()
                 for j, pj, cj, wj, ej in hist.get(n, []):
-                    if j == i:
+                    if j == i or (gr and group[j] == gr):
                         continue
                     over = (pm & pj) and (cm & cj)
                     if (over and (wr or wj)) or (bank and (ej is None or ej != fixed)):
@@ -734,17 +782,18 @@ def depend(ops):
                 h = hist.setdefault(n, [])
                 if wr:
                     bank = n[0] == "p" and n[1:].isdigit()
-                    h[:] = [x for x in h if x[0] == i or (x[1] & ~pm) or (x[2] & ~cm) or (bank and x[4] != fixed and cm + 1 != 1 << 512)]
+                    h[:] = [x for x in h if x[0] == i or (gr and group[x[0]] == gr) or (x[1] & ~pm) or (x[2] & ~cm) or (bank and x[4] != fixed and cm + 1 != 1 << 512)]
                 h.append((i, pm, cm, wr, fixed))
         o["deps"] = deps
 
 
-def search(ops, seed, tries, nj=4, amp=1500.0, temp=100.0):
+def search(ops, seed, tries, polish=0, nj=6, amp=1200.0, temp=60.0, temp2=20.0):
     n = len(ops)
     succ, dep = [[] for _ in range(n)], []
     for i, o in enumerate(ops):
         gr = o["alts"][0][2][2].get("group")
-        dep.append([(j, bool(gr) and gr == ops[j]["alts"][0][2][2].get("group"), ops[j]["kind"] == "c") for j in o["deps"]])
+        dep.append([(j, bool(gr) and gr == ops[j]["alts"][0][2][2].get("group"), ops[j]["kind"] == "c", True)
+                    for j in o["deps"]])
         for j in o["deps"]:
             succ[j].append(i)
     base = [min(a[1] for a in o["alts"]) + o["lat"] + LAT_X + (o["extra"] or 0.0) for o in ops]
@@ -770,8 +819,8 @@ def search(ops, seed, tries, nj=4, amp=1500.0, temp=100.0):
         def arrive(i, now):
             for e in cost[i]:
                 s = 0.0
-                for j, same, cj in dep[i]:
-                    x = fin[j] - 60.0 if same else fin[j] + (LAT_S if cj and eng[j] == e else LAT_X)
+                for j, same, cj, raw in dep[i]:
+                    x = start[j] if same else fin[j] + (LAT_S if cj and eng[j] == e else LAT_X)
                     if x > s:
                         s = x
                 p = -prio[i] + (shy[i] if e == "V" and len(cost[i]) > 1 else 0.0)
@@ -837,8 +886,8 @@ def search(ops, seed, tries, nj=4, amp=1500.0, temp=100.0):
         for i in order:
             e = eng[i]
             s = free[e]
-            for j, same, cj in dep[i]:
-                x = fin[j] - 60.0 if same else fin[j] + (ls if cj and eng[j] == e else lx)
+            for j, same, cj, raw in dep[i]:
+                x = 0.0 if same else fin[j] + (ls if cj and eng[j] == e else lx)
                 if x > s:
                     s = x
             s = free[e] = s + cs[i][e]
@@ -851,7 +900,7 @@ def search(ops, seed, tries, nj=4, amp=1500.0, temp=100.0):
 
     def times(jit, shy):
         order, start, fin, eng = schedule(jit, shy)
-        return [replay(order, eng, k) for k in range(len(MODELS))]
+        return [max(fin)] + [replay(order, eng, k) for k in range(1, len(MODELS))]
 
     rng = np.random.RandomState(seed)
     both = [i for i in range(n) if len(cost[i]) > 1]
@@ -872,10 +921,110 @@ def search(ops, seed, tries, nj=4, amp=1500.0, temp=100.0):
             if m < best:
                 best, keep = m, (j2, s2)
     order, start, fin, eng = schedule(*keep)
+
+    def run(order, eng, k, p, old):
+        cs, lt = others[k]
+        pre, post, lx, ls = MODELS[k][3], MODELS[k][4], MODELS[k][7], MODELS[k][8]
+        fin, end, by = (list(x) for x in old) if old else ([0.0] * n, [0.0] * n, [0] * n)
+        last, dlast = {}, None
+        for q in range(p - 1, -1, -1):
+            i = order[q]
+            last.setdefault(eng[i], i)
+            if dlast is None and moves[i]:
+                dlast = i
+            if len(last) == 5 and dlast is not None:
+                break
+        dfree = fin[dlast] - post if dlast is not None else 0.0
+        for q in range(p, n):
+            i = order[q]
+            e = eng[i]
+            b = last.get(e)
+            s = end[b] if b is not None else 0.0
+            b = -1 - b if b is not None else n
+            for j, same, cj, raw in dep[i]:
+                x = 0.0 if same else fin[j] + (ls if cj and eng[j] == e else lx)
+                if x > s:
+                    s, b = x, j
+            s = end[i] = s + cs[i][e]
+            last[e] = i
+            if moves[i]:
+                if dfree > s + pre:
+                    s, b = dfree - pre, -1 - dlast
+                dfree = s + lt[i] - post
+                fin[i], dlast = dfree + post, i
+            else:
+                fin[i] = s + lt[i]
+            by[i] = b
+        return fin, end, by
+
+    ks = range(len(MODELS))
+    state = [run(order, eng, k, 0, None) for k in ks]
+    cur = best = sum(max(s[0]) * w for s, w in zip(state, norm))
+    keep = (order, eng)
+    for it in range(polish):
+        k = rng.randint(0, len(MODELS))
+        fin, end, by = state[k]
+        i, held = fin.index(max(fin)), []
+        while i < n:
+            b = by[i]
+            if b < 0:
+                b = -1 - b
+                held.append((b, i))
+            i = b
+        u, v = held[rng.randint(0, len(held))]
+        where = {x: q for q, x in enumerate(order)}
+        pu, pv, o2, e2, kind = where[u], where[v], list(order), eng, rng.randint(0, 4)
+        if it % 3 == 0:
+            e, cs = "VVA"[rng.randint(0, 3)], others[k][0]
+            line = [x for x in order if eng[x] == e]
+            idle = [(x, end[y], end[x] - cs[x][e]) for y, x in zip(line, line[1:]) if end[x] - cs[x][e] - end[y] > 60.0]
+            x, a, b = idle[rng.randint(0, len(idle))]
+            pu = where[x]
+            fit = [y for y in order[pu + 1:] if e in cost[y] and cs[y][e] < b - a + 150.0 and
+                   all(where[d[0]] < pu and fin[d[0]] + LAT_S < a + 100.0 for d in dep[y])]
+            if not fit:
+                continue
+            v = fit[int(len(fit) * rng.random_sample() ** 2)]
+            o2.insert(pu, o2.pop(where[v]))
+            e2 = list(eng)
+            e2[v] = e
+        elif kind == 0 and (len(cost[u]) > 1 or len(cost[v]) > 1):
+            x = u if len(cost[v]) == 1 or (len(cost[u]) > 1 and it % 2) else v
+            e2 = list(eng)
+            e2[x] = [e for e in cost[x] if e != eng[x]][0]
+            pu = where[x]
+        elif kind % 2 and all(where[s] > pv for s in succ[u]):
+            o2.insert(min(pv + rng.randint(0, 12), min([where[s] for s in succ[u]] + [n]) - 1), o2.pop(pu))
+        elif all(where[d[0]] < pu for d in dep[v]):
+            pu = max([pu - rng.randint(0, 12)] + [where[d[0]] + 1 for d in dep[v]])
+            o2.insert(pu, o2.pop(pv))
+        else:
+            continue
+        room = temp2 * (1 - it / polish) * float(rng.exponential())
+        s2, m = list(state), cur
+        for q in ks:
+            q = (k + q) % len(MODELS)
+            s2[q] = run(o2, e2, q, pu, state[q])
+            m += (max(s2[q][0]) - max(state[q][0])) * norm[q]
+            if m > cur + room + 60.0:
+                break
+        if m <= cur + room:
+            cur, order, eng, state = m, o2, e2, s2
+            end = state[0][1]
+            o2 = sorted(order, key=lambda i: end[i] - cost[i][eng[i]])
+            if it % 8 == 0 and o2 != order:
+                s2 = [run(o2, eng, k, 0, None) for k in ks]
+                m2 = sum(max(s[0]) * w for s, w in zip(s2, norm))
+                if m2 <= cur:
+                    cur, order, state = m2, o2, s2
+            if cur < best:
+                best, keep = cur, (order, eng)
+    order, eng = keep
+    state = [run(order, eng, k, 0, None) for k in ks]
     for o, e in zip(ops, eng):
         o["pick"] = [a for a in o["alts"] if a[0] == e][0]
-    ops[0]["times"] = times(*keep)
-    return order, start, fin
+    ops[0]["times"] = [max(s[0]) for s in state]
+    return order, [state[0][1][i] - cost[i][eng[i]] for i in range(n)], state[0][0]
 
 
 _plan = []
@@ -885,7 +1034,7 @@ def plan():
     if not _plan:
         ops = build()
         depend(ops)
-        _plan.append((ops,) + search(ops, SEED, TRIES))
+        _plan.append((ops,) + search(ops, SEED, TRIES, POLISH))
     return _plan[0]
 
 
@@ -896,7 +1045,7 @@ def rank_program(g, core, T, topo):
     ops, order = plan()[0:2]
     Q = {"V": g.vector, "A": g.scalar, "P": g.tensor, "G": g, "Y": g.sync}
     calls = {"tensor_copy": g.vector.tensor_copy, "tensor_tensor": g.vector.tensor_tensor, "tensor_scalar": g.vector.tensor_scalar,
-             "memset": g.vector.memset, "tensor_tensor_scan": g.vector.tensor_tensor_scan, "tensor_reduce": g.vector.tensor_reduce,
+             "memset": g.vector.memset, "tensor_tensor_scan": g.vector.tensor_tensor_scan, "transpose": g.vector.transpose,
              "activation": g.scalar.activation, "iota": g.iota, "affine_select": g.affine_select}
 
     def real(x):

@@ -10,28 +10,31 @@ OFF = L
 CEN = 1920.0
 MAGIC = 12582912.0
 BAR = 262144.0
-NG1, NGD, NRB, NDB, NCC, LATE = 4, 7, 5, 3, 10, 2
+NG1, NG, LG, NB, LB, NQ, LQ = 8, 6, 3, 7, 2, 3, 3
 f32, bf, f16, i32, u16 = "float32", "bfloat16", "float16", "int32", "uint16"
 SB = {
     "ki": ([B0], i32), "kk": ([OFF + W + 32], f32), "xx": ([W], bf), "dtab": ([B0 + 2 * L], f32),
-    "rk": ([R, L], f32), "qa": ([R, 32], u16), "of3": ([16, 96], u16), "kw3": ([16, R, 32], u16), "kv16": ([L], f16), "ws": ([8, 144], f16), "m4": ([144], f32),
+    "rk": ([R, L], f32), "qa": ([R, 32], u16), "of3": ([16, 96], u16), "kw3": ([16, R, 32], u16), "kv16": ([L], f16), "ws": ([8, 144], f16),
     "rx0": ([B0], bf), "rx1": ([B0 + L], bf), "rx2": ([B0 + 2 * L], bf),
-    "cb": ([2048], f32), "nb": ([R, 1152], bf), "pkv": ([L], f32), "nv": ([R, L], f32), "vv": ([L], f32),
+    "cb": ([2048], f32), "nb": ([R, 1152], bf), "pkv": ([L], f32), "nv": ([2, L], f32), "vv": ([L], f32),
     "kvf": ([L], f32), "l67": ([2, 32], f32),
-    "cu": ([R * 16, 32], u16), "cc": ([NCC + 3, 128], f16), "kp": ([L], bf),
-    "g1": ([NG1, 2 * L], f16), "gh": ([3, 2, L], f16), "gd": ([NGD + 2 * LATE, L, 2], f16),
-    "bb": ([2, L], bf), "rb": ([NRB + LATE + 2, L, 2], bf), "db": ([NDB + 2 * LATE, 256, 2], bf),
-    "dv": ([3, 256, 2], f32), "barc": ([32], bf), "sc0": ([128], f32), "sc1": ([L], f32), "sc2": ([L], f32), "uu": ([L], bf), "sd1": ([272], f32), "li": ([2, L], f16),
+    "cu": ([R * L], u16), "kp": ([L], bf),
+    "g1": ([NG1, 2 * L], u16), "gh": ([3, 2, L], f16),
+    "gd": ([NG + LG, 2 * L], f16), "rb": ([(NB + LB) * 2 * L], bf), "eq": ([NQ + LQ, 384], bf), "sv": ([R, 384], f16),
+    "zz": ([3, 36, 4], f16), "wd": ([48], f32), "wv": ([48], f16), "w8": ([10, 8], bf), "tht": ([4, 32], f32),
+    "pat": ([3, 292], f32), "sxc": ([144], f32), "sxn": ([2, 32], f32),
+    "bb": ([2, L], bf),
+    "barc": ([32], bf), "sc0": ([128], f32), "sc1": ([L], f32), "sc2": ([L], f32), "uu": ([L], bf), "sd1": ([272], f32), "li": ([2, L], f16),
     "km": ([L], f32), "val": ([L], f32), "xm16": ([L], f16),
     "ga": ([2048], bf), "ra": ([128, 16], bf), "xs": ([128], bf), "du": ([128], u16),
-    "sm": ([22, 32], f32), "si": ([2, 8], i32), "sa": ([2, 96], i32), "su": ([12, 32], u16), "m16": ([32], f16),
-    "pc": ([8], i32), "col": ([48], f32), "ix": ([144], f32), "sxc": ([144], f32), "sxn": ([2, 32], f32),
-    "mi": ([2, 32], i32), "mf": ([32], bf), "sxw": ([R, 32], f32),
+    "sm": ([23, 32], f32), "si": ([2, 8], i32), "sa": ([2, 96], i32), "su": ([12, 32], u16), "m16": ([32], f16),
+    "pc": ([8], i32), "col": ([48], f32), "ix": ([144], f32),
+    "sxw": ([R, 32], f32),
     "ns": ([256], bf), "seg": ([256], bf), "bs": ([256], f16), "srow": ([128], f32), "fl": ([128], f16),
-    "we": ([8, 144], bf), "weh": ([2, 144], f16), "rr": ([16, 128], f16), "ll": ([16, 128], f16),
-    "mb": ([5, 128], bf), "mh": ([8, 128], f16), "blk": ([128], f32), "mask": ([32], f32),
+    "we": ([6, 144], bf), "weh": ([1, 144], f16), "rr": ([16, 128], f16), "ll": ([16, 128], f16),
+    "mb": ([9, 128], bf), "blk": ([128], f32), "mask": ([32], f32),
     "kc": ([2, L], bf), "rs0": ([L], bf), "rstk": ([L], bf), "dm0": ([L], bf), "rs1": ([272], bf),
-    "ia": ([2, 32], f32), "itc": ([2, 32], f16), "kq": ([128], f16),
+    "stp": ([L], bf), "ia": ([2, 32], f32), "itc": ([3, 32], f16), "kq": ([128], f16),
     "thi": ([4], i32), "thf": ([4], f32), "wi": ([4], i32), "l8": ([128], f32),
 }
 SCRATCH = {n: ("sbuf", [128] + s, d) for n, (s, d) in SB.items()}
@@ -49,8 +52,8 @@ MODELS = [(0.9, 1.56, 3.8, 900.0, 400.0, 280.0, 3.5, 260.0, 170.0, 0.52, 100.0, 
           (0.9, 1.3, 2.5, 1300.0, 600.0, 220.0, 4.5, 290.0, 200.0, 0.51, 150.0, 8000.0)]
 DPRE, DPOST = MODELS[0][3:5]
 LAT_X, LAT_S = MODELS[0][7:9]
-SEED, TRIES, POLISH, SHY, TOL, DEL = 0, 600, 55000, 4000.0, 200.0, 600.0
-KK2 = [(0, 1024, "VA"), (1024, 2048, "VA"), (2048, B0, "VA")]
+SEED, TRIES, POLISH, SHY, TOL, DEL = 0, 300, 52000, 20000.0, 200.0, 600.0
+SWEEPS, SLACK, BIAS = 0, 500.0, (0.0, 1.0, 300.0, 1000.0)
 LEAD = [0.0, 0.0, 0.0]
 SOON = 15000.0
 S_ = slice
@@ -106,13 +109,15 @@ def kof(t, j, e):
 
 BOTH = (0, 1)
 QUADS = [[(0, 1), (2, 3), (4, 5), (6, 7)], [(0, 1), (4, 5), (6, 7)], [(0, 1), (6, 7)]]
-NAMES_PE = [(0, 2), (), ()]
-BATCH = [(0, 1), (1, 2), (2, 4), (4, 6), (6, 8)]
+NAMES_PE = [(0,), (), ()]
+BATCH = [(0, 1), (1, 2), (2, 4)]
 ASK_V = [(), (), (0,)]
 DYN = [[], [((3, "LW"), (2, "LL"))], [((2, "LL"), (3, "LL")), ((4, "WM"), (5, "MM"))]]
 PIECES = [[1] * 8, [1, 1, 1, 1, 4, 4, 4, 4], [1, 1, 1, 1, 4, 4, 4, 4]]
 KVF = "G"
-HOLD, HALVES, MEAN = True, (1, 1, 1), 256
+MEAN, WED = 256, 128
+WHOLE = [(2, 3, 4, 5, 6), (), ()]
+BANKS, DTE, XAT = [(4, 5, 6, 7), (4, 5), (4, 5)], "G", 0
 
 
 def build(model=None):
@@ -241,64 +246,55 @@ def build(model=None):
 
     for a, b in ((0, 1024), (1024, 2048), (2048, B0)):
         dma([(ap("ki", S_(a, b)), ap("kin", S_(a, b)))], extra=6e6 - 100.0 * a)
-    dma([(ap("xx", S_(0, B0)), ap("xf", ALL))])
+    if not XAT:
+        dma([(ap("xx", S_(0, B0)), ap("xf", ALL))])
     dma([(pap("thi", S_(0, 8), S_(0, R)), ap("th", ALL)), (ap("wi", S_(0, R)), ap("w", ALL))])
 
-    PM, PG, Q8, PP, C15, N67, DE, DO, H0, H1, H1B, BAR0, BAR1, CCOL, GB, GS, _a, _b, P16, TMP = range(20)
-    WF, TH, THR, GS2, P64 = 24, 27, 30, 33, 34
+    PP, PM, PG, Q4, C15, N67, CI, ZC, S16, TMP, XC, _1, _2, KC, _1, _2, DE, DO = range(18)
+    WF, P64 = 28, 34
     iota(pc(0), [[0, 1]], 0, 1, 1e6)
     iota(ap("ix", ALL), [[1, 144]], 0, 0, 1e6)
     ts(pc(1), pc(0), 15, A.bitwise_and)
     ts(pc(2), pc(0), 4, A.arith_shift_right)
-    ts(pc(3), pc(0), 7, A.bitwise_and)
-    copy(ap("col", S_(0, 3)), ap("pc", S_(1, 4)))
-    copy(c1(PP), pc(0))
-    ts(c1(C15), c1(PG), 16.0, A.mult, 15.0, A.add)
+    ts(pc(3), pc(0), 3, A.bitwise_and)
+    copy(ap("col", S_(0, 4)), ap("pc", S_(0, 4)))
+    lin(c1(C15), c1(PG), scale=16.0, bias=15.0)
     ts(ap("mask", S_(0, 16)), ap("ix", S_(0, 16)), c1(PM), A.is_equal)
-    ts(ap("mask", S_(16, 32)), ap("mask", S_(0, 16)), -CEN, A.mult)
-    ts(c1(TMP), mk(6), -1.0, A.mult, mk(7), A.subtract)
-    ts(c1(N67), c1(TMP), 1.0, A.add)
-    ts(c1(DE), c1(PM), W - CEN, A.add)
-    ts(c1(DO), c1(PM), W + 16 - CEN, A.add)
-    ts(c1(H0), c1(PM), 7.5, A.is_lt)
-    ts(c1(H1B), c1(PM), 7.5, A.is_gt, c1(C15), A.add)
-    ts(c1(BAR0), c1(Q8), 6.5, A.is_lt, BAR, A.mult)
-    ts(c1(CCOL), c1(Q8), 5.5, A.is_lt, 0.5, A.mult)
-    ts(c1(TMP + 1), c1(Q8), 6.0, A.not_equal, -2040.0, A.mult)
-    ts(c1(GB), mk(15), 6120.0, A.mult, c1(TMP + 1), A.add)
-    ts(c1(GS), c1(PM), 14.5, A.is_lt)
-    ts(c1(GS2), c1(PM), 5.5, A.is_lt)
-    ts(c1(P64), c1(PM), 64.0, A.mult)
+    lin(ap("mask", S_(16, 32)), ap("mask", S_(0, 16)), scale=-CEN)
+    ts(c1(TMP), mk(6), mk(7), A.add, -1.0, A.mult)
+    lin(c1(N67), c1(TMP), bias=1.0)
+    for i, c in enumerate((W, W + 16, DUM, DUM + 16)):
+        lin(c1(DE + i), c1(PM), bias=c - CEN)
+    lin(c1(CI), c1(PM), scale=8.0, bias=c1(PG))
+    lin(c1(S16), mk(7), scale=16.0)
+    lin(ap("col", S_(XC, XC + R)), ap("mask", S_(8, 8 + R)), scale=BAR)
+    lin(ap("col", S_(KC, KC + R)), ap("col", S_(XC, XC + R)), bias=c1(S16))
+    WD, WV = ap("wd", ALL), ap("wv", ALL)
+    ts(WD, ap("ix", S_(0, 48)), c1(CI), A.is_equal)
+    lin(WV, WD)
+    W16, WM32, WNUM, WKEY, _3, _4, WMOD, _5, _6, W1 = range(10)
+    ts(ap("w8", W1, ALL), ap("ix", S_(0, 8)), c1(PG), A.is_equal)
+    for i, c in [(W16, 16.0), (WM32, -32.0), (WNUM, mk(11))] + [(WKEY + t, c1(KC + t)) for t in range(R)] + [(WMOD + t, c1(XC + t)) for t in (1, 2)]:
+        lin(ap("w8", i, ALL), ap("w8", W1, ALL), scale=c)
+    lin(c1(P64), c1(PM), scale=64.0)
     copy(ap("col", S_(WF, WF + R)), ap("wi", S_(0, R)))
-    E16, EM32, EBAR, EMX, EY, EW = range(6)
-    ts(ap("we", EBAR, ALL), ap("ix", ALL), c1(H1B), A.is_equal, c1(BAR0), A.mult)
-    for i, c in [(E16, 16.0), (EM32, -32.0), (EMX, 4096.0), (EY, -2048.0),
-                 (EW, c1(WF)), (EW + 1, c1(WF + 1)), (EW + 2, c1(WF + 2))]:
-        ts(ap("we", i, ALL), ap("ix", ALL), c1(C15), A.is_equal, c, A.mult)
+    E16, EMX, EY, EW = range(4)
     ts(ap("weh", 0, ALL), ap("ix", ALL), c1(C15), A.is_equal)
-    memset(ap("ws", ALL), 0.0)
-    one = ap("ws", ALL, S_(15, 144, 16))
-    memset(one, 1.0)
-    add([("G", 170 + 2 * CY * 72, ("affine_select", [one, one, [[-1, 8], [-16, 9]], A.is_equal, 0.0, 0, 1], {}))], [one], [one], extra=2e4)
-    lin(ap("weh", 1, ALL), ap("ws", 7, ALL), scale=16.0)
+    for i, c in [(E16, 16.0), (EMX, 4096.0), (EY, -2048.0), (EW, c1(WF)), (EW + 1, c1(WF + 1)), (EW + 2, c1(WF + 2))]:
+        lin(ap("we", i, ALL), ap("weh", 0, ALL), scale=c)
+    for k in list(range(BATCH[-1][1])) + [7]:
+        lin(ap("ws", k, ALL), ap("weh", 0, ALL), scale=mk(k))
     memset(ap("rr", ALL), 1.0 / 64)
     add([("G", 170 + 2 * CY * 2048, ("affine_select", [ap("rr", ALL), ap("rr", ALL), [[-1, 16], [-16, 8], [0, 16]], A.is_equal, 0.0, 0, 1], {}))],
         [ap("rr", ALL)], [ap("rr", ALL)])
     add([("G", 170 + 2 * CY * 2048, ("affine_select", [ap("ll", ALL), ap("rr", ALL), [[0, 16], [-1, 128]], A.not_equal, -1.0 / 64, 0, 1], {}))],
         [ap("rr", ALL)], [ap("ll", ALL)])
-    IB, NIB, HIB, ZB = [ap("mb", i, ALL) for i in range(4)]
-    IH, HIH, NI64, I16H, C0, R7, W7, C1S = [ap("mh", i, ALL) for i in range(8)]
+    IB, I8K, NIB, HIB, IBAR, NI64, I16, R7, W7 = [ap("mb", i, ALL) for i in range(9)]
     ix128 = ap("ix", S_(0, 128))
     ts(IB, ix128, c1(PP), A.is_equal)
-    ts(IH, ix128, c1(PP), A.is_equal)
-    ts(c1(TMP + 3), c1(PP), 8.0, A.add)
-    ts(C1S, ix128, c1(TMP + 3), A.is_equal, c1(H0), A.mult)
-    for m, c in [(NIB, -1.0), (HIB, 0.5), (ZB, 0.0)]:
+    for m, c in [(NIB, -1.0), (HIB, 0.5), (IBAR, BAR), (NI64, -1.0 / 64), (I16, 16.0), (I8K, 8192.0)]:
         lin(m, IB, scale=c)
-    for m, c in [(HIH, 0.5), (NI64, -1.0 / 64), (I16H, 16.0), (C0, c1(H0)), (R7, c1(CCOL))]:
-        lin(m, IH, scale=c)
-    mm([(P(3, S_(144, 272)), IH, C0), (P(3, S_(144, 272)), wsl("weh", 0, 15), R7)])
-    lin(C0, P(3, S_(144, 272)))
+    memset(ap("zz", ALL, ALL, ALL), 0.0)
     lin(W7, ix128, scale=0.0, bias=mk(7))
     lin(R7, ap("rr", 7, ALL), scale=-4096.0)
     memset(ap("barc", ALL), BAR)
@@ -311,36 +307,38 @@ def build(model=None):
     for n, w_, step, c in (("rs0", L, 16, 1), ("rstk", L, 16, (1 << 24) - 1), ("rs1", 272, 17, 1)):
         iota(ap(n, ALL), [[0, w_]], 0, 0)
         iota(ap(n, S_(0, w_, step)), [[0, w_ // step]], c, 0)
-    for t in range(R):
-        iota(ap("nv", t, ALL), [[1, L]], B0 + L * t, 0)
     iota(ap("seg", ALL), [[0, 8], [1, 32]], 0, 0)
     iota(ap("ns", ALL), [[4096, 2], [256, 4], [0, 32]], 0, 0)
-    ts(pc(6), pc(1), 3, A.bitwise_and)
-    ts(c1(P64 + 1), pc(6), 1008.0, A.mult, 32.0, A.add)
-    ts(c1(P64 + 2), c1(PM), 16.0, A.mult, c1(P64 + 1), A.add)
-    ts(ap("ns", ALL), ap("ns", ALL), c1(P64 + 2), A.add)
+    lin(c1(P64 + 1), c1(Q4), scale=1008.0, bias=32.0)
+    lin(c1(P64 + 2), c1(PM), scale=16.0, bias=c1(P64 + 1))
+    lin(ap("ns", ALL), ap("ns", ALL), bias=c1(P64 + 2))
     iota(ap("srow", ALL), [[64, 2], [1, 16], [16, 4]], 511, 0)
     lin(ap("srow", ALL), ap("srow", ALL), scale=1.0 / 512)
     iota(ap("kk", S_(0, OFF)), [[0, OFF]], 0, 0)
     iota(ap("ia", 0, ALL), [[16, 32]], 0, 0)
     ts(ap("itc", 0, ALL), ap("ia", 0, ALL), c1(PM), A.add, 1.0 / 512, A.mult)
-    ts(ap("itc", 1, ALL), ap("ia", 0, ALL), 0.0, A.mult, 511.0, A.add)
-    ts(ap("ia", 1, ALL), ap("ia", 0, ALL), c1(PM), A.add, -float(OFF), A.add)
+    lin(ap("itc", 1, ALL), ap("ia", 0, ALL), scale=0.0, bias=511.0)
+    ts(ap("itc", 2, ALL), ap("ia", 0, ALL), c1(PM), A.add, -float(OFF), A.add)
+    lin(ap("ia", 1, ALL), ap("itc", 2, ALL), bias=OFF + DUM - 4096.0)
+    iota(ap("stp", ALL), [[-2, 16], [0, 32]], 300, 0)
     iota(ap("blk", ALL), [[1024, 2], [1, 64]], 0, 0)
     lin(ap("kq", ALL), ap("blk", ALL), bias=c1(P64))
     p8 = S_(0, 8)
     iota(pap("l8", p8, ALL), [[1, 8], [0, 16]], 0, -1)
     ts(pap("l8", p8, ALL), pap("l8", p8, ALL), 0.0, A.is_equal)
     copy(pap("thf", p8, S_(0, R)), pap("thi", p8, S_(0, R)))
-    mm([(P(1, S_(300, 300 + R)), pap("l8", p8, ALL), pap("thf", p8, S_(0, R)))])
-    ts(c1(TH), P(1, S_(300, 301)), 16.0, A.mult, -0.5, A.add)
-    ts(ap("col", S_(TH + 1, TH + R)), P(1, S_(301, 300 + R)), 16.0, A.mult, -8.5, A.add)
+    for t in range(R):
+        lin(pap("sc1", p8, S_(128 * t, 128 * t + 128)), pap("l8", p8, ALL), scale=0.0, bias=pap("thf", p8, S_(t, t + 1)))
+    mm([(P(1, S_(300 + 32 * t, 332 + 32 * t)), pap("sc1", p8, S_(128 * t, 128 * t + 128)), pap("l8", p8, S_(0, 128, 4))) for t in range(R)])
+    lin(ap("tht", 0, ALL), P(1, S_(300, 332)), scale=16.0, bias=-0.5)
+    lin(ap("tht", S_(1, R), ALL), P(1, S_(332, 396)), scale=16.0, bias=-8.5)
 
     def o1(t, j, e):
         return ap("of3", kof(t, j, e), S_(32 * t, 32 * t + 32))
 
-    def cu(t, j, e):
-        return ap("cu", 16 * t + 2 * j + e, ALL)
+    def cu(t, j, e, a=0, b=32):
+        c = 32 * (16 * t + 2 * j + e)
+        return ap("cu", S_(c + a, c + b))
 
     def lists():
         for h in BOTH:
@@ -357,25 +355,50 @@ def build(model=None):
             a, b = 1 if k < BATCH[-1][1] else 0, 1 if k in (6, 7) else R
             if a < b:
                 dma([(ap("of3", k, S_(32 * a, 32 * b)), pap("kw3", row(k), ALL, S_(a, b), ALL))])
+            if k + 1 == XAT:
+                mark["lists"] = len(ops) - 1
+                dma([(ap("xx", S_(0, B0)), ap("xf", ALL))], after="lists")
+
+    cnt = {}
+
+    def nxt(n, m, late=0):
+        k = cnt.get((n, late), 0)
+        cnt[(n, late)] = k + 1
+        return m + k % late if late else k % m
+
+    def bank(t):
+        return BANKS[t][nxt(("pb", BANKS[t]), len(BANKS[t]))]
+
+    def suitors(t):
+        b = bank(0)
+        mm([(P(b, S_(2 * c + e, 384, 8)), ap("dtab", S_(4 * c + t, 2048, 16)), WD) for c in range(4) for e in BOTH])
+        lin(ap("sv", t, ALL), P(b, S_(0, 384)), bias=-CEN)
 
     lists()
-    for a, b, eng in KK2:
+    for a, b in ((0, 1024), (1024, 2048), (2048, B0)):
+        lin(ap("dtab", S_(a, b)), ap("ki", S_(a, b)), eng=DTE)
+    for a, b in ((0, 1024), (1024, 2048), (2048, B0)):
         lin(kk(a, b), ap("ki", S_(a, b)), eng="G")
-        lin(ap("dtab", S_(a, b)), ap("ki", S_(a, b)), scale=c1(GS2), eng=eng)
-    iota(ap("m4", ALL), [[0, 36], [1, 4]], 0, 0)
-    iota(ap("dtab", S_(B0, B0 + 2 * L)), [[0, L // 2], [1, 4]], 0, 0)
-    dma([(pap("dtab", row(6), S_(0, B0)), ap("m4", ALL))])
+    iota(ap("dtab", S_(B0, B0 + 2 * L)), [[0, 2 * L]], 0, 0)
+    iota(ap("pat", 0, ALL), [[0, 292]], int(CEN), 0)
+    iota(ap("pat", 0, S_(0, 292, 4)), [[0, 73]], int(CEN) + 1, 0)
+    for p, a, n, w_ in ((1, 0, 8, 288), (2, B0, 4, 256)):
+        iota(ap("pat", p, S_(0, w_)), [[1, w_]], a, w_)
+        dma([(pap("dtab", row(8 + t), S_(a, a + n * w_)), pap("pat", S_(0, 8 * n), 0, S_(4 - t, 4 - t + w_))) for t in range(R)] +
+            [(pap("dtab", S_(16 * g + 11, 16 * g + 12), S_(a, a + n * w_)), pap("pat", S_(0, n), p, S_(0, w_))) for g in range(8)])
     mm([(P(3, S_(0, 144)), wsl("we", E16, r), ap("xx", S_(144 * r, 144 * r + 144))) for r in range(16)])
-    lin(ap("sxc", ALL), P(3, S_(0, 144)), scale=1.0 / 16)
+    lin(ap("sxc", ALL), P(3, S_(0, 144)), scale=1.0 / 16, bias=-120.0)
     dma([(pap("dtab", row(7), S_(0, B0)), ap("sxc", ALL))])
     for t in range(R):
-        lin(xv(t), ap("xx", vcols(t)), eng="G" if t else "VA")
+        lin(xv(t), ap("xx", vcols(t)), eng="G" if t else "VAG")
+    for t in range(R):
+        suitors(t)
     for t in range(R):
         mm([(P(1, S_(32 * t, 32 * t + 32)), wsl("we", EW + t, r), ap("nb", t, S_(r, L, 16))) for r in range(16)])
-    mm([(P(1, S_(128, 224)), wsl("we", E16, r), ap("nb", ALL, S_(r, L, 16))) for r in range(16)])
+    mm([(P(1, S_(128 + 32 * t + b, 160 + 32 * t, 4)), ap("nb", t, S_(b, L, 4)), ap("w8", W16, ALL)) for t in range(R) for b in range(4)])
     copy(ap("sa", 0, ALL), P(1, S_(0, 96)))
-    ts(ap("sxw", 0, ALL), P(1, S_(128, 160)), 32640.0, A.add)
-    ts(ap("sxw", S_(1, R), ALL), P(1, S_(160, 224)), 32632.0, A.add)
+    lin(ap("sxw", 0, ALL), P(1, S_(128, 160)), bias=32640.0)
+    lin(ap("sxw", S_(1, R), ALL), P(1, S_(160, 224)), bias=32632.0)
     ts(ap("sa", 1, ALL), ap("sa", 0, ALL), 2047, A.bitwise_and)
     copy(ap("su", S_(0, R), ALL), ap("sa", 1, ALL))
     for t in range(R):
@@ -390,13 +413,6 @@ def build(model=None):
         if t == 2:
             push(ap("rx2", S_(0, B0)), ap("xx", S_(0, B0)), -3, ("names", 2))
 
-    cnt = {}
-
-    def nxt(n, m, late=0):
-        k = cnt.get((n, late), 0)
-        cnt[(n, late)] = k + 1
-        return m + k % late if late else k % m
-
     def pos(t, b, j, es):
         return P(b + t % 2, S_(j, L, 8)) if len(es) == 2 else P(b + t % 2, S_(j + 8 * es[0], L, 16))
 
@@ -404,20 +420,12 @@ def build(model=None):
         return S_(32 * es[0], 32 * es[-1] + 32)
 
     def names_static(t, js, es, late=False):
-        s = nxt("cc", NCC, 3 * late)
-        prs, nums = [], []
         for i, j in enumerate(js):
-            g = nxt("g1", NG1, 1 * late)
+            g = nxt("g1", NG1)
             for e in es:
-                lin(ap("g1", g, S_(L * e, L * e + L)), ind(ap("ki", ALL), o1(t, j, e)), bias=-CEN)
-                ops[-1]["extra"] = LEAD[t] * (PIECES[t][j] > 1)
-            pj = [(ap("cc", s, S_(64 * i + 32 * e, 64 * i + 32 * e + 32)), pap("g1", row((kof(t, j, e) + t) % 16), g, S_(L * e, L * e + L))) for e in es]
-            dma(pj)
-            nums += [(pos(t, 2, j, (e,)), IH, pj[n][0]) for n, e in enumerate(es)]
-        mark[("late" if late else "names", t)] = len(ops) - 1
-        c, n = 16 * t + 2 * js[0] + es[0], 32 * len(es) * len(js)
-        ts(ap("cu", S_(c, c + n // 32), ALL), ap("cc", s, S_(32 * es[0], 32 * es[0] + n)), CEN, A.add)
-        numbers(t, nums)
+                lin(ap("g1", g, S_(L * e, L * e + L)), ind(ap("ki", ALL), o1(t, j, e)))
+            dma([(cu(t, j, e), pap("g1", row((kof(t, j, e) + t) % 16), g, S_(L * e, L * e + L))) for e in es])
+        mark[("names", t)] = len(ops) - 1
 
     def names_pe(t, j, es, late=True):
         s, b, n = nxt("gh", 3), 7 if t == 1 else 6 + j % 2, 32 * len(es)
@@ -425,79 +433,53 @@ def build(model=None):
             kr = (kof(t, j, e) + t) % 16
             lin(ap("gh", s, i, ALL), ind(kk(0, B0 + L * t) if late else ap("ki", ALL), o1(t, j, e)), scale=mk(kr), bias=mk(16 + kr))
         mm([(P(b, S_(0, n)), wsl("weh", 0, r), ap("gh", s, S_(0, len(es)), S_(32 * r, 32 * r + 32))) for r in range(16)])
-        c = 16 * t + 2 * j + es[0]
-        ts(ap("cu", S_(c, c + len(es)), ALL), P(b, S_(0, n)), CEN, A.add)
+        lin(cu(t, j, es[0], 0, n), P(b, S_(0, n)), bias=CEN)
         mark[("late" if late else "names", t)] = len(ops) - 1
-        s = nxt("cc", NCC, 3 * late)
-        lin(ap("cc", s, S_(0, n)), P(b, S_(0, n)))
-        nums = []
-        for i, e in enumerate(es):
-            c = ap("cc", s, S_(32 * i, 32 * i + 32))
-            if t and kof(t, j, e) == 8:
-                mark[("c8", t)] = c
-            else:
-                nums.append((pos(t, 2, j, (e,)), IH, c))
-        numbers(t, nums)
 
     def halves(t, kinds):
         return [(j, tuple(e for e in BOTH if m[e] in kinds)) for q in DYN[t] for j, m in q if set(m) & set(kinds)]
 
-    def terms(t, j, es, lst):
-        ee = S_(es[0], es[-1] + 1)
-        for w_, i, n, s in lst:
-            mm([(pos(t, 0, j, es), wsl(w_, i, r), ap(n, s, S_(r, L, 16), ee)) for r in range(16)], ("k", t))
+    def sums(b, t, j, e, src, w_):
+        return [(P(b + t % 2, S_(16 * c + j + 8 * e, L, 64)), src(c), ap("w8", w_, ALL)) for c in range(4)]
 
-    place = {}
+    def features(t, j, es, late=False, hold=False):
+        s = nxt("rb", NB, LB * late)
+        for i, e in enumerate(es):
+            z = L * (2 * s + i)
+            for ls, off in pieces(t, j, e, PIECES[t][j]):
+                tt(ap("rb", S_(z + ls.start, z + ls.stop)), ind(ap("xx", S_(0, B0 + L * t * late)), off), ap("nb", t, ls), A.min)
+                if hold:
+                    ops[-1]["after"].append(mark["named"])
+            mm(sums(0, t, j, e, lambda c: ap("rb", S_(z + c, z + L, 4)), WM32), ("k", t))
 
-    def score_quad(t, js, parts):
-        late = not isinstance(js[0], int)
-        quad = js if late else [(j, "MM") for j in js]
-        wd = {"M": B0, "L": B0 + L * t}
-        if parts in "fpF":
-            for j, m in quad:
-                if parts != "F" and (PIECES[t][j] > 1 and HOLD) != (parts == "p"):
-                    continue
-                if (t, j) not in place:
-                    place[(t, j)] = nxt("rb", NRB, 2 * LATE * late)
-                rs = place[(t, j)]
-                for e in BOTH:
-                    if m[e] == ("L" if parts == "F" else "M"):
-                        for ls, off in pieces(t, j, e, PIECES[t][j]):
-                            tt(ap("rb", rs, ls, e), ind(ap("xx", S_(0, wd[m[e]])), off), ap("nb", t, ls), A.min)
-                            if parts == "p":
-                                ops[-1]["after"].append(mark["named"])
-                if ("L" in m) == ("F" in parts):
-                    terms(t, j, tuple(e for e in BOTH if m[e] != "W"), [("we", EM32, "rb", rs)])
-            return
-        for j, m in quad:
-            es = tuple(e for e in BOTH if (m[e] == "M") == (parts == "b"))
-            if not es:
-                continue
-            if (t, j, "b") not in place:
-                place[(t, j, "b")] = nxt("gd", NGD, 2 * LATE * late), nxt("db", NDB, 2 * LATE * late)
-            g, ds = place[(t, j, "b")]
-            for e in es:
-                if m[e] == "W":
-                    lin(ap("gd", g, ALL, e), ind(kk(0, B0 + L * t), cu(t, j, e)), scale=c1(GS2), bias=c1(GB))
-                    mark[("d8", t)] = (j, e, ds)
-                else:
-                    lin(ap("gd", g, ALL, e), ind(ap("dtab", S_(0, wd[m[e]])), cu(t, j, e)), scale=c1(GS), bias=c1(GB))
-            b, ee, w_ = 4 + nxt("pb", 2), S_(es[0], es[-1] + 1), 256 * len(es)
-            mm([(P(b, S_(0, w_)), c, ap("gd", g, S_(h, L, 2), ee)) for h, c in enumerate((C0, C1S))])
-            n = HALVES[t] if parts == "b" and len(es) == 2 else 1
-            for q in range(n):
-                ls = S_(256 // n * q, 256 // n * (q + 1))
-                tt(ap("db", ds, ls, ee), P(b, S_(w_ // n * q, w_ // n * (q + 1))), ap("dv", t % 2, ls, ee), A.is_equal)
-            es = tuple(e for e in es if m[e] != "W")
-            if es:
-                terms(t, j, es, [("weh", 1, "gd", g)])
-                mm(barred(pos(t, 0, j, es), ds, es), ("k", t))
+    def blood(t, j, es, late=False, asked=False):
+        n, g, q, b = len(es), nxt("gd", NG, LG * late), nxt("eq", NQ, LQ * late), bank(t)
+        whole = n == 2 and not late and j in WHOLE[t]
+        if whole:
+            lin(ap("gd", g, ALL), ind(ap("dtab", S_(0, B0)), cu(t, j, 0, 0, 64)), bias=-CEN)
+        for i, e in enumerate(es):
+            if not whole:
+                lin(ap("gd", g, S_(L * i, L * i + L)), ind(ap("dtab", S_(0, B0 + L * t * late)), cu(t, j, e)), bias=-CEN)
+            blocks = [ap("gd", g, S_(L * i + c, L * i + L, 4)) for c in range(4)]
+            mm([(P(b, S_(n * c + i, 192 * n, 4 * n)), blocks[c], WV) for c in range(4)], ("u", t, j, es))
+            if not asked:
+                mm(sums(0, t, j, e, lambda c: blocks[c], WKEY + t), ("k", t))
+            mm(sums(2, t, j, e, lambda c: blocks[c], WNUM), ("c", t))
+        w_ = 32 * n
+        tt(ap("eq", q, S_(0, 6 * w_)), P(b, S_(0, 6 * w_)), ap("sv", t, S_(0, 384, 2 // n)), A.is_equal)
+        if asked:
+            mark[("d8", t)] = (j, es[0], g, q)
+        else:
+            mm([(pos(t, 0, j, es), IBAR, ap("eq", q, S_(w_ * a, w_ * a + w_))) for a in range(6)], ("k", t))
 
-    def barred(o, ds, es):
-        return [(o, wsl("we", EBAR, 2 * r), ap("db", ds, S_(r, 256, 8), S_(es[0], es[-1] + 1))) for r in range(8)]
+    def turned(i):
+        return ap("zz", i, S_(3, 35, 4), ALL)
+
+    def listed(o, i, w_):
+        return [(o, ap("zz", i, S_(3 - a, 35 - a), ALL), ap("mb", w_, S_(a, 128, 4))) for a in range(4)]
 
     def pieces(t, j, e, n):
-        return [(S_(L // n * q, L // n * (q + 1)), ap("cu", 16 * t + 2 * j + e, S_(32 // n * q, 32 // n * (q + 1)))) for q in range(n)]
+        return [(S_(L // n * q, L // n * (q + 1)), cu(t, j, e, 32 // n * q, 32 // n * (q + 1))) for q in range(n)]
 
     def least(t):
         kb, cb_ = t % 2, 2 + t % 2
@@ -508,47 +490,36 @@ def build(model=None):
         scan(ap("sc2", ALL), ap("uu", ALL), P(cb_), A.mult, A.max)
         tt(sm(13), ap("sc1", ends), ap("sxw", t, ALL), A.add)
         ts(sm(3), ap("sc2", ends), MAGIC * 4096, A.add, -MAGIC * 4096, A.add)
-        ts(sm(0), sm(13), 100000.0, A.is_gt, 4096.0, A.mult)
-        tt(sm(15), ap("sc2", ends), sm(3), A.subtract)
-        tt(sm(14) if t else ap("m16", ALL), sm(15), sm(0), A.add)
+        ts(sm(0) if t else turned(2), sm(13), 100000.0, A.is_gt, 4096.0, A.mult)
+        tt(sm(15) if t else turned(0), ap("sc2", ends), sm(3), A.subtract)
         if t:
-            j, e, ds = mark[("d8", t)]
-            ts(sm(3), sm(13), 100000.0, A.min)
-            tt(sm(16), mark[("c8", t)], sm(14), A.subtract)
-            copy(ap("mi", 0, ALL), cu(t, j, e))
-            ts(ap("mi", 1, ALL), ap("mi", 0, ALL), 3, A.bitwise_and)
-            ts(ap("mf", ALL), ap("mi", 1, ALL), float(t), A.is_equal, BAR, A.mult)
+            j, e = mark[("d8", t)][:2]
+            ts(sm(1), sm(13), 100000.0, A.min)
+            lin(sm(22), pos(t, 2, j, (e,)), bias=4096.0 * (j + 8 * e) - 65536.0)
+            tt(sm(16), sm(22), sm(0), A.subtract)
 
     def score_asked(t):
-        j, e, ds = mark[("d8", t)]
-        o = P(2 + (t - 1) % 2, S_(0, 32))
-        mm([(o, IB, ap("mf", ALL))] + barred(o, ds, (e,)), ("x", t))
+        j, e, g, q = mark[("d8", t)]
+        ob = 2 + (t - 1) % 2
+        o = P(ob, S_(0, 32))
+        mm([(o, IBAR, ap("eq", q, S_(32 * a, 32 * a + 32))) for a in range(6)] +
+           [(P(ob, S_(c, 32, 4)), ap("gd", g, S_(c, L, 4)), ap("w8", WMOD + t, ALL)) for c in range(4)], ("x", t))
         tt(ap("bb", 0, ALL), ind(ap("xx", S_(0, B0 + L * t)), cu(t, j, e)), xv(t), A.subtract)
         ts(ap("bb", 1, ALL), ap("bb", 0, ALL), 0.0, A.min)
-        for i, w_ in enumerate((E16, EM32)):
-            mm([(o, wsl("we", w_, r), ap("bb", i, S_(r, L, 16))) for r in range(16)], ("x", t))
-        tt(sm(17), o, sm(3), A.is_lt)
+        for i in BOTH:
+            mm([(P(ob, S_(c, 32, 4)), ap("bb", i, S_(c, L, 4)), ap("w8", i, ALL)) for c in range(4)], ("x", t))
+        tt(sm(17), o, sm(1), A.is_lt)
+        tt(sm(14), o, sm(1), A.is_ge)
         tt(sm(19), o, sm(13), A.min)
         tt(sm(18), sm(17), sm(16), A.mult)
-        tt(ap("m16", ALL), sm(14), sm(18), A.add)
+        tt(turned(0), sm(15), sm(14), A.mult)
+        tt(turned(2), sm(18), sm(0), A.add)
 
     def opens(t, which):
         if which == "k":
             mm([(P(t % 2), IB, ap("kc", t % 2, ALL))] + [(pos(t, 0, j, es), IB, ap("barc", ALL)) for j, es in halves(t, "W")], ("k", t))
         else:
             mm([(P(2 + t % 2), IB, ap("kp", ALL))], ("c", t))
-            mark[("open", t)] = True
-            numbers(t, [])
-
-    held = [[], [], []]
-
-    def numbers(t, nums):
-        held[t].append(nums)
-        if ("open", t) in mark:
-            for x in held[t]:
-                if x:
-                    mm(x, ("c", t))
-            del held[t][:]
 
     def sm(i, *ix):
         return ap("sm", i, *(ix if ix else (ALL,)))
@@ -569,9 +540,10 @@ def build(model=None):
         for c in (KV, WEDV, ASKV):
             lin(ap("cb", c), src, eng="G")
         iota(ap("vv", ALL), [[4, L]], t, 0)
-        dma([(pap("kk", row(7), S_(0, OFF)), pap("nv", row(7), t, ALL)), (pap("kk", row(6), S_(0, OFF)), pap("vv", row(6), ALL))])
-        dma([(pap("cb", row(7), WEDV), pap("nv", row(7), t, ALL)), (pap("cb", row(9 + t), ASKV), pap("nv", row(7), t, ALL))])
-        dma([(pap("cb", row(0), CHILD), pap("vv", row(0), ALL))] + [(pap("cb", row(j), CHILD), pap("nv", row(j), t, ALL)) for j in (6, 7)] +
+        iota(ap("nv", t % 2, ALL), [[1, L]], B0 + L * t, 0)
+        dma([(pap("kk", row(7), S_(0, OFF)), pap("nv", row(7), t % 2, ALL)), (pap("kk", row(6), S_(0, OFF)), pap("vv", row(6), ALL))])
+        dma([(pap("cb", row(7), WEDV), pap("nv", row(7), t % 2, ALL)), (pap("cb", row(9 + t), ASKV), pap("nv", row(7), t % 2, ALL))])
+        dma([(pap("cb", row(0), CHILD), pap("vv", row(0), ALL))] + [(pap("cb", row(j), CHILD), pap("nv", row(j), t % 2, ALL)) for j in (6, 7)] +
             [(pap("cb", row(b), CHILD), pap("cb", row(a), KV)) for a, b in ((0, 2), (1, 3), (7, 8))])
 
     def answer(t):
@@ -580,24 +552,28 @@ def build(model=None):
 
     def tail(t):
         n0 = B0 + L * t
-        thr = c1(TH) if t == 0 else c1(THR + t)
         ends = S_(15, L, 16)
         kb, cb_ = t % 2 if t else 6, 2 + t % 2
-        key = sm(19 if t else 13)
-        ts(sm(1), key, thr, A.subtract, 8192.0, A.mult)
-        tt(sm(2), sm(1), ap("ia", 1, ALL), A.max)
+        tt(turned(1), sm(19 if t else 13), ap("tht", 3 if t else 0, ALL), A.is_gt)
+        LM, LF = P(cb_, S_(64, 96)), P(cb_, S_(96, 128))
+        last = t + 1 == R
+        mm(listed(LM, 0, 0) + listed(LM, 2, 0))
+        mm([(LF, IB, ap("itc", 2, ALL))] * (not last) + listed(LF, 1, 1))
         m16 = ap("m16", ALL)
-        ts(su(MU), m16, n0 - 1 - CEN, A.min, CEN, A.add)
-        ts(sm(20), m16, n0 - 1 - CEN, A.min, CEN, A.add)
-        tt(sm(4), sm(20), sm(2), A.min)
-        ts(su(I1), sm(4), float(OFF), A.add)
+        copy(m16, LM)
+        ts(su(MU), LM, n0 - 1 - CEN, A.min, CEN, A.add)
+        ts(sm(20), LM, n0 - 1 - CEN, A.min, CEN, A.add)
+        if not last:
+            tt(sm(4), LF, sm(20), A.min)
+            ts(su(I1), sm(4), float(OFF), A.add)
         mm([(P(6), IB, ap("dm0", ALL))], ("d0", t))
         mm([(P(6, S_(r + 1, L, 16)), ap("ll", r, ALL), m16) for r in range(15)], ("d0", t))
-        mm([(P(7, S_(0, 272, 17)), ZB, ap("rs1", S_(0, 16)))], ("d1", t))
+        mm([(P(7, S_(0, 272, 17)), IB, ap("rs1", S_(1, 17)))], ("d1", t))
         mm([x for r in range(16) for x in ((P(7, S_(r + 1, 272, 17)), ap("rr", r, ALL), ap("m16", S_(0, 32, 2))),
                                            (P(7, S_(r + 1, 272, 17)), NI64, ap("m16", S_(1, 32, 2))))], ("d1", t))
         lin(ap("km", ALL), ind(kk(0, n0), su(MU)), scale=c1(N67))
-        lin(ap("val", ALL), ind(kk(-OFF, n0), su(I1)))
+        if not last:
+            lin(ap("val", ALL), ind(kk(-OFF, n0), su(I1)))
         lin(ap("xm16", ALL), ind(ap("xx", S_(0, n0)), su(MU)), bias=-0.5)
         scan(ap("sc2", ALL), P(6), ap("rs0", ALL), A.mult, A.add)
         scan(ap("sd1", ALL), P(7, S_(0, 272)), ap("rs1", ALL), A.mult, A.add)
@@ -605,24 +581,35 @@ def build(model=None):
         vop("transpose", sm(21), [sm(20)], [sm(20)])
         dma([(pap("cb", S_(16 * h + 1, 128, 32), CHILD), sm(21, S_(16 * h, 16 * h + 16))) for h in BOTH])
         dma([(pap("cb", row(6), WEDV), pap("cb", row(1), CHILD))])
-        mm([(P(kb), HIH, ap("xm16", ALL)), (P(kb), HIB, xv(t))])
+        mm([(P(kb), HIB, ap("xm16", ALL)), (P(kb), HIB, xv(t))])
         for a in range(0, L, MEAN):
             ts(ap("nb", t, S_(512 + a, 512 + a + MEAN)), P(kb, S_(a, a + MEAN)), MAGIC, A.add, -MAGIC, A.add)
         if t + 1 < R:
             dma([(ap("xx", S_(n0, n0 + L)), ap("nb", t, S_(512, 1024)))])
-            blood_rows(t, [pap("cb", row(j), CHILD) for j in range(6)], lambda a, b: ap("nb", t, S_(512 + a, 512 + b)))
+            sum_row(t, lambda a, b: ap("nb", t, S_(512 + a, 512 + b)))
         ts(sm(5), ap("sc2", ends), 0.0, A.is_equal, 8192.0, A.mult)
         ts(sm(6, S_(0, 16)), ap("sd1", S_(16, 272, 17)), 0.0, A.is_equal, 8192.0, A.mult)
         tt(sm(7), m16, sm(5), A.add)
-        tt(sm(6, S_(16, 32)), sm(7, S_(1, 32, 2)), sm(6, S_(0, 16)), A.add)
-        ts(su(SO, S_(1, 32, 2)), sm(6, S_(16, 32)), c1(DO), A.min, CEN, A.add)
-        ts(su(SO, S_(0, 32, 2)), sm(7, S_(0, 32, 2)), c1(DE), A.min, CEN, A.add)
-        for a in range(15, -1, -1):
-            tt(ind(kk(0, W + 32), su(SO, S_(2 * a, 2 * a + 2))), ap("val", S_(32 * a, 32 * a + 32)), ap("km", S_(32 * a, 32 * a + 32)), A.max)
-        tt(ap("li", 0, ALL), ind(kk(0, n0), su(MU)), ap("nv", t, ALL), A.not_equal)
+        ts(su(SO, S_(0, 32, 2)), sm(7, S_(0, 32, 2)), c1(DE + 2 * last), A.min, CEN, A.add)
+        tt(sm(7, S_(1, 32, 2)), sm(7, S_(1, 32, 2)), sm(6, S_(0, 16)), A.add)
+        ts(su(SO, S_(1, 32, 2)), sm(7, S_(1, 32, 2)), c1(DO + 2 * last), A.min, CEN, A.add)
+        if not last:
+            for a in range(15, -1, -1):
+                tt(ind(kk(0, W + 32), su(SO, S_(2 * a, 2 * a + 2))), ap("val", S_(32 * a, 32 * a + 32)), ap("km", S_(32 * a, 32 * a + 32)), A.max)
+            tt(ap("li", 0, ALL), ind(kk(0, n0), su(MU)), ap("nv", t % 2, ALL), A.not_equal)
+        else:
+            tab = [ap("rb", S_(3584 * h, 3584 * h + n0 + 48)) for h in BOTH]
+            for a in range(7, -1, -1):
+                for h in BOTH:
+                    copy(ind(tab[h], su(SO, S_(16 * h + 2 * a, 16 * h + 2 * a + 2))), ap("stp", S_(256 * h + 32 * a, 256 * h + 32 * a + 32)))
+            tt(sm(4), LF, sm(7), A.add)
+            ts(su(I1), sm(4), n0 + 40 - CEN, A.min, CEN, A.add)
+            tt(ap("uu", S_(0, 256)), ind(tab[0], su(I1, S_(16, 32))), ap("stp", S_(256, L)), A.max)
+            tt(ap("li", 0, S_(0, 256)), ind(tab[0], su(I1, S_(0, 16))), ap("stp", S_(0, 256)), A.not_equal)
+            tt(ap("li", 0, S_(256, L)), ind(tab[1], su(I1, S_(16, 32))), ap("uu", S_(0, 256)), A.not_equal)
         scan(ap("li", 1, ALL), ap("li", 0, ALL), ap("li", 0, ALL), A.add, A.max)
         Z, Y = P(7, S_(320, 352)), P(7, S_(352, 384))
-        mm([(P(7, S_(320, 384)), IH, ap("itc", ALL, ALL))] + [(P(7, S_(320, 384)), wsl("ws", 7, r), ap("li", ALL, S_(r, L, 16))) for r in range(16)])
+        mm([(P(7, S_(320, 384)), IB, ap("itc", S_(0, 2), ALL))] + [(P(7, S_(320, 384)), wsl("ws", 7, r), ap("li", ALL, S_(r, L, 16))) for r in range(16)])
         ts(sm(8), Y, 1.0 / 512, A.mult)
         tt(sm(9), Z, sm(8), A.min)
         ts(su(ONEW), Z, 512.0, A.mult)
@@ -636,24 +623,32 @@ def build(model=None):
         scan(ap("bs", ALL), P(kb, S_(0, 256)), ap("seg", ALL), A.max, A.min)
         copy(su(RO, S_(0, 8)), ap("bs", S_(31, 256, 32)))
         tt(ap("fl", ALL), ind(sm(8), su(RO, S_(0, 8))), ap("srow", ALL), A.is_le)
-        mm([(P(cb_, S_(0, 8)), I16H, ap("bs", S_(31, 256, 32)))] +
+        mm([(P(cb_, S_(0, 8)), I16, ap("bs", S_(31, 256, 32)))] +
            [(P(cb_, S_(0, 8)), wsl("weh", 0, r), ap("fl", S_(r, 128, 16))) for r in range(16)])
         ts(su(RO, S_(8, 16)), P(cb_, S_(0, 8)), 511.0, A.min)
         copy(ap("du", ALL), ind(ap("rk", t, ALL), su(RO, S_(8, 16))))
         lin(ap("xs", ALL), ind(xv(t), su(RO, S_(8, 16))))
+        if last:
+            ts(sm(5), Z, 1.0, A.is_ge, 4096.0, A.mult)
+            tt(sm(6), sm(5), ap("ia", 1, ALL), A.add)
+            tt(sm(5), sm(6), sm(20), A.max)
+            copy(su(SO), sm(5))
+            for a in range(0, L, WED):
+                tt(ind(kk(0, W), su(SO, S_(a // 16, (a + WED) // 16))), kk(a - OFF, a + WED - OFF), ap("km", S_(a, a + WED)), A.max)
         lin(kk(t, 2048, 4), ind(ap("cb", ALL), su(OVC)))
         lin(kk(n0, n0 + L), ind(ap("cb", S_(0, 1024)), su(ONEW)))
         if t + 1 < R:
+            dma([(pap("dtab", row(j), S_(n0, n0 + L)), kk(n0, n0 + L, 1, row(j))) for j in range(6)])
             mm([(P(6, S_(0, 1)), W7, ap("li", 1, S_(L - 1, L)))])
             ts(pc(4), P(6, S_(0, 1)), -1.0, A.mult, 4096.0, A.add)
             ts(pc(5), pc(4), 15, A.bitwise_and)
-            ts(c1(THR + t + 1), pc(5), 16.0, A.mult, c1(TH + t + 1), A.add)
+            lin(c1(ZC), pc(5), scale=16.0)
+            lin(ap("tht", 3, ALL), ap("tht", t + 1, ALL), bias=c1(ZC))
 
-    def blood_rows(t, rows, feats):
+    def sum_row(t, feats):
         n0, s = B0 + L * t, nxt("sxn", 2)
-        dma([(pap("dtab", row(j), S_(n0, n0 + L)), rows[j]) for j in range(6)])
         mm([(P(6, S_(64, 96)), wsl("we", E16, r), feats(32 * r, 32 * r + 32)) for r in range(16)])
-        lin(ap("sxn", s, ALL), P(6, S_(64, 96)), scale=1.0 / 16)
+        lin(ap("sxn", s, ALL), P(6, S_(64, 96)), scale=1.0 / 16, bias=-120.0)
         dma([(pap("dtab", row(7), S_(n0, n0 + L)), ap("sxn", s, ALL))])
 
     def stores(t):
@@ -682,7 +677,7 @@ def build(model=None):
             mm([(P(banks[b], S_(k, L, 8)), IB, ap("ga", S_(1024 * h + 8 * q + k, 1024 * h + 1024, 16))) for k in range(8)], ("a", t, b))
             act(ap("ra", S_(64 * h, 64 * h + 64), S_(8 * q, 8 * q + 8)), P(banks[b]), F.Abs, scale=128.0)
         o = P(7, S_(0, 128))
-        mm([(o, IH, ap("kq", ALL))], ("o", t))
+        mm([(o, IB, ap("kq", ALL))], ("o", t))
         for h in range(2):
             oh, byv = P(7, S_(64 * h, 64 * h + 64)), h in ASK_V[t]
             if byv:
@@ -701,59 +696,63 @@ def build(model=None):
         for u in range(t + 1, R):
             push(ap("rx%d" % u, S_(n0, n0 + L)), ap("xx", S_(n0, n0 + L)), -1 - u)
 
-    def suitors(t):
-        for s, c in ((2, 4), (t % 2, 0)):
-            for e in BOTH:
-                lin(ap("dv", s, ALL, e), ap("dtab", S_(t + c, 2048, 8)), eng="G")
-        dma([(pap("dv", row(j + 8), t % 2, ALL, ALL), pap("dv", row(j), 2, ALL, ALL)) for j in range(7)])
+    def names(t):
+        for js in QUADS[t]:
+            if js[0] in NAMES_PE[t]:
+                for j in js:
+                    names_pe(t, j, BOTH, False)
+            else:
+                names_static(t, js, BOTH)
+        for j, es in halves(t, "M"):
+            names_static(t, (j,), es)
+        bulk(t)
 
-    def statics(t, parts):
-        if "f" in parts:
-            opens(t, "k")
-            for js in QUADS[t]:
-                if js[0] in NAMES_PE[t]:
-                    for j in js:
-                        names_pe(t, j, BOTH, False)
-                else:
-                    names_static(t, js, BOTH)
-            for j, es in halves(t, "M"):
-                names_static(t, (j,), es)
-            bulk(t)
-        if "b" in parts:
-            suitors(t)
-            opens(t, "c")
-        for js in QUADS[t] + DYN[t]:
-            for x in parts:
-                score_quad(t, js, x)
+    def still(t, short):
+        return [(j, es) for j, es in [(j, BOTH) for js in QUADS[t] for j in js] + halves(t, "M") if (PIECES[t][j] > 1) == short]
 
-    statics(0, "fb")
+    opens(0, "k")
+    opens(0, "c")
+    names(0)
+    for j, es in still(0, False):
+        features(0, j, es)
+        blood(0, j, es)
     answer(0)
     prepare(0)
     least(0)
+    opens(1, "k")
+    opens(1, "c")
+    names(1)
+    opens(2, "k")
+    names(2)
     for t in range(R):
         if t == 0:
-            statics(1, "fb")
-            statics(2, "f")
+            for u in (1, 2):
+                for j, es in still(u, False):
+                    features(u, j, es)
         if t == 1:
-            statics(2, "b")
+            opens(2, "c")
         if t + 1 < R:
-            statics(t + 1, "p")
+            for j, es in still(t + 1, False) + still(t + 1, True):
+                blood(t + 1, j, es)
+            for j, es in still(t + 1, True):
+                features(t + 1, j, es, hold=True)
         tail(t)
         if t + 1 < R:
             prepare(t + 1)
             for j, es in halves(t + 1, "LW"):
                 names_pe(t + 1, j, es)
-            for q in DYN[t + 1]:
-                score_quad(t + 1, q, "B")
-                score_quad(t + 1, q, "F")
+            for j, es in halves(t + 1, "L"):
+                blood(t + 1, j, es, True)
+                features(t + 1, j, es, True)
+            for j, es in halves(t + 1, "W"):
+                blood(t + 1, j, es, True, True)
             least(t + 1)
         stores(t)
         ask(t)
         if t + 1 < R:
             score_asked(t + 1)
         if t + 2 < R:
-            n0 = B0 + L * t
-            blood_rows(t, [kk(n0, n0 + L, 1, row(j)) for j in range(6)], lambda a, b: ap("xx", S_(n0 + a, n0 + b)))
+            sum_row(t, lambda a, b: ap("xx", S_(B0 + L * t + a, B0 + L * t + b)))
     return ops
 
 
@@ -921,6 +920,85 @@ def search(ops, seed, tries, polish=0, nj=6, amp=1200.0, temp=60.0, temp2=20.0):
             if m < best:
                 best, keep = m, (j2, s2)
     order, start, fin, eng = schedule(*keep)
+
+    after = [[] for _ in range(n)]
+    for i in range(n):
+        for j, same, cj, raw in dep[i]:
+            after[j].append((i, same, cj))
+
+    def gap(line, s, c):
+        a, b = 0, len(line)
+        while a < b:
+            h = (a + b) // 2
+            if line[h][1] <= s:
+                a = h + 1
+            else:
+                b = h
+        while a < len(line) and line[a][0] < s + c:
+            s = max(s, line[a][1])
+            a += 1
+        return s, a
+
+    def sweep(seq, eng, k, back, choose):
+        cs, lt = others[k]
+        pre, post, lx, ls = MODELS[k][3], MODELS[k][4], MODELS[k][7], MODELS[k][8]
+        lines, eng = {e: [] for e in queues + "D"}, list(eng)
+        fin, at = [0.0] * n, [0.0] * n
+        for i in seq:
+            pick = None
+            for e in (cs[i] if choose and len(cs[i]) > 1 else (eng[i],)):
+                s, c = 0.0, cs[i][e]
+                if back:
+                    for j, same, cj in after[i]:
+                        x = fin[j] - lt[i] if same else fin[j] + (ls if cj and eng[j] == e else lx)
+                        if x > s:
+                            s = x
+                else:
+                    for j, same, cj, raw in dep[i]:
+                        x = fin[j] - lt[j] if same else fin[j] + (ls if cj and eng[j] == e else lx)
+                        if x > s:
+                            s = x
+                d = None
+                if moves[i]:
+                    w = lt[i] - pre - post
+                    if back:
+                        d = gap(lines["D"], s + post, w)
+                        s, a = gap(lines[e], d[0] + w + pre, c)
+                        f = s + c
+                    else:
+                        s, a = gap(lines[e], s, c)
+                        d = gap(lines["D"], s + c + pre, w)
+                        if e == "Y":
+                            s, a = gap(lines[e], d[0] - pre - c, c)
+                        f = max(d[0], s + c + pre) + w + post
+                else:
+                    s, a = gap(lines[e], s + lt[i] if back else s, c)
+                    f = s + c + (0.0 if back else lt[i])
+                x = f + (choose if e == "V" else 0.0)
+                if pick is None or x < pick[0]:
+                    pick = (x, e, s, a, c, f, d)
+            x, e, s, a, c, f, d = pick
+            lines[e].insert(a, (s, s + c))
+            if d:
+                lines["D"].insert(d[1], (d[0], d[0] + lt[i] - pre - post))
+            eng[i], fin[i], at[i] = e, f, s + c if back else s
+        return sorted(seq, key=lambda i: -at[i] if back else at[i]), eng
+
+    def total(order, eng):
+        return sum(replay(order, eng, k) * norm[k] for k in range(len(MODELS)))
+
+    best = cur = total(order, eng)
+    keep = (order, eng)
+    for it in range(SWEEPS):
+        k = rng.randint(0, len(MODELS))
+        o2, e2 = sweep(order[::-1], eng, k, True, BIAS[rng.randint(0, len(BIAS))])
+        o2, e2 = sweep(o2, e2, k, False, BIAS[rng.randint(0, len(BIAS))])
+        m = total(o2, e2)
+        if m <= cur + SLACK * (1 - it / SWEEPS) * float(rng.exponential()):
+            cur, order, eng = m, o2, e2
+            if m < best:
+                best, keep = m, (o2, e2)
+    order, eng = keep
 
     def run(order, eng, k, p, old):
         cs, lt = others[k]

import numpy as np
from concourse.mybir import dt, AluOpType, AxisListType, ActivationFunctionType

A = AluOpType
F = ActivationFunctionType
B0, L, R, NR = 2304, 512, 3, 8
W = B0 + R * L
DUM = B0 + 2 * L
OFF = L
CEN = 1920.0
MAGIC = 12582912.0
BAR = 262144.0
NG1, NG, LG, NB, LB, NQ, LQ = 8, 6, 3, 7, 2, 3, 3
f32, bf, f16, i32, u16 = "float32", "bfloat16", "float16", "int32", "uint16"
SB = {
    "ki": ([B0], i32), "kk": ([OFF + W + 32], f32), "xx": ([W], bf), "dtab": ([B0 + 2 * L], f32),
    "rk": ([R, L], f32), "qa": ([R, 32], u16), "of3": ([16, 96], u16), "kw3": ([16, R, 32], u16), "kv16": ([L], f16), "ws": ([8, 144], f16),
    "rx0": ([B0], bf), "rx1": ([B0 + L], bf), "rx2": ([B0 + 2 * L], bf),
    "cb": ([2048], f32), "nb": ([R, 1152], bf), "pkv": ([L], f32), "nv": ([2, L], f32), "vv": ([L], f32),
    "kvf": ([L], f32), "l67": ([2, 32], f32),
    "cu": ([R * L], u16), "kp": ([L], bf),
    "g1": ([NG1, 2 * L], u16), "gh": ([3, 2, L], f16),
    "gd": ([NG + LG, 2 * L], f16), "rb": ([(NB + LB) * 2 * L], bf), "eq": ([NQ + LQ, 384], bf), "sv": ([R, 384], f16),
    "zz": ([3, 36, 4], f16), "wd": ([48], f32), "wv": ([48], f16), "w8": ([10, 8], bf), "tht": ([4, 32], f32),
    "pat": ([3, 292], f32), "sxc": ([144], f32), "sxn": ([2, 32], f32),
    "bb": ([2, L], bf),
    "barc": ([32], bf), "sc0": ([128], f32), "sc1": ([L], f32), "sc2": ([L], f32), "uu": ([L], bf), "sd1": ([272], f32), "li": ([2, L], f16),
    "km": ([L], f32), "val": ([L], f32), "xm16": ([L], f16),
    "ga": ([2048], bf), "ra": ([128, 16], bf), "xs": ([128], bf), "du": ([128], u16),
    "sm": ([23, 32], f32), "si": ([2, 8], i32), "sa": ([2, 96], i32), "su": ([12, 32], u16), "m16": ([32], f16),
    "pc": ([8], i32), "col": ([48], f32), "ix": ([144], f32),
    "sxw": ([R, 32], f32),
    "ns": ([256], bf), "seg": ([256], bf), "bs": ([256], f16), "srow": ([128], f32), "fl": ([128], f16),
    "we": ([6, 144], bf), "weh": ([1, 144], f16), "rr": ([16, 128], f16), "ll": ([16, 128], f16),
    "mb": ([9, 128], bf), "blk": ([128], f32), "mask": ([32], f32),
    "kc": ([2, L], bf), "rs0": ([L], bf), "rstk": ([L], bf), "dm0": ([L], bf), "rs1": ([272], bf),
    "stp": ([L], bf), "ia": ([2, 32], f32), "itc": ([3, 32], f16), "kq": ([128], f16),
    "thi": ([4], i32), "thf": ([4], f32), "wi": ([4], i32), "l8": ([128], f32),
}
SCRATCH = {n: ("sbuf", [128] + s, d) for n, (s, d) in SB.items()}
for _b in range(8):
    SCRATCH["p%d" % _b] = ("psum", [128, 512], f32)
NDS = 140
SEMAPHORES = ["eV", "eA", "eP", "eG"] + ["q%d" % i for i in range(NDS)]
SHAPES = {n: v[1] for n, v in SCRATCH.items()}
SHAPES.update({"kin": [128, B0], "xf": [128, B0], "th": [8, R], "w": [128, R], "yk": [128, W], "yx": [128, R * L]})
WIDE = {n: (2 if v[2] in (bf, f16, u16) else 4) for n, v in SCRATCH.items()}

MODELS = [(0.9, 1.56, 3.8, 900.0, 400.0, 280.0, 3.5, 260.0, 170.0, 0.52, 100.0, 4000.0),
          (1.1, 2.0, 3.0, 800.0, 400.0, 300.0, 2.5, 240.0, 160.0, 0.51, 60.0, 2000.0),
          (1.1, 1.2, 5.5, 1000.0, 500.0, 300.0, 3.0, 300.0, 200.0, 0.55, 100.0, 6000.0),
          (0.9, 1.3, 2.5, 1300.0, 600.0, 220.0, 4.5, 290.0, 200.0, 0.51, 150.0, 8000.0)]
DPRE, DPOST = MODELS[0][3:5]
LAT_X, LAT_S = MODELS[0][7:9]
SEED, TRIES, POLISH, SHY, TOL, DEL = 0, 300, 52000, 20000.0, 200.0, 600.0
SWEEPS, SLACK, BIAS = 0, 500.0, (0.0, 1.0, 300.0, 1000.0)
LEAD = [0.0, 0.0, 0.0]
SOON = 15000.0
S_ = slice
ALL = slice(None)


def ap(n, *ix):
    return (n, (ALL,) + ix)


def pap(n, ps, *ix):
    return (n, (ps,) + ix)


def ind(win, off):
    return ("*", win, off)


def row(j):
    return S_(j, 128, 16)


_cache = {}


def region(a):
    key = repr(a)
    if key not in _cache:
        n, ix = a
        sh = SHAPES[n]
        ps = np.arange(sh[0])[ix[0]]
        tot = int(np.prod(sh[1:]))
        cs = np.arange(tot).reshape(sh[1:])[ix[1:]].reshape(-1)
        pm = sum(1 << int(p) for p in ps)
        bits = np.zeros(tot, np.uint8)
        bits[cs] = 1
        cm = int.from_bytes(np.packbits(bits, bitorder="little").tobytes(), "little")
        _cache[key] = (n, pm, cm, len(cs), len(ps))
    return _cache[key]


def flat(xs):
    out = []
    for x in xs:
        if isinstance(x, tuple):
            out += [x[1], x[2]] if x[0] == "*" else [x]
    return out


def kof(t, j, e):
    return (2 * j + e + (1 if t == 1 else 0)) % 16


BOTH = (0, 1)
QUADS = [[(0, 1), (2, 3), (4, 5), (6, 7)], [(0, 1), (4, 5), (6, 7)], [(0, 1), (6, 7)]]
NAMES_PE = [(0,), (), ()]
BATCH = [(0, 1), (1, 2), (2, 4)]
ASK_V = [(), (), (0,)]
DYN = [[], [((3, "LW"), (2, "LL"))], [((2, "LL"), (3, "LL")), ((4, "WM"), (5, "MM"))]]
PIECES = [[1] * 8, [1, 1, 1, 1, 4, 4, 4, 4], [1, 1, 1, 1, 4, 4, 4, 4]]
KVF = "G"
MEAN, WED = 256, 128
WHOLE = [(2, 3, 4, 5, 6), (), ()]
BANKS, DTE, XAT = [(4, 5, 6, 7), (4, 5), (4, 5)], "G", 0


def build(model=None):
    CY, GAM, SIG, DPRE, DPOST, DBW, DROW = (model or MODELS[0])[:7]
    PCY = CY * (model or MODELS[0])[9]
    ISSUE, FIRST = (tuple(model or MODELS[0]) + (60.0, 0.0))[10:12]
    ops = []

    mark = {}

    def add(alts, reads, writes, lat=0.0, kind="c", extra=None, after=None):
        ops.append({"alts": alts, "r": [region(x) for x in flat(reads)], "w": [region(x) for x in flat(writes)],
                    "lat": lat, "kind": kind, "extra": extra, "after": [mark[after]] if after else []})

    def split(out):
        return ([out[2]], [out[1]]) if out[0] == "*" else ([], [out])

    def vcost(out, ins, tt=False):
        if out[0] == "*":
            return 50 + region(out[2])[3] * 16 * SIG * CY
        n = region(out)[3]
        if ins[0][0] == "*":
            return 50 + n * GAM * CY
        if tt:
            f = 1.0 if any(x[0][0] == "p" and x[0][1:].isdigit() for x in ins) else 2.0
        else:
            f = 0.5 if all(WIDE[x[0]] == 2 for x in [out] + ins) else 1.0
        return max(64, n * f) * CY + 20

    def acost(out, in_):
        n = region(out)[3]
        return 65 + n * GAM * CY if in_[0] == "*" else max(64, n) * CY + 40

    def vop(name, out, args, ins, tt=False):
        r, w = split(out)
        add([("V", vcost(out, ins, tt), (name, [out] + args, {}))], r + [x for x in args if isinstance(x, tuple)], w)

    def copy(out, in_):
        vop("tensor_copy", out, [in_], [in_])

    def tt(out, a, b, op):
        vop("tensor_tensor", out, [a, b, op], [a, b], True)

    def ts(out, a, s1, op0, s2=None, op1=None):
        vop("tensor_scalar", out, [a, s1, s2, op0] + ([] if op1 is None else [op1]), [a])

    def memset(out, c):
        add([("V", max(64, region(out)[3] * WIDE[out[0]] / 4) * CY + 20, ("memset", [out, c], {}))], [], [out])

    def scan(out, d0, d1, op0, op1):
        vop("tensor_tensor_scan", out, [d0, d1, 0.0, op0, op1], [d0, d1])

    def actalt(out, in_, func, scale, bias):
        kw = {}
        if scale is not None:
            kw["scale"] = scale
        if bias is not None:
            kw["bias"] = bias
        return ("A", acost(out, in_), ("activation", [out, in_, func], kw))

    def act(out, in_, func, scale=None, bias=None):
        add([actalt(out, in_, func, scale, bias)], [in_, scale, bias], [out])

    def lin(out, in_, scale=None, bias=None, eng="VA"):
        alts = []
        if "A" in eng:
            alts.append(actalt(out, in_, F.Identity, scale, bias))
        if "V" in eng:
            if scale is None and bias is None:
                c = ("tensor_copy", [out, in_], {})
            elif scale is None:
                c = ("tensor_scalar", [out, in_, bias, None, A.add], {})
            elif bias is None:
                c = ("tensor_scalar", [out, in_, scale, None, A.mult], {})
            else:
                c = ("tensor_scalar", [out, in_, scale, bias, A.mult, A.add], {})
            alts.append(("V", vcost(out, [in_]), c))
        if "G" in eng:
            n = region(out)[3]
            alts.append(("G", 170 + 2 * CY * n, ("affine_select", [out, in_, [[0, n]], A.is_ge, 0.0, 0, 0], {})))
        add(alts, [in_, scale, bias], [out])

    def mm(lst, group=None):
        cost = sum(max(64, region(x[2])[3]) * (WIDE[x[2][0]] ** 2 / 4) * PCY for x in lst)
        add([("P", cost, ("mm", lst, {"group": group}))], [x[1] for x in lst] + [x[2] for x in lst], [x[0] for x in lst], lat=60.0)

    def iota(out, pat, base, cm, extra=None):
        kw = {} if SCRATCH[out[0]][2] == i32 else {"allow_small_or_imprecise_dtypes": True}
        add([("G", 130 + 2 * CY * region(out)[3], ("iota", [out, pat, base, cm], kw))], [], [out], extra=extra)

    def dma(pairs, q="Y", after=None, extra=None):
        by = sum(region(o)[3] * region(o)[4] * WIDE.get(o[0], 2 if o[0] == "yx" else 4) for o, i in pairs)
        rows = sum(max(16, region(o)[4], region(i)[4]) for o, i in pairs)
        add([(q, ISSUE * len(pairs), ("dma", pairs, {}))], [i for o, i in pairs], [o for o, i in pairs],
            lat=DPRE + DPOST + by / DBW + rows * DROW, kind="d", after=after, extra=extra)

    def push(dst, src, t, after=None):
        by = region(dst)[3] * 128 * WIDE[dst[0]]
        add([("G", 300.0 + ("push" not in mark) * FIRST, ("push", [dst, src, t], {"group": "push"}))], [src], [dst],
            lat=DPRE + DPOST + by / DBW + 128 * DROW, kind="p", after=after, extra=None if "push" in mark else SOON)
        mark["push"] = True

    def P(b, *ix):
        return ap("p%d" % b, *(ix if ix else (ALL,)))

    def c1(i):
        return ap("col", S_(i, i + 1))

    def mk(k):
        return ap("mask", S_(k, k + 1))

    def wsl(name, i, r):
        return ap(name, i, S_(15 - r, 143 - r))

    def vcols(t):
        return S_(t, 2048, 4)

    def kk(a, b, step=1, ps=ALL):
        return pap("kk", ps, S_(OFF + a, OFF + b, step))

    def xv(t):
        return ap("nb", t, S_(0, L))

    def pc(i):
        return ap("pc", S_(i, i + 1))

    for a, b in ((0, 1024), (1024, 2048), (2048, B0)):
        dma([(ap("ki", S_(a, b)), ap("kin", S_(a, b)))], extra=6e6 - 100.0 * a)
    if not XAT:
        dma([(ap("xx", S_(0, B0)), ap("xf", ALL))])
    dma([(pap("thi", S_(0, 8), S_(0, R)), ap("th", ALL)), (ap("wi", S_(0, R)), ap("w", ALL))])

    PP, PM, PG, Q4, C15, N67, CI, ZC, S16, TMP, XC, _1, _2, KC, _1, _2, DE, DO = range(18)
    WF, P64 = 28, 34
    iota(pc(0), [[0, 1]], 0, 1, 1e6)
    iota(ap("ix", ALL), [[1, 144]], 0, 0, 1e6)
    ts(pc(1), pc(0), 15, A.bitwise_and)
    ts(pc(2), pc(0), 4, A.arith_shift_right)
    ts(pc(3), pc(0), 3, A.bitwise_and)
    copy(ap("col", S_(0, 4)), ap("pc", S_(0, 4)))
    lin(c1(C15), c1(PG), scale=16.0, bias=15.0)
    ts(ap("mask", S_(0, 16)), ap("ix", S_(0, 16)), c1(PM), A.is_equal)
    lin(ap("mask", S_(16, 32)), ap("mask", S_(0, 16)), scale=-CEN)
    ts(c1(TMP), mk(6), mk(7), A.add, -1.0, A.mult)
    lin(c1(N67), c1(TMP), bias=1.0)
    for i, c in enumerate((W, W + 16, DUM, DUM + 16)):
        lin(c1(DE + i), c1(PM), bias=c - CEN)
    lin(c1(CI), c1(PM), scale=8.0, bias=c1(PG))
    lin(c1(S16), mk(7), scale=16.0)
    lin(ap("col", S_(XC, XC + R)), ap("mask", S_(8, 8 + R)), scale=BAR)
    lin(ap("col", S_(KC, KC + R)), ap("col", S_(XC, XC + R)), bias=c1(S16))
    WD, WV = ap("wd", ALL), ap("wv", ALL)
    ts(WD, ap("ix", S_(0, 48)), c1(CI), A.is_equal)
    lin(WV, WD)
    W16, WM32, WNUM, WKEY, _3, _4, WMOD, _5, _6, W1 = range(10)
    ts(ap("w8", W1, ALL), ap("ix", S_(0, 8)), c1(PG), A.is_equal)
    for i, c in [(W16, 16.0), (WM32, -32.0), (WNUM, mk(11))] + [(WKEY + t, c1(KC + t)) for t in range(R)] + [(WMOD + t, c1(XC + t)) for t in (1, 2)]:
        lin(ap("w8", i, ALL), ap("w8", W1, ALL), scale=c)
    lin(c1(P64), c1(PM), scale=64.0)
    copy(ap("col", S_(WF, WF + R)), ap("wi", S_(0, R)))
    E16, EMX, EY, EW = range(4)
    ts(ap("weh", 0, ALL), ap("ix", ALL), c1(C15), A.is_equal)
    for i, c in [(E16, 16.0), (EMX, 4096.0), (EY, -2048.0), (EW, c1(WF)), (EW + 1, c1(WF + 1)), (EW + 2, c1(WF + 2))]:
        lin(ap("we", i, ALL), ap("weh", 0, ALL), scale=c)
    for k in list(range(BATCH[-1][1])) + [7]:
        lin(ap("ws", k, ALL), ap("weh", 0, ALL), scale=mk(k))
    memset(ap("rr", ALL), 1.0 / 64)
    add([("G", 170 + 2 * CY * 2048, ("affine_select", [ap("rr", ALL), ap("rr", ALL), [[-1, 16], [-16, 8], [0, 16]], A.is_equal, 0.0, 0, 1], {}))],
        [ap("rr", ALL)], [ap("rr", ALL)])
    add([("G", 170 + 2 * CY * 2048, ("affine_select", [ap("ll", ALL), ap("rr", ALL), [[0, 16], [-1, 128]], A.not_equal, -1.0 / 64, 0, 1], {}))],
        [ap("rr", ALL)], [ap("ll", ALL)])
    IB, I8K, NIB, HIB, IBAR, NI64, I16, R7, W7 = [ap("mb", i, ALL) for i in range(9)]
    ix128 = ap("ix", S_(0, 128))
    ts(IB, ix128, c1(PP), A.is_equal)
    for m, c in [(NIB, -1.0), (HIB, 0.5), (IBAR, BAR), (NI64, -1.0 / 64), (I16, 16.0), (I8K, 8192.0)]:
        lin(m, IB, scale=c)
    memset(ap("zz", ALL, ALL, ALL), 0.0)
    lin(W7, ix128, scale=0.0, bias=mk(7))
    lin(R7, ap("rr", 7, ALL), scale=-4096.0)
    memset(ap("barc", ALL), BAR)
    iota(ap("kc", 0, ALL), [[0, 32], [1, 2], [2, 8]], 0, 0)
    iota(ap("uu", ALL), [[0, 32], [1, 16]], 0, 0)
    iota(ap("kc", 1, ALL), [[0, 32], [1, 2], [2, 8]], 1, 0)
    memset(ap("kc", 1, S_(15, L, 16)), 0.0)
    ts(ap("dm0", ALL), ap("uu", ALL), c1(PM), A.is_gt, 128.0, A.mult)
    iota(ap("kp", ALL), [[0, 32], [-4096, 16]], 65536, 0)
    for n, w_, step, c in (("rs0", L, 16, 1), ("rstk", L, 16, (1 << 24) - 1), ("rs1", 272, 17, 1)):
        iota(ap(n, ALL), [[0, w_]], 0, 0)
        iota(ap(n, S_(0, w_, step)), [[0, w_ // step]], c, 0)
    iota(ap("seg", ALL), [[0, 8], [1, 32]], 0, 0)
    iota(ap("ns", ALL), [[4096, 2], [256, 4], [0, 32]], 0, 0)
    lin(c1(P64 + 1), c1(Q4), scale=1008.0, bias=32.0)
    lin(c1(P64 + 2), c1(PM), scale=16.0, bias=c1(P64 + 1))
    lin(ap("ns", ALL), ap("ns", ALL), bias=c1(P64 + 2))
    iota(ap("srow", ALL), [[64, 2], [1, 16], [16, 4]], 511, 0)
    lin(ap("srow", ALL), ap("srow", ALL), scale=1.0 / 512)
    iota(ap("kk", S_(0, OFF)), [[0, OFF]], 0, 0)
    iota(ap("ia", 0, ALL), [[16, 32]], 0, 0)
    ts(ap("itc", 0, ALL), ap("ia", 0, ALL), c1(PM), A.add, 1.0 / 512, A.mult)
    lin(ap("itc", 1, ALL), ap("ia", 0, ALL), scale=0.0, bias=511.0)
    ts(ap("itc", 2, ALL), ap("ia", 0, ALL), c1(PM), A.add, -float(OFF), A.add)
    lin(ap("ia", 1, ALL), ap("itc", 2, ALL), bias=OFF + DUM - 4096.0)
    iota(ap("stp", ALL), [[-2, 16], [0, 32]], 300, 0)
    iota(ap("blk", ALL), [[1024, 2], [1, 64]], 0, 0)
    lin(ap("kq", ALL), ap("blk", ALL), bias=c1(P64))
    p8 = S_(0, 8)
    iota(pap("l8", p8, ALL), [[1, 8], [0, 16]], 0, -1)
    ts(pap("l8", p8, ALL), pap("l8", p8, ALL), 0.0, A.is_equal)
    copy(pap("thf", p8, S_(0, R)), pap("thi", p8, S_(0, R)))
    for t in range(R):
        lin(pap("sc1", p8, S_(128 * t, 128 * t + 128)), pap("l8", p8, ALL), scale=0.0, bias=pap("thf", p8, S_(t, t + 1)))
    mm([(P(1, S_(300 + 32 * t, 332 + 32 * t)), pap("sc1", p8, S_(128 * t, 128 * t + 128)), pap("l8", p8, S_(0, 128, 4))) for t in range(R)])
    lin(ap("tht", 0, ALL), P(1, S_(300, 332)), scale=16.0, bias=-0.5)
    lin(ap("tht", S_(1, R), ALL), P(1, S_(332, 396)), scale=16.0, bias=-8.5)

    def o1(t, j, e):
        return ap("of3", kof(t, j, e), S_(32 * t, 32 * t + 32))

    def cu(t, j, e, a=0, b=32):
        c = 32 * (16 * t + 2 * j + e)
        return ap("cu", S_(c + a, c + b))

    def lists():
        for h in BOTH:
            lin(ap("kv16", S_(h, L, 2)), ap("ki", S_(1024 * h, 1024 * h + 1024, 4)), bias=-CEN)
        for i, (a, b) in enumerate(BATCH):
            for k in range(a, b):
                o = P(4 + i % 2, S_(32 * (k - a), 32 * (k - a) + 32))
                mm([(o, wsl("ws", k, r), ap("kv16", S_(32 * r, 32 * r + 32))) for r in range(16)])
            ts(ap("of3", S_(a, b), S_(0, 32)), P(4 + i % 2, S_(0, 32 * (b - a))), CEN, A.add)
        for u in range(R):
            for h in BOTH:
                copy(ap("kw3", ALL, u, S_(h, 32, 2)), ap("ki", S_(1024 * h + u, 1024 * h + 1024, 4)))
        for k in range(16):
            a, b = 1 if k < BATCH[-1][1] else 0, 1 if k in (6, 7) else R
            if a < b:
                dma([(ap("of3", k, S_(32 * a, 32 * b)), pap("kw3", row(k), ALL, S_(a, b), ALL))])
            if k + 1 == XAT:
                mark["lists"] = len(ops) - 1
                dma([(ap("xx", S_(0, B0)), ap("xf", ALL))], after="lists")

    cnt = {}

    def nxt(n, m, late=0):
        k = cnt.get((n, late), 0)
        cnt[(n, late)] = k + 1
        return m + k % late if late else k % m

    def bank(t):
        return BANKS[t][nxt(("pb", BANKS[t]), len(BANKS[t]))]

    def suitors(t):
        b = bank(0)
        mm([(P(b, S_(2 * c + e, 384, 8)), ap("dtab", S_(4 * c + t, 2048, 16)), WD) for c in range(4) for e in BOTH])
        lin(ap("sv", t, ALL), P(b, S_(0, 384)), bias=-CEN)

    lists()
    for a, b in ((0, 1024), (1024, 2048), (2048, B0)):
        lin(ap("dtab", S_(a, b)), ap("ki", S_(a, b)), eng=DTE)
    for a, b in ((0, 1024), (1024, 2048), (2048, B0)):
        lin(kk(a, b), ap("ki", S_(a, b)), eng="G")
    iota(ap("dtab", S_(B0, B0 + 2 * L)), [[0, 2 * L]], 0, 0)
    iota(ap("pat", 0, ALL), [[0, 292]], int(CEN), 0)
    iota(ap("pat", 0, S_(0, 292, 4)), [[0, 73]], int(CEN) + 1, 0)
    for p, a, n, w_ in ((1, 0, 8, 288), (2, B0, 4, 256)):
        iota(ap("pat", p, S_(0, w_)), [[1, w_]], a, w_)
        dma([(pap("dtab", row(8 + t), S_(a, a + n * w_)), pap("pat", S_(0, 8 * n), 0, S_(4 - t, 4 - t + w_))) for t in range(R)] +
            [(pap("dtab", S_(16 * g + 11, 16 * g + 12), S_(a, a + n * w_)), pap("pat", S_(0, n), p, S_(0, w_))) for g in range(8)])
    mm([(P(3, S_(0, 144)), wsl("we", E16, r), ap("xx", S_(144 * r, 144 * r + 144))) for r in range(16)])
    lin(ap("sxc", ALL), P(3, S_(0, 144)), scale=1.0 / 16, bias=-120.0)
    dma([(pap("dtab", row(7), S_(0, B0)), ap("sxc", ALL))])
    for t in range(R):
        lin(xv(t), ap("xx", vcols(t)), eng="G" if t else "VAG")
    for t in range(R):
        suitors(t)
    for t in range(R):
        mm([(P(1, S_(32 * t, 32 * t + 32)), wsl("we", EW + t, r), ap("nb", t, S_(r, L, 16))) for r in range(16)])
    mm([(P(1, S_(128 + 32 * t + b, 160 + 32 * t, 4)), ap("nb", t, S_(b, L, 4)), ap("w8", W16, ALL)) for t in range(R) for b in range(4)])
    copy(ap("sa", 0, ALL), P(1, S_(0, 96)))
    lin(ap("sxw", 0, ALL), P(1, S_(128, 160)), bias=32640.0)
    lin(ap("sxw", S_(1, R), ALL), P(1, S_(160, 224)), bias=32632.0)
    ts(ap("sa", 1, ALL), ap("sa", 0, ALL), 2047, A.bitwise_and)
    copy(ap("su", S_(0, R), ALL), ap("sa", 1, ALL))
    for t in range(R):
        push(ap("qa", t, ALL), ap("su", t, ALL), 1 + t)

    def bulk(t):
        if t == 0:
            push(ap("rx0", ALL), ap("xx", S_(0, B0)), -1, ("names", 0))
            dma([(pap("yk", row(j), S_(0, B0)), kk(0, B0, 1, row(j))) for j in range(16) if j not in (6, 7, 9, 10, 11)], after=("names", 0))
        if t == 1:
            push(ap("rx1", S_(0, B0)), ap("xx", S_(0, B0)), -2, ("names", 1))
        if t == 2:
            push(ap("rx2", S_(0, B0)), ap("xx", S_(0, B0)), -3, ("names", 2))

    def pos(t, b, j, es):
        return P(b + t % 2, S_(j, L, 8)) if len(es) == 2 else P(b + t % 2, S_(j + 8 * es[0], L, 16))

    def es_(es):
        return S_(32 * es[0], 32 * es[-1] + 32)

    def names_static(t, js, es, late=False):
        for i, j in enumerate(js):
            g = nxt("g1", NG1)
            for e in es:
                lin(ap("g1", g, S_(L * e, L * e + L)), ind(ap("ki", ALL), o1(t, j, e)))
            dma([(cu(t, j, e), pap("g1", row((kof(t, j, e) + t) % 16), g, S_(L * e, L * e + L))) for e in es])
        mark[("names", t)] = len(ops) - 1

    def names_pe(t, j, es, late=True):
        s, b, n = nxt("gh", 3), 7 if t == 1 else 6 + j % 2, 32 * len(es)
        for i, e in enumerate(es):
            kr = (kof(t, j, e) + t) % 16
            lin(ap("gh", s, i, ALL), ind(kk(0, B0 + L * t) if late else ap("ki", ALL), o1(t, j, e)), scale=mk(kr), bias=mk(16 + kr))
        mm([(P(b, S_(0, n)), wsl("weh", 0, r), ap("gh", s, S_(0, len(es)), S_(32 * r, 32 * r + 32))) for r in range(16)])
        lin(cu(t, j, es[0], 0, n), P(b, S_(0, n)), bias=CEN)
        mark[("late" if late else "names", t)] = len(ops) - 1

    def halves(t, kinds):
        return [(j, tuple(e for e in BOTH if m[e] in kinds)) for q in DYN[t] for j, m in q if set(m) & set(kinds)]

    def sums(b, t, j, e, src, w_):
        return [(P(b + t % 2, S_(16 * c + j + 8 * e, L, 64)), src(c), ap("w8", w_, ALL)) for c in range(4)]

    def features(t, j, es, late=False, hold=False):
        s = nxt("rb", NB, LB * late)
        for i, e in enumerate(es):
            z = L * (2 * s + i)
            for ls, off in pieces(t, j, e, PIECES[t][j]):
                tt(ap("rb", S_(z + ls.start, z + ls.stop)), ind(ap("xx", S_(0, B0 + L * t * late)), off), ap("nb", t, ls), A.min)
                if hold:
                    ops[-1]["after"].append(mark["named"])
            mm(sums(0, t, j, e, lambda c: ap("rb", S_(z + c, z + L, 4)), WM32), ("k", t))

    def blood(t, j, es, late=False, asked=False):
        n, g, q, b = len(es), nxt("gd", NG, LG * late), nxt("eq", NQ, LQ * late), bank(t)
        whole = n == 2 and not late and j in WHOLE[t]
        if whole:
            lin(ap("gd", g, ALL), ind(ap("dtab", S_(0, B0)), cu(t, j, 0, 0, 64)), bias=-CEN)
        for i, e in enumerate(es):
            if not whole:
                lin(ap("gd", g, S_(L * i, L * i + L)), ind(ap("dtab", S_(0, B0 + L * t * late)), cu(t, j, e)), bias=-CEN)
            blocks = [ap("gd", g, S_(L * i + c, L * i + L, 4)) for c in range(4)]
            mm([(P(b, S_(n * c + i, 192 * n, 4 * n)), blocks[c], WV) for c in range(4)], ("u", t, j, es))
            if not asked:
                mm(sums(0, t, j, e, lambda c: blocks[c], WKEY + t), ("k", t))
            mm(sums(2, t, j, e, lambda c: blocks[c], WNUM), ("c", t))
        w_ = 32 * n
        tt(ap("eq", q, S_(0, 6 * w_)), P(b, S_(0, 6 * w_)), ap("sv", t, S_(0, 384, 2 // n)), A.is_equal)
        if asked:
            mark[("d8", t)] = (j, es[0], g, q)
        else:
            mm([(pos(t, 0, j, es), IBAR, ap("eq", q, S_(w_ * a, w_ * a + w_))) for a in range(6)], ("k", t))

    def turned(i):
        return ap("zz", i, S_(3, 35, 4), ALL)

    def listed(o, i, w_):
        return [(o, ap("zz", i, S_(3 - a, 35 - a), ALL), ap("mb", w_, S_(a, 128, 4))) for a in range(4)]

    def pieces(t, j, e, n):
        return [(S_(L // n * q, L // n * (q + 1)), cu(t, j, e, 32 // n * q, 32 // n * (q + 1))) for q in range(n)]

    def least(t):
        kb, cb_ = t % 2, 2 + t % 2
        ends = S_(15, L, 16)
        scan(ap("sc1", ALL), ap("rstk", ALL), P(kb), A.add, A.min)
        mark["named"] = len(ops) - 1
        tt(ap("uu", ALL), P(kb), ap("sc1", ALL), A.not_equal)
        scan(ap("sc2", ALL), ap("uu", ALL), P(cb_), A.mult, A.max)
        tt(sm(13), ap("sc1", ends), ap("sxw", t, ALL), A.add)
        ts(sm(3), ap("sc2", ends), MAGIC * 4096, A.add, -MAGIC * 4096, A.add)
        ts(sm(0) if t else turned(2), sm(13), 100000.0, A.is_gt, 4096.0, A.mult)
        tt(sm(15) if t else turned(0), ap("sc2", ends), sm(3), A.subtract)
        if t:
            j, e = mark[("d8", t)][:2]
            ts(sm(1), sm(13), 100000.0, A.min)
            lin(sm(22), pos(t, 2, j, (e,)), bias=4096.0 * (j + 8 * e) - 65536.0)
            tt(sm(16), sm(22), sm(0), A.subtract)

    def score_asked(t):
        j, e, g, q = mark[("d8", t)]
        ob = 2 + (t - 1) % 2
        o = P(ob, S_(0, 32))
        mm([(o, IBAR, ap("eq", q, S_(32 * a, 32 * a + 32))) for a in range(6)] +
           [(P(ob, S_(c, 32, 4)), ap("gd", g, S_(c, L, 4)), ap("w8", WMOD + t, ALL)) for c in range(4)], ("x", t))
        tt(ap("bb", 0, ALL), ind(ap("xx", S_(0, B0 + L * t)), cu(t, j, e)), xv(t), A.subtract)
        ts(ap("bb", 1, ALL), ap("bb", 0, ALL), 0.0, A.min)
        for i in BOTH:
            mm([(P(ob, S_(c, 32, 4)), ap("bb", i, S_(c, L, 4)), ap("w8", i, ALL)) for c in range(4)], ("x", t))
        tt(sm(17), o, sm(1), A.is_lt)
        tt(sm(14), o, sm(1), A.is_ge)
        tt(sm(19), o, sm(13), A.min)
        tt(sm(18), sm(17), sm(16), A.mult)
        tt(turned(0), sm(15), sm(14), A.mult)
        tt(turned(2), sm(18), sm(0), A.add)

    def opens(t, which):
        if which == "k":
            mm([(P(t % 2), IB, ap("kc", t % 2, ALL))] + [(pos(t, 0, j, es), IB, ap("barc", ALL)) for j, es in halves(t, "W")], ("k", t))
        else:
            mm([(P(2 + t % 2), IB, ap("kp", ALL))], ("c", t))

    def sm(i, *ix):
        return ap("sm", i, *(ix if ix else (ALL,)))

    def su(i, *ix):
        return ap("su", i, *(ix if ix else (ALL,)))

    MU, I1, SO, RO, ONEW, OVC, NO, XI = range(3, 11)
    CHILD, KV, WEDV, ASKV = [S_(L * i, L * i + L) for i in range(4)]

    def prepare(t):
        src = kk(t, 2048, 4)
        if t:
            for h in BOTH:
                lin(ap("kvf", S_(h, L, 2)), kk(1024 * h + t, 1024 * h + 1024, 4), eng=KVF)
            dma([(ap("l67", i, ALL), pap("kvf", row(6 + i), ALL)) for i in BOTH])
            copy(ap("of3", S_(6, 8), S_(32 * t, 32 * t + 32)), ap("l67", ALL, ALL))
        for c in (KV, WEDV, ASKV):
            lin(ap("cb", c), src, eng="G")
        iota(ap("vv", ALL), [[4, L]], t, 0)
        iota(ap("nv", t % 2, ALL), [[1, L]], B0 + L * t, 0)
        dma([(pap("kk", row(7), S_(0, OFF)), pap("nv", row(7), t % 2, ALL)), (pap("kk", row(6), S_(0, OFF)), pap("vv", row(6), ALL))])
        dma([(pap("cb", row(7), WEDV), pap("nv", row(7), t % 2, ALL)), (pap("cb", row(9 + t), ASKV), pap("nv", row(7), t % 2, ALL))])
        dma([(pap("cb", row(0), CHILD), pap("vv", row(0), ALL))] + [(pap("cb", row(j), CHILD), pap("nv", row(j), t % 2, ALL)) for j in (6, 7)] +
            [(pap("cb", row(b), CHILD), pap("cb", row(a), KV)) for a, b in ((0, 2), (1, 3), (7, 8))])

    def answer(t):
        lin(ap("pkv", ALL), ind(kk(0, 2048) if t else ap("ki", S_(0, 2048)), ap("qa", t, ALL)))
        push(ap("rk", t, ALL), ap("pkv", ALL), -1 - t)

    def tail(t):
        n0 = B0 + L * t
        ends = S_(15, L, 16)
        kb, cb_ = t % 2 if t else 6, 2 + t % 2
        tt(turned(1), sm(19 if t else 13), ap("tht", 3 if t else 0, ALL), A.is_gt)
        LM, LF = P(cb_, S_(64, 96)), P(cb_, S_(96, 128))
        last = t + 1 == R
        mm(listed(LM, 0, 0) + listed(LM, 2, 0))
        mm([(LF, IB, ap("itc", 2, ALL))] * (not last) + listed(LF, 1, 1))
        m16 = ap("m16", ALL)
        copy(m16, LM)
        ts(su(MU), LM, n0 - 1 - CEN, A.min, CEN, A.add)
        ts(sm(20), LM, n0 - 1 - CEN, A.min, CEN, A.add)
        if not last:
            tt(sm(4), LF, sm(20), A.min)
            ts(su(I1), sm(4), float(OFF), A.add)
        mm([(P(6), IB, ap("dm0", ALL))], ("d0", t))
        mm([(P(6, S_(r + 1, L, 16)), ap("ll", r, ALL), m16) for r in range(15)], ("d0", t))
        mm([(P(7, S_(0, 272, 17)), IB, ap("rs1", S_(1, 17)))], ("d1", t))
        mm([x for r in range(16) for x in ((P(7, S_(r + 1, 272, 17)), ap("rr", r, ALL), ap("m16", S_(0, 32, 2))),
                                           (P(7, S_(r + 1, 272, 17)), NI64, ap("m16", S_(1, 32, 2))))], ("d1", t))
        lin(ap("km", ALL), ind(kk(0, n0), su(MU)), scale=c1(N67))
        if not last:
            lin(ap("val", ALL), ind(kk(-OFF, n0), su(I1)))
        lin(ap("xm16", ALL), ind(ap("xx", S_(0, n0)), su(MU)), bias=-0.5)
        scan(ap("sc2", ALL), P(6), ap("rs0", ALL), A.mult, A.add)
        scan(ap("sd1", ALL), P(7, S_(0, 272)), ap("rs1", ALL), A.mult, A.add)
        dma([(pap("cb", row(b), CHILD), pap("km", row(a), ALL)) for a, b in [(0, 4), (1, 5)] + [(k, k) for k in range(9, 16)]])
        vop("transpose", sm(21), [sm(20)], [sm(20)])
        dma([(pap("cb", S_(16 * h + 1, 128, 32), CHILD), sm(21, S_(16 * h, 16 * h + 16))) for h in BOTH])
        dma([(pap("cb", row(6), WEDV), pap("cb", row(1), CHILD))])
        mm([(P(kb), HIB, ap("xm16", ALL)), (P(kb), HIB, xv(t))])
        for a in range(0, L, MEAN):
            ts(ap("nb", t, S_(512 + a, 512 + a + MEAN)), P(kb, S_(a, a + MEAN)), MAGIC, A.add, -MAGIC, A.add)
        if t + 1 < R:
            dma([(ap("xx", S_(n0, n0 + L)), ap("nb", t, S_(512, 1024)))])
            sum_row(t, lambda a, b: ap("nb", t, S_(512 + a, 512 + b)))
        ts(sm(5), ap("sc2", ends), 0.0, A.is_equal, 8192.0, A.mult)
        ts(sm(6, S_(0, 16)), ap("sd1", S_(16, 272, 17)), 0.0, A.is_equal, 8192.0, A.mult)
        tt(sm(7), m16, sm(5), A.add)
        ts(su(SO, S_(0, 32, 2)), sm(7, S_(0, 32, 2)), c1(DE + 2 * last), A.min, CEN, A.add)
        tt(sm(7, S_(1, 32, 2)), sm(7, S_(1, 32, 2)), sm(6, S_(0, 16)), A.add)
        ts(su(SO, S_(1, 32, 2)), sm(7, S_(1, 32, 2)), c1(DO + 2 * last), A.min, CEN, A.add)
        if not last:
            for a in range(15, -1, -1):
                tt(ind(kk(0, W + 32), su(SO, S_(2 * a, 2 * a + 2))), ap("val", S_(32 * a, 32 * a + 32)), ap("km", S_(32 * a, 32 * a + 32)), A.max)
            tt(ap("li", 0, ALL), ind(kk(0, n0), su(MU)), ap("nv", t % 2, ALL), A.not_equal)
        else:
            tab = [ap("rb", S_(3584 * h, 3584 * h + n0 + 48)) for h in BOTH]
            for a in range(7, -1, -1):
                for h in BOTH:
                    copy(ind(tab[h], su(SO, S_(16 * h + 2 * a, 16 * h + 2 * a + 2))), ap("stp", S_(256 * h + 32 * a, 256 * h + 32 * a + 32)))
            tt(sm(4), LF, sm(7), A.add)
            ts(su(I1), sm(4), n0 + 40 - CEN, A.min, CEN, A.add)
            tt(ap("uu", S_(0, 256)), ind(tab[0], su(I1, S_(16, 32))), ap("stp", S_(256, L)), A.max)
            tt(ap("li", 0, S_(0, 256)), ind(tab[0], su(I1, S_(0, 16))), ap("stp", S_(0, 256)), A.not_equal)
            tt(ap("li", 0, S_(256, L)), ind(tab[1], su(I1, S_(16, 32))), ap("uu", S_(0, 256)), A.not_equal)
        scan(ap("li", 1, ALL), ap("li", 0, ALL), ap("li", 0, ALL), A.add, A.max)
        Z, Y = P(7, S_(320, 352)), P(7, S_(352, 384))
        mm([(P(7, S_(320, 384)), IB, ap("itc", S_(0, 2), ALL))] + [(P(7, S_(320, 384)), wsl("ws", 7, r), ap("li", ALL, S_(r, L, 16))) for r in range(16)])
        ts(sm(8), Y, 1.0 / 512, A.mult)
        tt(sm(9), Z, sm(8), A.min)
        ts(su(ONEW), Z, 512.0, A.mult)
        ts(sm(10), sm(9), 639.5 / 512, A.is_gt, -2.0, A.mult)
        tt(sm(11), Z, sm(10), A.add)
        ts(su(OVC), sm(11), 512.0, A.mult, 1024.0, A.add)
        tt(sm(12), sm(11), sm(9), A.min)
        ts(su(XI), sm(12), 512.0, A.mult, 512.0, A.add)
        mm([(P(kb, S_(0, 256)), IB, ap("ns", ALL))] +
           [(P(kb, S_(32 * a + 1, 32 * a + 32)), R7, ap("li", 1, S_(15, 496, 16))) for a in range(8)])
        scan(ap("bs", ALL), P(kb, S_(0, 256)), ap("seg", ALL), A.max, A.min)
        copy(su(RO, S_(0, 8)), ap("bs", S_(31, 256, 32)))
        tt(ap("fl", ALL), ind(sm(8), su(RO, S_(0, 8))), ap("srow", ALL), A.is_le)
        mm([(P(cb_, S_(0, 8)), I16, ap("bs", S_(31, 256, 32)))] +
           [(P(cb_, S_(0, 8)), wsl("weh", 0, r), ap("fl", S_(r, 128, 16))) for r in range(16)])
        ts(su(RO, S_(8, 16)), P(cb_, S_(0, 8)), 511.0, A.min)
        copy(ap("du", ALL), ind(ap("rk", t, ALL), su(RO, S_(8, 16))))
        lin(ap("xs", ALL), ind(xv(t), su(RO, S_(8, 16))))
        if last:
            ts(sm(5), Z, 1.0, A.is_ge, 4096.0, A.mult)
            tt(sm(6), sm(5), ap("ia", 1, ALL), A.add)
            tt(sm(5), sm(6), sm(20), A.max)
            copy(su(SO), sm(5))
            for a in range(0, L, WED):
                tt(ind(kk(0, W), su(SO, S_(a // 16, (a + WED) // 16))), kk(a - OFF, a + WED - OFF), ap("km", S_(a, a + WED)), A.max)
        lin(kk(t, 2048, 4), ind(ap("cb", ALL), su(OVC)))
        lin(kk(n0, n0 + L), ind(ap("cb", S_(0, 1024)), su(ONEW)))
        if t + 1 < R:
            dma([(pap("dtab", row(j), S_(n0, n0 + L)), kk(n0, n0 + L, 1, row(j))) for j in range(6)])
            mm([(P(6, S_(0, 1)), W7, ap("li", 1, S_(L - 1, L)))])
            ts(pc(4), P(6, S_(0, 1)), -1.0, A.mult, 4096.0, A.add)
            ts(pc(5), pc(4), 15, A.bitwise_and)
            lin(c1(ZC), pc(5), scale=16.0)
            lin(ap("tht", 3, ALL), ap("tht", t + 1, ALL), bias=c1(ZC))

    def sum_row(t, feats):
        n0, s = B0 + L * t, nxt("sxn", 2)
        mm([(P(6, S_(64, 96)), wsl("we", E16, r), feats(32 * r, 32 * r + 32)) for r in range(16)])
        lin(ap("sxn", s, ALL), P(6, S_(64, 96)), scale=1.0 / 16, bias=-120.0)
        dma([(pap("dtab", row(7), S_(n0, n0 + L)), ap("sxn", s, ALL))])

    def stores(t):
        n0 = B0 + L * t
        if t + 1 < R:
            answer(t + 1)
        st = [(pap("yk", row(9 + t), S_(0, B0)), kk(0, B0, 1, row(9 + t)))]
        if t + 1 == R:
            dma(st + [(pap("yk", row(j), S_(0, n0)), kk(0, n0, 1, row(j))) for j in (6, 7)])
            st = []
        dma(st + [(ap("yk", S_(n0, n0 + L)), kk(n0, n0 + L))], after=("late", t + 1) if t + 1 < R else None)

    def ask(t):
        n0 = B0 + L * t
        kb, cb_ = t % 2 if t else 6, 2 + t % 2
        banks = [cb_, kb, cb_, kb] if t + 1 < R else [cb_, kb, 4, 5]
        for b in range(4):
            lin(ap("ga", S_(L * b, L * b + L)), ind(ap("rx%d" % t, ALL), ap("du", S_(32 * b, 32 * b + 32))))
        for b in range(4):
            h, q = b // 2, b % 2
            if h in ASK_V[t]:
                mm([(P(banks[b], S_(k, L, 16)), IB, ap("xs", S_(32 * b, 32 * b + 32))) for k in range(16)])
                tt(ap("ra", S_(32 * b, 32 * b + 32), ALL), ap("ga", S_(L * b, L * b + L)), P(banks[b]), A.max)
                continue
            mm([(P(banks[b], S_(k, L, 8)), NIB, ap("xs", S_(64 * h, 64 * h + 64))) for k in range(8)], ("a", t, b))
            mm([(P(banks[b], S_(k, L, 8)), IB, ap("ga", S_(1024 * h + 8 * q + k, 1024 * h + 1024, 16))) for k in range(8)], ("a", t, b))
            act(ap("ra", S_(64 * h, 64 * h + 64), S_(8 * q, 8 * q + 8)), P(banks[b]), F.Abs, scale=128.0)
        o = P(7, S_(0, 128))
        mm([(o, IB, ap("kq", ALL))], ("o", t))
        for h in range(2):
            oh, byv = P(7, S_(64 * h, 64 * h + 64)), h in ASK_V[t]
            if byv:
                mm([(oh, wsl("we", EY, r), ap("ga", S_(1024 * h + 64 * r, 1024 * h + 64 * r + 64))) for r in range(16)], ("o", t))
            for rs in ((range(8), range(8, 16)) if byv else (range(16),)):
                mm([(oh, wsl("we", EMX if byv else E16, r), ap("ra", S_(64 * h + 4 * r, 64 * h + 4 * r + 4), ALL)) for r in rs], ("o", t))
        scan(ap("sc0", ALL), ap("rstk", S_(0, 128)), o, A.add, A.min)
        copy(ap("si", 0, ALL), ap("sc0", S_(15, 128, 16)))
        ts(ap("si", 1, ALL), ap("si", 0, ALL), 2047, A.bitwise_and)
        copy(su(NO, S_(0, 8)), ap("si", 1, ALL))
        lin(ap("nb", t, S_(1024, 1152)), ind(ap("ga", ALL), su(NO, S_(0, 8))))
        n = 1 if t + 1 < R else 2
        for a, b in [(L // n * h, L // n * (h + 1)) for h in range(n)]:
            lin(ap("xx", S_(n0 + a, n0 + b)), ind(ap("nb", t, ALL), su(XI, S_(a // 16, b // 16))))
        dma([(ap("yx", S_(L * t, L * t + L)), ap("xx", S_(n0, n0 + L)))])
        for u in range(t + 1, R):
            push(ap("rx%d" % u, S_(n0, n0 + L)), ap("xx", S_(n0, n0 + L)), -1 - u)

    def names(t):
        for js in QUADS[t]:
            if js[0] in NAMES_PE[t]:
                for j in js:
                    names_pe(t, j, BOTH, False)
            else:
                names_static(t, js, BOTH)
        for j, es in halves(t, "M"):
            names_static(t, (j,), es)
        bulk(t)

    def still(t, short):
        return [(j, es) for j, es in [(j, BOTH) for js in QUADS[t] for j in js] + halves(t, "M") if (PIECES[t][j] > 1) == short]

    opens(0, "k")
    opens(0, "c")
    names(0)
    for j, es in still(0, False):
        features(0, j, es)
        blood(0, j, es)
    answer(0)
    prepare(0)
    least(0)
    opens(1, "k")
    opens(1, "c")
    names(1)
    opens(2, "k")
    names(2)
    for t in range(R):
        if t == 0:
            for u in (1, 2):
                for j, es in still(u, False):
                    features(u, j, es)
        if t == 1:
            opens(2, "c")
        if t + 1 < R:
            for j, es in still(t + 1, False) + still(t + 1, True):
                blood(t + 1, j, es)
            for j, es in still(t + 1, True):
                features(t + 1, j, es, hold=True)
        tail(t)
        if t + 1 < R:
            prepare(t + 1)
            for j, es in halves(t + 1, "LW"):
                names_pe(t + 1, j, es)
            for j, es in halves(t + 1, "L"):
                blood(t + 1, j, es, True)
                features(t + 1, j, es, True)
            for j, es in halves(t + 1, "W"):
                blood(t + 1, j, es, True, True)
            least(t + 1)
        stores(t)
        ask(t)
        if t + 1 < R:
            score_asked(t + 1)
        if t + 2 < R:
            sum_row(t, lambda a, b: ap("xx", S_(B0 + L * t + a, B0 + L * t + b)))
    return ops


def depend(ops):
    hist, head = {}, {}
    group = [o["alts"][0][2][2].get("group") for o in ops]
    for i, o in enumerate(ops):
        deps = {j: False for j in o["after"]}
        fixed = o["alts"][0][0] if len(o["alts"]) == 1 else None
        gr = group[i]
        if gr:
            if gr in head:
                deps[head[gr]] = False
            head.setdefault(gr, i)
        for regs, wr in ((o["r"], False), (o["w"], True)):
            for n, pm, cm, _1, _2 in regs:
                bank = n[0] == "p" and n[1:].isdigit()
                for j, pj, cj, wj, ej in hist.get(n, []):
                    if j == i or (gr and group[j] == gr):
                        continue
                    over = (pm & pj) and (cm & cj)
                    if (over and (wr or wj)) or (bank and (ej is None or ej != fixed)):
                        deps[j] = deps.get(j, False) or bool(over and wj and not wr)
        for regs, wr in ((o["r"], False), (o["w"], True)):
            for n, pm, cm, _1, _2 in regs:
                h = hist.setdefault(n, [])
                if wr:
                    bank = n[0] == "p" and n[1:].isdigit()
                    h[:] = [x for x in h if x[0] == i or (gr and group[x[0]] == gr) or (x[1] & ~pm) or (x[2] & ~cm) or (bank and x[4] != fixed and cm + 1 != 1 << 512)]
                h.append((i, pm, cm, wr, fixed))
        o["deps"] = deps


def search(ops, seed, tries, polish=0, nj=6, amp=1200.0, temp=60.0, temp2=20.0):
    n = len(ops)
    succ, dep = [[] for _ in range(n)], []
    for i, o in enumerate(ops):
        gr = o["alts"][0][2][2].get("group")
        dep.append([(j, bool(gr) and gr == ops[j]["alts"][0][2][2].get("group"), ops[j]["kind"] == "c", True)
                    for j in o["deps"]])
        for j in o["deps"]:
            succ[j].append(i)
    base = [min(a[1] for a in o["alts"]) + o["lat"] + LAT_X + (o["extra"] or 0.0) for o in ops]
    cost = [{a[0]: a[1] for a in o["alts"]} for o in ops]
    lat = [o["lat"] for o in ops]
    moves = [o["kind"] != "c" for o in ops]

    queues = "VAPGY"

    def schedule(jit, shy):
        prio = [0.0] * n
        for i in range(n - 1, -1, -1):
            m = 0.0
            for s in succ[i]:
                if prio[s] > m:
                    m = prio[s]
            prio[i] = base[i] + jit[i] + m
        left = [len(d) for d in dep]
        pool, free, wake = {e: [] for e in queues}, {e: 0.0 for e in queues}, {e: 0.0 for e in queues}
        fin, start, eng = [0.0] * n, [0.0] * n, [None] * n
        dfree = 0.0

        def arrive(i, now):
            for e in cost[i]:
                s = 0.0
                for j, same, cj, raw in dep[i]:
                    x = start[j] if same else fin[j] + (LAT_S if cj and eng[j] == e else LAT_X)
                    if x > s:
                        s = x
                p = -prio[i] + (shy[i] if e == "V" and len(cost[i]) > 1 else 0.0)
                pl = pool[e]
                k = len(pl)
                while k and pl[k - 1][0] > p:
                    k -= 1
                pl.insert(k, (p, s, cost[i][e], i))
                w = max(s, free[e], now)
                if w < wake[e]:
                    wake[e] = w

        for i in range(n):
            if not left[i]:
                arrive(i, 0.0)
        order = []
        while len(order) < n:
            e = min(queues, key=wake.get)
            t = wake[e]
            if e == "Y" and t < dfree - DPRE - 100.0:
                wake[e] = dfree - DPRE - 100.0
                continue
            pl = pool[e]
            lim, top, pick, soon, k = 1e18, None, None, 1e18, 0
            while k < len(pl):
                p, s, c, i = pl[k]
                if eng[i]:
                    pl.pop(k)
                    continue
                if s <= t:
                    if t + c <= lim or p - top < DEL:
                        pick = k
                        break
                else:
                    soon, lim = min(soon, s), min(lim, s + TOL)
                    if top is None:
                        top = p
                k += 1
            if pick is None:
                wake[e] = soon
                continue
            p, s, c, i = pl.pop(pick)
            eng[i], start[i] = e, t
            wake[e] = free[e] = t + c
            fin[i] = t + c + lat[i]
            if moves[i]:
                dfree = max(t + c + DPRE, dfree) + lat[i] - DPRE - DPOST
                fin[i] = dfree + DPOST
            order.append(i)
            for s in succ[i]:
                left[s] -= 1
                if not left[s]:
                    arrive(s, t)
        return order, start, fin, eng

    others = [build(m) for m in MODELS]
    others = [([{a[0]: a[1] for a in o["alts"]} for o in x], [o["lat"] for o in x]) for x in others]

    def replay(order, eng, k):
        cs, lt = others[k]
        pre, post, lx, ls = MODELS[k][3], MODELS[k][4], MODELS[k][7], MODELS[k][8]
        free, fin, dfree = {e: 0.0 for e in queues}, [0.0] * n, 0.0
        for i in order:
            e = eng[i]
            s = free[e]
            for j, same, cj, raw in dep[i]:
                x = 0.0 if same else fin[j] + (ls if cj and eng[j] == e else lx)
                if x > s:
                    s = x
            s = free[e] = s + cs[i][e]
            if moves[i]:
                dfree = max(s + pre, dfree) + lt[i] - pre - post
                fin[i] = dfree + post
            else:
                fin[i] = s + lt[i]
        return max(fin)

    def times(jit, shy):
        order, start, fin, eng = schedule(jit, shy)
        return [max(fin)] + [replay(order, eng, k) for k in range(1, len(MODELS))]

    rng = np.random.RandomState(seed)
    both = [i for i in range(n) if len(cost[i]) > 1]
    jit, shy = [0.0] * n, [SHY] * n
    norm = times(jit, shy)
    norm = [norm[0] / x / len(norm) for x in norm]
    cur = best = norm[0] * len(norm) * 1e9
    keep = (jit, shy)
    for k in range(tries):
        j2, s2 = list(jit), list(shy)
        for i in rng.randint(0, n, nj):
            j2[i] = max(0.0, j2[i] + amp * float(rng.standard_normal()))
        if k % 2:
            s2[both[rng.randint(0, len(both))]] = (0.0, SHY, 1e5)[rng.randint(0, 3)]
        m = sum(a * b for a, b in zip(times(j2, s2), norm))
        if m <= cur + temp * (1 - k / tries) * float(rng.exponential()):
            cur, jit, shy = m, j2, s2
            if m < best:
                best, keep = m, (j2, s2)
    order, start, fin, eng = schedule(*keep)

    after = [[] for _ in range(n)]
    for i in range(n):
        for j, same, cj, raw in dep[i]:
            after[j].append((i, same, cj))

    def gap(line, s, c):
        a, b = 0, len(line)
        while a < b:
            h = (a + b) // 2
            if line[h][1] <= s:
                a = h + 1
            else:
                b = h
        while a < len(line) and line[a][0] < s + c:
            s = max(s, line[a][1])
            a += 1
        return s, a

    def sweep(seq, eng, k, back, choose):
        cs, lt = others[k]
        pre, post, lx, ls = MODELS[k][3], MODELS[k][4], MODELS[k][7], MODELS[k][8]
        lines, eng = {e: [] for e in queues + "D"}, list(eng)
        fin, at = [0.0] * n, [0.0] * n
        for i in seq:
            pick = None
            for e in (cs[i] if choose and len(cs[i]) > 1 else (eng[i],)):
                s, c = 0.0, cs[i][e]
                if back:
                    for j, same, cj in after[i]:
                        x = fin[j] - lt[i] if same else fin[j] + (ls if cj and eng[j] == e else lx)
                        if x > s:
                            s = x
                else:
                    for j, same, cj, raw in dep[i]:
                        x = fin[j] - lt[j] if same else fin[j] + (ls if cj and eng[j] == e else lx)
                        if x > s:
                            s = x
                d = None
                if moves[i]:
                    w = lt[i] - pre - post
                    if back:
                        d = gap(lines["D"], s + post, w)
                        s, a = gap(lines[e], d[0] + w + pre, c)
                        f = s + c
                    else:
                        s, a = gap(lines[e], s, c)
                        d = gap(lines["D"], s + c + pre, w)
                        if e == "Y":
                            s, a = gap(lines[e], d[0] - pre - c, c)
                        f = max(d[0], s + c + pre) + w + post
                else:
                    s, a = gap(lines[e], s + lt[i] if back else s, c)
                    f = s + c + (0.0 if back else lt[i])
                x = f + (choose if e == "V" else 0.0)
                if pick is None or x < pick[0]:
                    pick = (x, e, s, a, c, f, d)
            x, e, s, a, c, f, d = pick
            lines[e].insert(a, (s, s + c))
            if d:
                lines["D"].insert(d[1], (d[0], d[0] + lt[i] - pre - post))
            eng[i], fin[i], at[i] = e, f, s + c if back else s
        return sorted(seq, key=lambda i: -at[i] if back else at[i]), eng

    def total(order, eng):
        return sum(replay(order, eng, k) * norm[k] for k in range(len(MODELS)))

    best = cur = total(order, eng)
    keep = (order, eng)
    for it in range(SWEEPS):
        k = rng.randint(0, len(MODELS))
        o2, e2 = sweep(order[::-1], eng, k, True, BIAS[rng.randint(0, len(BIAS))])
        o2, e2 = sweep(o2, e2, k, False, BIAS[rng.randint(0, len(BIAS))])
        m = total(o2, e2)
        if m <= cur + SLACK * (1 - it / SWEEPS) * float(rng.exponential()):
            cur, order, eng = m, o2, e2
            if m < best:
                best, keep = m, (o2, e2)
    order, eng = keep

    def run(order, eng, k, p, old):
        cs, lt = others[k]
        pre, post, lx, ls = MODELS[k][3], MODELS[k][4], MODELS[k][7], MODELS[k][8]
        fin, end, by = (list(x) for x in old) if old else ([0.0] * n, [0.0] * n, [0] * n)
        last, dlast = {}, None
        for q in range(p - 1, -1, -1):
            i = order[q]
            last.setdefault(eng[i], i)
            if dlast is None and moves[i]:
                dlast = i
            if len(last) == 5 and dlast is not None:
                break
        dfree = fin[dlast] - post if dlast is not None else 0.0
        for q in range(p, n):
            i = order[q]
            e = eng[i]
            b = last.get(e)
            s = end[b] if b is not None else 0.0
            b = -1 - b if b is not None else n
            for j, same, cj, raw in dep[i]:
                x = 0.0 if same else fin[j] + (ls if cj and eng[j] == e else lx)
                if x > s:
                    s, b = x, j
            s = end[i] = s + cs[i][e]
            last[e] = i
            if moves[i]:
                if dfree > s + pre:
                    s, b = dfree - pre, -1 - dlast
                dfree = s + lt[i] - post
                fin[i], dlast = dfree + post, i
            else:
                fin[i] = s + lt[i]
            by[i] = b
        return fin, end, by

    ks = range(len(MODELS))
    state = [run(order, eng, k, 0, None) for k in ks]
    cur = best = sum(max(s[0]) * w for s, w in zip(state, norm))
    keep = (order, eng)
    for it in range(polish):
        k = rng.randint(0, len(MODELS))
        fin, end, by = state[k]
        i, held = fin.index(max(fin)), []
        while i < n:
            b = by[i]
            if b < 0:
                b = -1 - b
                held.append((b, i))
            i = b
        u, v = held[rng.randint(0, len(held))]
        where = {x: q for q, x in enumerate(order)}
        pu, pv, o2, e2, kind = where[u], where[v], list(order), eng, rng.randint(0, 4)
        if it % 3 == 0:
            e, cs = "VVA"[rng.randint(0, 3)], others[k][0]
            line = [x for x in order if eng[x] == e]
            idle = [(x, end[y], end[x] - cs[x][e]) for y, x in zip(line, line[1:]) if end[x] - cs[x][e] - end[y] > 60.0]
            x, a, b = idle[rng.randint(0, len(idle))]
            pu = where[x]
            fit = [y for y in order[pu + 1:] if e in cost[y] and cs[y][e] < b - a + 150.0 and
                   all(where[d[0]] < pu and fin[d[0]] + LAT_S < a + 100.0 for d in dep[y])]
            if not fit:
                continue
            v = fit[int(len(fit) * rng.random_sample() ** 2)]
            o2.insert(pu, o2.pop(where[v]))
            e2 = list(eng)
            e2[v] = e
        elif kind == 0 and (len(cost[u]) > 1 or len(cost[v]) > 1):
            x = u if len(cost[v]) == 1 or (len(cost[u]) > 1 and it % 2) else v
            e2 = list(eng)
            e2[x] = [e for e in cost[x] if e != eng[x]][0]
            pu = where[x]
        elif kind % 2 and all(where[s] > pv for s in succ[u]):
            o2.insert(min(pv + rng.randint(0, 12), min([where[s] for s in succ[u]] + [n]) - 1), o2.pop(pu))
        elif all(where[d[0]] < pu for d in dep[v]):
            pu = max([pu - rng.randint(0, 12)] + [where[d[0]] + 1 for d in dep[v]])
            o2.insert(pu, o2.pop(pv))
        else:
            continue
        room = temp2 * (1 - it / polish) * float(rng.exponential())
        s2, m = list(state), cur
        for q in ks:
            q = (k + q) % len(MODELS)
            s2[q] = run(o2, e2, q, pu, state[q])
            m += (max(s2[q][0]) - max(state[q][0])) * norm[q]
            if m > cur + room + 60.0:
                break
        if m <= cur + room:
            cur, order, eng, state = m, o2, e2, s2
            end = state[0][1]
            o2 = sorted(order, key=lambda i: end[i] - cost[i][eng[i]])
            if it % 8 == 0 and o2 != order:
                s2 = [run(o2, eng, k, 0, None) for k in ks]
                m2 = sum(max(s[0]) * w for s, w in zip(s2, norm))
                if m2 <= cur:
                    cur, order, state = m2, o2, s2
            if cur < best:
                best, keep = cur, (order, eng)
    order, eng = keep
    state = [run(order, eng, k, 0, None) for k in ks]
    for o, e in zip(ops, eng):
        o["pick"] = [a for a in o["alts"] if a[0] == e][0]
    ops[0]["times"] = [max(s[0]) for s in state]
    return order, [state[0][1][i] - cost[i][eng[i]] for i in range(n)], state[0][0]


_plan = []


def plan():
    if not _plan:
        ops = build()
        depend(ops)
        _plan.append((ops,) + search(ops, SEED, TRIES, POLISH))
    return _plan[0]


def rank_program(g, core, T, topo):
    rank = T.rank_of(core)
    if rank is None:
        return
    ops, order = plan()[0:2]
    Q = {"V": g.vector, "A": g.scalar, "P": g.tensor, "G": g, "Y": g.sync}
    calls = {"tensor_copy": g.vector.tensor_copy, "tensor_tensor": g.vector.tensor_tensor, "tensor_scalar": g.vector.tensor_scalar,
             "memset": g.vector.memset, "tensor_tensor_scan": g.vector.tensor_tensor_scan, "transpose": g.vector.transpose,
             "activation": g.scalar.activation, "iota": g.iota, "affine_select": g.affine_select}

    def real(x):
        if isinstance(x, tuple):
            return real(x[1]).indirect(real(x[2])) if x[0] == "*" else T[x[0]][x[1]]
        return x

    count = {e: 0 for e in "VAPG"}
    seen = {e: {} for e in Q}
    done, total, nq, size = {}, {}, [0], {}
    for o in ops:
        gr = o["pick"][2][2].get("group")
        size[gr] = size.get(gr, 0) + 1
    left = dict(size)

    def fresh():
        nq[0] += 1
        return "q%d" % (nq[0] - 1)

    for i in order:
        o = ops[i]
        e, _c, (name, args, kw) = o["pick"]
        need = {}
        for j, raw in o["deps"].items():
            if kw.get("group") and kw["group"] == ops[j]["pick"][2][2].get("group"):
                continue
            s, v = done[j][1 if raw else 0]
            need[s] = max(need.get(s, 0), v)
        for s, v in need.items():
            if seen[e].get(s, 0) < v:
                Q[e].wait_ge(T.sem[s], v)
                seen[e][s] = v
        if name == "dma":
            s = fresh()
            for out, in_ in args:
                Q[e].dma_start(real(out), real(in_)).then_inc(T.sem[s], 16)
            total[s] = 16 * len(args)
            done[i] = ((s, total[s]), (s, total[s]))
        elif name == "push":
            dst = T.cores[(rank + args[2]) % NR]
            rid, pid, _s = topo.addr(dst)
            sl, sr = fresh(), fresh()
            g.remote_dma(real(args[0]), real(args[1]), T.sem[sr], T.sem[sl], pid, rid, topo.mask(core, dst))
            total[sl] = total[sr] = len(topo.engines(core, dst))
            done[i] = ((sl, total[sl]), (sr, total[sr]))
        else:
            if name == "mm":
                gr = kw["group"]
                first = gr is None or left[gr] == size[gr]
                last = gr is None or left[gr] == 1
                if gr is not None:
                    left[gr] -= 1
                for k, (out, lt, rh) in enumerate(args):
                    ins = g.tensor.matmul(real(out), real(lt), real(rh), k == 0 and first, k == len(args) - 1 and last)
            else:
                ins = calls[name](*[real(x) for x in args], **{k: real(x) for k, x in kw.items()})
            count[e] += 1
            ins.then_inc(T.sem["e" + e], 1)
            total["e" + e] = count[e]
            done[i] = (("e" + e, count[e]), ("e" + e, count[e]))
    for s, v in total.items():
        if seen["G"].get(s, 0) < v:
            g.wait_ge(T.sem[s], v)
